import numpy as np
import ml_dtypes


def mxq(x, axis, fmt="e4m3"):
    dtype, down = {"e4m3": (ml_dtypes.float8_e4m3fn, 7), "e5m2": (ml_dtypes.float8_e5m2, 14)}[fmt]
    v = np.moveaxis(np.asarray(x, np.float32).astype(ml_dtypes.bfloat16).astype(np.float64), axis, -1)
    blocks = v.reshape(v.shape[:-1] + (-1, 32))
    amax = np.abs(blocks).max(-1, keepdims=True)
    byte = np.maximum(np.where(amax > 0, np.frexp(amax)[1] - 1 + 127, 0) - down, 1)
    scale = np.exp2(byte - 127.0)
    codes = (blocks / scale).astype(np.float32).astype(dtype).astype(np.float64)
    return np.moveaxis((codes * scale).reshape(v.shape), -1, axis)


WIDE = False


def mx_kscale(k):
    if not WIDE:
        return np.ones(k)
    levels = np.array([10, -10, 5, -5, 0])
    if k % 512:
        return np.exp2(np.random.permutation(np.resize(levels, k // 32))).repeat(32)
    a = np.empty((k // 512, 16))
    for p in range(k // 512):
        a[p, :8] = np.random.permutation(np.resize(levels, 8))
        for g in range(8):
            far = levels[np.abs(levels - a[p, g]) >= 10]
            a[p, g + 8] = far[np.random.randint(len(far))]
    return np.exp2(a.ravel()).repeat(32)


def f64(x):
    return np.asarray(x).astype(np.float64)


def striped(idx):
    return np.tile(idx.reshape(-1, 16).T, (8, 1)).astype(np.uint16)


def unstriped(offs):
    return offs[:16].T.reshape(-1).astype(np.int64)


E2M1 = np.array([0.0, 0.5, 1.0, 1.5, 2.0, 3.0, 4.0, 6.0, -0.0, -0.5, -1.0, -1.5, -2.0, -3.0, -4.0, -6.0])


def pack_weight(w, fmt):
    k, n = w.shape
    w = f64(np.asarray(w, np.float32).astype(ml_dtypes.bfloat16)).reshape(k // 32, 32, n)
    amax = np.abs(w).max(1)
    if fmt == "e4m3":
        byte = np.frexp(amax)[1] - 1 + 127 - 7
    else:
        mant, ex = np.frexp(amax / 6.0)
        byte = np.where(mant > 0.5, ex, ex - 1) + 127
    byte = np.clip(np.where(amax > 0, byte, 1), 1, 254)
    scaled = (w * np.exp2(127.0 - byte)[:, None, :]).reshape(k, n).astype(np.float32)
    by_word = np.ascontiguousarray(scaled.reshape(k // 512, 128, 4, n).transpose(0, 1, 3, 2))
    if fmt == "e4m3":
        words = by_word.astype(ml_dtypes.float8_e4m3fn).view(np.uint8)
    else:
        c = by_word.astype(ml_dtypes.float4_e2m1fn).view(np.uint8) & 0xF
        words = (c[..., 0::2] | (c[..., 1::2] << 4)).reshape(k // 512, 128, 2 * n)
    return np.ascontiguousarray(words), np.ascontiguousarray(byte.astype(np.uint8).reshape(k // 512, 16, n))


def unpack_weight(words, scales, fmt):
    g, _, n = scales.shape
    words = np.ascontiguousarray(words).reshape(g, 128, n, -1)
    if fmt == "e4m3":
        vals = words.view(ml_dtypes.float8_e4m3fn).astype(np.float64)
    else:
        nib = np.empty((g, 128, n, 4), np.uint8)
        nib[..., 0::2] = words & 0xF
        nib[..., 1::2] = words >> 4
        vals = E2M1[nib]
    vals = vals * np.repeat(np.exp2(scales.astype(np.float64) - 127.0), 8, axis=1)[..., None]
    return vals.transpose(0, 1, 3, 2).reshape(g * 512, n)


def gelu(v):
    return 0.5 * v * (1.0 + np.tanh(np.sqrt(2.0 / np.pi) * (v + 0.044715 * v**3)))


K, H, N, T, S = 1024, 512, 512, 2048, 1024


def setup_inputs():
    n = np.random.standard_normal
    s = mx_kscale(K)[:, None]
    u = mx_kscale(H)[:, None]
    tab_words, tab_scales = pack_weight(n((K, T)) * s, "e4m3")
    wo_words, wo_scales = pack_weight(n((K, H)) / np.sqrt(K) / s * u.T, "e2m1")
    wg_words, wg_scales = pack_weight(1.5 * n((K, H)) / np.sqrt(K) / s, "e4m3")
    return {
        "tab_words": tab_words, "tab_scales": tab_scales,
        "offs": striped(np.random.permutation(T)[:S]),
        "wo_words": wo_words, "wo_scales": wo_scales,
        "wg_words": wg_words, "wg_scales": wg_scales,
        "wn": (n((K, H)) / np.sqrt(K) / s * u.T).astype(np.float32),
        "w2": (n((H, N)) / np.sqrt(H) / u).astype(np.float32),
        "bo": (0.5 * n(N)).astype(np.float32),
    }


def reference(tab_words, tab_scales, offs, wo_words, wo_scales, wg_words, wg_scales, wn, w2, bo):
    v = unpack_weight(tab_words, tab_scales, "e4m3")[:, unstriped(offs)]
    wo = unpack_weight(wo_words, wo_scales, "e2m1")
    wg = unpack_weight(wg_words, wg_scales, "e4m3")
    old = wo.T @ v
    new = mxq(f64(wn), 0, "e4m3").T @ v
    gate = wg.T @ v
    h = old + (new - old) / (1.0 + np.exp(-gate))
    y = mxq(f64(w2), 0, "e4m3").T @ mxq(h, 0, "e4m3")
    return y + f64(bo)[:, None]

@@ -1,0 +1,314 @@
+from contextlib import ExitStack
+
+import concourse.mybir as mybir
+
+K, H, N, T, S = 1024, 512, 512, 2048, 1024
+FLOPS = 2 * S * H * (3 * K + N)
+
+F32 = mybir.dt.float32
+BF16 = mybir.dt.bfloat16
+I32 = mybir.dt.int32
+U32 = mybir.dt.uint32
+U16 = mybir.dt.uint16
+U8 = mybir.dt.uint8
+FP8X4 = mybir.dt.float8_e4m3fn_x4
+FP4X4 = mybir.dt.float4_e2m1fn_x4
+ALU = mybir.AluOpType
+ACT = mybir.ActivationFunctionType
+
+P = 128
+PACK = 4
+PASSES = K // (P * PACK)
+HALF = 512
+RUN = 8
+CHUNKS = [(0, 256), (256, 256), (512, 256), (768, 128), (896, 128)]
+
+
+def tile_list_session_memory_blend_kernel(
+    tc, tab_words, tab_scales, offs, wo_words, wo_scales, wg_words, wg_scales, wn, w2, bo, out
+):
+    nc = tc.nc
+    with ExitStack() as ctx:
+        keep = ctx.enter_context(tc.tile_pool(name="keep", bufs=1))
+        overlay = ctx.enter_context(tc.tile_pool(name="overlay", bufs=1))
+        ring = ctx.enter_context(tc.tile_pool(name="ring", bufs=3))
+        psum = ctx.enter_context(tc.psum_pool(name="psum", bufs=1))
+
+        def tile(shape, dtype, name, tag=""):
+            return keep.tile(shape, dtype, name=name, tag=tag, align_bytes=64)
+
+        offsets = keep.tile([P, S // 16], U16, name="offsets")
+        tab_w = [tile([P, T], U32, "tab_w%d" % a, "slot_tab%d" % a) for a in range(PASSES)]
+        tab_s = overlay.tile([P, T], U8, name="tab_s", align_bytes=64, offset=512)
+        ws_raw = tile([P, 4, H], U8, "ws_raw")
+        wg_s = tile([P, PASSES, H], U8, "wg_s")
+        wg_raw = tile([P, PASSES, H], I32, "wg_raw", "slot_wg")
+        wg = tile([P, PASSES, H], I32, "wg")
+        wo_raw = tile([P, PASSES, 2 * H], U8, "wo_raw", "slot_wo")
+        wo = tile([P, PASSES, 2 * H], U8, "wo")
+        wn_bf = [tile([P, PACK * H], BF16, "wn_bf%d" % a) for a in range(PASSES)]
+        wn_c = [tile([P, H], U32, "wn_c%d" % a) for a in range(PASSES)]
+        wn_s = [tile([P, H], U8, "wn_s%d" % a) for a in range(PASSES)]
+        w2_bf = tile([P, PACK * N], BF16, "w2_bf")
+        w2_c = tile([P, N], U32, "w2_c")
+        w2_s = tile([P, N], U8, "w2_s")
+        v_w = [tile([P, S], U32, "v_w0")]
+        v_s = tile([P, S], U8, "v_s")
+        v_s1 = tile([P, S], U8, "v_s1")
+        sig = [tile([P, PACK, HALF], F32, "sig%d" % h) for h in range(2)]
+        keepold = [tile([P, PACK, HALF], F32, "keepold%d" % h) for h in range(2)]
+        warm_in = tile([P, 1], F32, "warm_in")
+        warm_out = tile([P, 1], F32, "warm_out")
+        banks = [psum.tile([P, 512], F32, name="bank%d" % b) for b in range(8)]
+
+        nc.gpsimd.memset(tab_s[:].bitcast(I32), 0)
+        nc.vector.memset(ws_raw[:].rearrange("p a c -> p (a c)").bitcast(I32), 0)
+        nc.vector.memset(warm_in[:], 0.0)
+        nc.vector.memset(v_s1[:].bitcast(I32), 0)
+
+        def load_table(a):
+            nc.sync.dma_start(
+                out=tab_w[a][:].bitcast(I32),
+                in_=tab_words[a].rearrange("p t i -> p (t i)").bitcast(I32),
+            )
+
+        nc.sync.dma_start(offsets[:], offs)
+        load_table(0)
+        nc.sync.dma_start(out=wg_raw[:], in_=wg_words.rearrange("a p c i -> p a (c i)").bitcast(I32))
+        nc.sync.dma_start(out=wo_raw[:].bitcast(I32), in_=wo_words.rearrange("a p c -> p a c").bitcast(I32))
+        load_table(1)
+        for q in range(4):
+            nc.gpsimd.dma_start(
+                out=tab_s[32 * q : 32 * q + 8, :].bitcast(I32),
+                in_=tab_scales[:, 4 * q : 4 * q + 4, :].bitcast(I32),
+            )
+        for first, src in ((0, wg_scales), (2, wo_scales)):
+            for q in range(4):
+                nc.scalar.dma_start(
+                    out=ws_raw[32 * q : 32 * q + 4, first : first + 2, :].bitcast(I32),
+                    in_=src[:, 4 * q : 4 * q + 4, :].rearrange("a r c -> r a c").bitcast(I32),
+                )
+        nc.scalar.activation(warm_out[:], warm_in[:], ACT.Sigmoid)
+
+        def gather_words(a, h):
+            nc.vector.tensor_copy(
+                out=v_w[a][:, h * HALF : (h + 1) * HALF], in_=tab_w[a][:].indirect(offsets[:, 32 * h : 32 * h + 32])
+            )
+
+        def permute(dst, src, words):
+            nc.vector.tensor_copy(
+                out=dst.rearrange("p a (t g i) -> p a t g i", t=PACK, i=words),
+                in_=src.rearrange("p a (g t i) -> p a t g i", t=PACK, i=words),
+            )
+
+        def load_wn(a, tag):
+            raw = tile([P, PACK, H], F32, "wn_raw%d" % a, tag)
+            nc.sync.dma_start(out=raw[:], in_=wn[a * 512 : (a + 1) * 512, :].rearrange("(p j) c -> p j c", j=PACK))
+            return raw
+
+        gather_words(0, 0)
+        gather_words(0, 1)
+        wn_raw = [load_wn(0, "slot_tab0")]
+        nc.vector.tensor_copy(out=v_s[:], in_=tab_s[:].indirect(offsets[:]))
+        for q in range(4):
+            nc.scalar.dma_start(
+                out=v_s1[32 * q : 32 * q + 4, :].bitcast(I32), in_=v_s[32 * q + 4 : 32 * q + 8, :].bitcast(I32)
+            )
+        permute(wg[:], wg_raw[:], RUN)
+        wn_raw.append(load_wn(1, "slot_wg"))
+        permute(wg_s[:].bitcast(I32), ws_raw[:, 0:2, :].bitcast(I32), RUN // 4)
+        v_w.append(overlay.tile([P, S], U32, name="v_w1", align_bytes=64, offset=1024))
+        gather_words(1, 0)
+        permute(wo[:].bitcast(I32), wo_raw[:].bitcast(I32), RUN // 2)
+        bias = tile([P, N // P], F32, "bias", "slot_wo")
+        with nc.allow_non_contiguous_dma(reason="one bias value for each partition"):
+            nc.sync.dma_start(out=bias[:], in_=bo.rearrange("(u p) -> p u", p=P))
+        wo_s = overlay.tile([P, PASSES, H], U8, name="wo_s", align_bytes=64, offset=0)
+        permute(wo_s[:].bitcast(I32), ws_raw[:, 2:4, :].bitcast(I32), RUN // 4)
+
+        def moving(a, start, width, shifted):
+            cols = slice(start, start + width)
+            codes = v_w[a][:, cols].bitcast(FP8X4)
+            if a == 0:
+                return codes, v_s[:, cols]
+            if shifted:
+                return codes, v_s1[:, cols]
+            return codes, v_s[4:P, cols]
+
+        def gate_pass(bank, h, t, a):
+            codes, scales = moving(a, h * HALF, HALF, False)
+            cols = slice(t * P, (t + 1) * P)
+            nc.tensor.matmul_mx(
+                out=banks[bank][:], lhsT=wg[:, a, cols].bitcast(FP8X4), lhsT_scale=wg_s[:, a, cols],
+                rhs=codes, rhs_scale=scales, start=(a == 0), stop=(a == PASSES - 1),
+            )
+
+        def old_pass(bank, h, t, a):
+            codes, scales = moving(a, h * HALF, HALF, True)
+            nc.tensor.matmul_mx(
+                out=banks[bank][:], lhsT=wo[:, a, 2 * t * P : 2 * (t + 1) * P].bitcast(FP4X4),
+                lhsT_scale=wo_s[:, a, t * P : (t + 1) * P],
+                rhs=codes, rhs_scale=scales, start=(a == 0), stop=(a == PASSES - 1),
+            )
+
+        def sigmoid(bank, h, t):
+            nc.scalar.activation(sig[h][:, t, :], banks[bank][:], ACT.Sigmoid)
+
+        def old_part(bank, h, t):
+            nc.vector.scalar_tensor_tensor(
+                out=keepold[h][:, t, :], in0=sig[h][:, t, :], scalar=1.0, in1=banks[bank][:],
+                op0=ALU.subtract, op1=ALU.mult,
+            )
+
+        def cast_views(a, t):
+            dst = wn_bf[a][:, t * 512 : (t + 1) * 512].rearrange("p (g i j) -> p g j i", i=RUN, j=PACK)
+            src = wn_raw[a][:].rearrange("p j (g t i) -> p t g j i", t=PACK, i=RUN)[:, t]
+            return dst, src
+
+        def cast_wn_gpsimd(a):
+            for t in range(PACK):
+                dst, src = cast_views(a, t)
+                nc.gpsimd.tensor_scalar(out=dst, in0=src, scalar1=1.0, scalar2=0.0, op0=ALU.mult, op1=ALU.add)
+
+        def cast_wn_scalar(a, t):
+            dst, src = cast_views(a, t)
+            nc.scalar.activation(dst, src, ACT.Copy)
+
+        def quantize_wn(a):
+            nc.vector.quantize_mx(out=wn_c[a][:].bitcast(FP8X4), scales=wn_s[a][:], in_=wn_bf[a][:])
+
+        def cast_w2(part):
+            cols = slice(part * 256, (part + 1) * 256)
+            nc.scalar.activation(
+                w2_bf[:, part * 1024 : (part + 1) * 1024].rearrange("p (c i t) -> p c t i", i=4, t=PACK),
+                w2_raw[:, :, cols].rearrange("p t (c i) -> p c t i", i=4),
+                ACT.Copy,
+            )
+
+        state = {}
+
+        def new_passes(c, bank_ids):
+            start, width = CHUNKS[c]
+            per_bank = PACK // len(bank_ids)
+            for t in range(PACK):
+                dst = banks[bank_ids[t // per_bank]][:, (t % per_bank) * width : (t % per_bank + 1) * width]
+                cols = slice(t * P, (t + 1) * P)
+                for a in range(PASSES):
+                    codes, scales = moving(a, start, width, False)
+                    nc.tensor.matmul_mx(
+                        out=dst, lhsT=wn_c[a][:, cols].bitcast(FP8X4), lhsT_scale=wn_s[a][:, cols],
+                        rhs=codes, rhs_scale=scales, start=(a == 0), stop=(a == PASSES - 1),
+                    )
+
+        def new_part(c, bank_ids, k):
+            start, width = CHUNKS[c]
+            h, off = divmod(start, HALF)
+            per_bank = PACK // len(bank_ids)
+            if k == 0:
+                state["new", c] = ring.tile([P, PACK, width], F32, name="gated_new", align_bytes=64)
+            ts = slice(k * per_bank, (k + 1) * per_bank)
+            nc.vector.tensor_tensor(
+                out=state["new", c][:, ts, :],
+                in0=banks[bank_ids[k]][:].rearrange("p (t n) -> p t n", n=width),
+                in1=sig[h][:, ts, off : off + width],
+                op=ALU.mult,
+            )
+
+        def blend(c):
+            start, width = CHUNKS[c]
+            h, off = divmod(start, HALF)
+            h_bf = ring.tile([P, PACK * width], BF16, name="h_bf", align_bytes=64)
+            state["h", c] = h_bf
+            nc.vector.tensor_tensor(
+                out=h_bf[:].rearrange("p (c i t) -> p c t i", i=2, t=PACK),
+                in0=state["new", c][:].rearrange("p t (c i) -> p c t i", i=2),
+                in1=keepold[h][:, :, off : off + width].rearrange("p t (c i) -> p c t i", i=2),
+                op=ALU.subtract,
+            )
+
+        def quantize_h(c):
+            start, width = CHUNKS[c]
+            h_c = ring.tile([P, width], U32, name="h_c", align_bytes=64)
+            h_s = ring.tile([P, width], U8, name="h_s", align_bytes=64)
+            state["hq", c] = (h_c, h_s)
+            nc.vector.quantize_mx(out=h_c[:].bitcast(FP8X4), scales=h_s[:], in_=state["h", c][:])
+
+        def predict(c, bank_ids):
+            start, width = CHUNKS[c]
+            per_bank = PACK // len(bank_ids)
+            h_c, h_s = state["hq", c]
+            y = ring.tile([P, N // P, width], F32, name="y", align_bytes=64)
+            for u in range(N // P):
+                dst = banks[bank_ids[u // per_bank]][:, (u % per_bank) * width : (u % per_bank + 1) * width]
+                cols = slice(u * P, (u + 1) * P)
+                nc.tensor.matmul_mx(
+                    out=dst, lhsT=w2_c[:, cols].bitcast(FP8X4), lhsT_scale=w2_s[:, cols],
+                    rhs=h_c[:].bitcast(FP8X4), rhs_scale=h_s[:], start=True, stop=True,
+                )
+            for u in range(N // P):
+                src = banks[bank_ids[u // per_bank]][:, (u % per_bank) * width : (u % per_bank + 1) * width]
+                nc.scalar.activation(y[:, u, :], src, ACT.Identity, bias=bias[:, u : u + 1])
+            nc.sync.dma_start(out=out.rearrange("(u p) j -> p u j", p=P)[:, :, start : start + width], in_=y[:])
+
+        for t in range(PACK):
+            gate_pass(t, 0, t, 0)
+        gather_words(1, 1)
+        w2_raw = tile([P, PACK, N], F32, "w2_raw", "slot_tab1")
+        w2_view = w2.rearrange("(g t i) n -> t g i n", t=PACK, i=RUN)
+        for t in range(PACK):
+            nc.sync.dma_start(out=w2_raw[:, t, :], in_=w2_view[t])
+        cast_wn_gpsimd(0)
+        for t in range(PACK):
+            gate_pass(t, 0, t, 1)
+            for a in range(PASSES):
+                old_pass(4 + t, 0, t, a)
+            sigmoid(t, 0, t)
+            old_part(4 + t, 0, t)
+
+        def second_half(t, gate_bank, old_bank):
+            for a in range(PASSES):
+                gate_pass(gate_bank, 1, t, a)
+            for a in range(PASSES):
+                old_pass(old_bank, 1, t, a)
+            sigmoid(gate_bank, 1, t)
+            old_part(old_bank, 1, t)
+
+        for t in range(PACK):
+            cast_wn_scalar(1, t)
+        quantize_wn(0)
+        second_half(0, 0, 4)
+        quantize_wn(1)
+        second_half(1, 1, 5)
+        cast_w2(0)
+        cast_w2(1)
+        new_passes(0, [2, 6])
+        new_passes(1, [3, 7])
+        new_part(0, [2, 6], 0)
+        new_part(0, [2, 6], 1)
+        new_part(1, [3, 7], 0)
+        blend(0)
+        new_part(1, [3, 7], 1)
+        second_half(2, 0, 4)
+        nc.vector.quantize_mx(out=w2_c[:].bitcast(FP8X4), scales=w2_s[:], in_=w2_bf[:])
+        quantize_h(0)
+        blend(1)
+        second_half(3, 1, 5)
+        predict(0, [2, 6])
+        quantize_h(1)
+        new_passes(2, [0, 4])
+        predict(1, [3, 7])
+        new_passes(3, [1])
+        new_passes(4, [5])
+        new_part(2, [0, 4], 0)
+        new_part(2, [0, 4], 1)
+        new_part(3, [1], 0)
+        blend(2)
+        new_part(4, [5], 0)
+        quantize_h(2)
+        blend(3)
+        predict(2, [2, 6])
+        blend(4)
+        quantize_h(3)
+        predict(3, [3])
+        quantize_h(4)
+        predict(4, [7])

@@ -20,7 +20,7 @@ P = 128
 PACK = 4
 PASSES = K // (P * PACK)
 HALF = 512
-RUN = 8
+RUN = 4
 CHUNKS = [(0, 256), (256, 256), (512, 256), (768, 128), (896, 128)]
 
 
@@ -30,7 +30,6 @@ def tile_list_session_memory_blend_kernel(
     nc = tc.nc
     with ExitStack() as ctx:
         keep = ctx.enter_context(tc.tile_pool(name="keep", bufs=1))
-        overlay = ctx.enter_context(tc.tile_pool(name="overlay", bufs=1))
         ring = ctx.enter_context(tc.tile_pool(name="ring", bufs=3))
         psum = ctx.enter_context(tc.psum_pool(name="psum", bufs=1))
 
@@ -39,12 +38,16 @@ def tile_list_session_memory_blend_kernel(
 
         offsets = keep.tile([P, S // 16], U16, name="offsets")
         tab_w = [tile([P, T], U32, "tab_w%d" % a, "slot_tab%d" % a) for a in range(PASSES)]
-        tab_s = overlay.tile([P, T], U8, name="tab_s", align_bytes=64, offset=512)
+        tab_s = tile([P, T], U8, "tab_s")
+        wg_raw = tile([P, PASSES, H], I32, "wg_raw")
+        wo_raw = tile([P, PASSES, 2 * H], U8, "wo_raw")
+        wn_raw = [tile([P, PACK, H], F32, "wn_raw%d" % a) for a in range(PASSES)]
+        warm_in = tile([P, 1], F32, "warm_in")
+        warm_out = tile([P, 1], F32, "warm_out")
         ws_raw = tile([P, 4, H], U8, "ws_raw")
         wg_s = tile([P, PASSES, H], U8, "wg_s")
-        wg_raw = tile([P, PASSES, H], I32, "wg_raw", "slot_wg")
+        wo_s = tile([P, PASSES, H], U8, "wo_s")
         wg = tile([P, PASSES, H], I32, "wg")
-        wo_raw = tile([P, PASSES, 2 * H], U8, "wo_raw", "slot_wo")
         wo = tile([P, PASSES, 2 * H], U8, "wo")
         wn_bf = [tile([P, PACK * H], BF16, "wn_bf%d" % a) for a in range(PASSES)]
         wn_c = [tile([P, H], U32, "wn_c%d" % a) for a in range(PASSES)]
@@ -52,18 +55,16 @@ def tile_list_session_memory_blend_kernel(
         w2_bf = tile([P, PACK * N], BF16, "w2_bf")
         w2_c = tile([P, N], U32, "w2_c")
         w2_s = tile([P, N], U8, "w2_s")
-        v_w = [tile([P, S], U32, "v_w0")]
+        v_w = [tile([P, S], U32, "v_w%d" % a) for a in range(PASSES)]
         v_s = tile([P, S], U8, "v_s")
         v_s1 = tile([P, S], U8, "v_s1")
         sig = [tile([P, PACK, HALF], F32, "sig%d" % h) for h in range(2)]
         keepold = [tile([P, PACK, HALF], F32, "keepold%d" % h) for h in range(2)]
-        warm_in = tile([P, 1], F32, "warm_in")
-        warm_out = tile([P, 1], F32, "warm_out")
         banks = [psum.tile([P, 512], F32, name="bank%d" % b) for b in range(8)]
 
         nc.gpsimd.memset(tab_s[:].bitcast(I32), 0)
+        nc.gpsimd.memset(warm_in[:], 0.0)
         nc.vector.memset(ws_raw[:].rearrange("p a c -> p (a c)").bitcast(I32), 0)
-        nc.vector.memset(warm_in[:], 0.0)
         nc.vector.memset(v_s1[:].bitcast(I32), 0)
 
         def load_table(a):
@@ -72,23 +73,33 @@ def tile_list_session_memory_blend_kernel(
                 in_=tab_words[a].rearrange("p t i -> p (t i)").bitcast(I32),
             )
 
-        nc.sync.dma_start(offsets[:], offs)
-        load_table(0)
-        nc.sync.dma_start(out=wg_raw[:], in_=wg_words.rearrange("a p c i -> p a (c i)").bitcast(I32))
-        nc.sync.dma_start(out=wo_raw[:].bitcast(I32), in_=wo_words.rearrange("a p c -> p a c").bitcast(I32))
-        load_table(1)
-        for q in range(4):
-            nc.gpsimd.dma_start(
-                out=tab_s[32 * q : 32 * q + 8, :].bitcast(I32),
-                in_=tab_scales[:, 4 * q : 4 * q + 4, :].bitcast(I32),
-            )
-        for first, src in ((0, wg_scales), (2, wo_scales)):
+        def load_weight_scales(queue, first, src):
             for q in range(4):
-                nc.scalar.dma_start(
+                queue.dma_start(
                     out=ws_raw[32 * q : 32 * q + 4, first : first + 2, :].bitcast(I32),
                     in_=src[:, 4 * q : 4 * q + 4, :].rearrange("a r c -> r a c").bitcast(I32),
                 )
+
+        def load_wn(a):
+            nc.sync.dma_start(
+                out=wn_raw[a][:], in_=wn[a * 512 : (a + 1) * 512, :].rearrange("(p j) c -> p j c", j=PACK)
+            )
+
+        nc.sync.dma_start(offsets[:], offs)
+        load_table(0)
+        for q in range(4):
+            nc.sync.dma_start(
+                out=tab_s[32 * q : 32 * q + 8, :].bitcast(I32),
+                in_=tab_scales[:, 4 * q : 4 * q + 4, :].bitcast(I32),
+            )
+        load_weight_scales(nc.scalar, 0, wg_scales)
+        load_weight_scales(nc.scalar, 2, wo_scales)
         nc.scalar.activation(warm_out[:], warm_in[:], ACT.Sigmoid)
+        nc.sync.dma_start(out=wg_raw[:], in_=wg_words.rearrange("a p c i -> p a (c i)").bitcast(I32))
+        nc.sync.dma_start(out=wo_raw[:].bitcast(I32), in_=wo_words.rearrange("a p c -> p a c").bitcast(I32))
+        load_wn(0)
+        load_table(1)
+        load_wn(1)
 
         def gather_words(a, h):
             nc.vector.tensor_copy(
@@ -101,30 +112,21 @@ def tile_list_session_memory_blend_kernel(
                 in_=src.rearrange("p a (g t i) -> p a t g i", t=PACK, i=words),
             )
 
-        def load_wn(a, tag):
-            raw = tile([P, PACK, H], F32, "wn_raw%d" % a, tag)
-            nc.sync.dma_start(out=raw[:], in_=wn[a * 512 : (a + 1) * 512, :].rearrange("(p j) c -> p j c", j=PACK))
-            return raw
-
         gather_words(0, 0)
-        gather_words(0, 1)
-        wn_raw = [load_wn(0, "slot_tab0")]
         nc.vector.tensor_copy(out=v_s[:], in_=tab_s[:].indirect(offsets[:]))
         for q in range(4):
             nc.scalar.dma_start(
                 out=v_s1[32 * q : 32 * q + 4, :].bitcast(I32), in_=v_s[32 * q + 4 : 32 * q + 8, :].bitcast(I32)
             )
         permute(wg[:], wg_raw[:], RUN)
-        wn_raw.append(load_wn(1, "slot_wg"))
         permute(wg_s[:].bitcast(I32), ws_raw[:, 0:2, :].bitcast(I32), RUN // 4)
-        v_w.append(overlay.tile([P, S], U32, name="v_w1", align_bytes=64, offset=1024))
-        gather_words(1, 0)
         permute(wo[:].bitcast(I32), wo_raw[:].bitcast(I32), RUN // 2)
-        bias = tile([P, N // P], F32, "bias", "slot_wo")
-        with nc.allow_non_contiguous_dma(reason="one bias value for each partition"):
-            nc.sync.dma_start(out=bias[:], in_=bo.rearrange("(u p) -> p u", p=P))
-        wo_s = overlay.tile([P, PASSES, H], U8, name="wo_s", align_bytes=64, offset=0)
         permute(wo_s[:].bitcast(I32), ws_raw[:, 2:4, :].bitcast(I32), RUN // 4)
+        gather_words(0, 1)
+        w2_raw = tile([P, PACK, N], F32, "w2_raw", "slot_tab0")
+        w2_view = w2.rearrange("(g t i) n -> t g i n", t=PACK, i=RUN)
+        for t in range(PACK):
+            nc.sync.dma_start(out=w2_raw[:, t, :], in_=w2_view[t])
 
         def moving(a, start, width, shifted):
             cols = slice(start, start + width)
@@ -165,10 +167,10 @@ def tile_list_session_memory_blend_kernel(
             src = wn_raw[a][:].rearrange("p j (g t i) -> p t g j i", t=PACK, i=RUN)[:, t]
             return dst, src
 
-        def cast_wn_gpsimd(a):
-            for t in range(PACK):
-                dst, src = cast_views(a, t)
-                nc.gpsimd.tensor_scalar(out=dst, in0=src, scalar1=1.0, scalar2=0.0, op0=ALU.mult, op1=ALU.add)
+        def cast_wn_gpsimd(a, t):
+            dst = wn_bf[a][:, t * 512 : (t + 1) * 512].rearrange("p (g i j) -> p g i j", i=RUN, j=PACK)
+            src = wn_raw[a][:].rearrange("p j (g t i) -> p t g i j", t=PACK, i=RUN)[:, t]
+            nc.gpsimd.tensor_scalar(out=dst, in0=src, scalar1=1.0, scalar2=0.0, op0=ALU.mult, op1=ALU.add)
 
         def cast_wn_scalar(a, t):
             dst, src = cast_views(a, t)
@@ -233,7 +235,7 @@ def tile_list_session_memory_blend_kernel(
             state["hq", c] = (h_c, h_s)
             nc.vector.quantize_mx(out=h_c[:].bitcast(FP8X4), scales=h_s[:], in_=state["h", c][:])
 
-        def predict(c, bank_ids):
+        def predict(c, bank_ids, on_vector=False):
             start, width = CHUNKS[c]
             per_bank = PACK // len(bank_ids)
             h_c, h_s = state["hq", c]
@@ -245,24 +247,45 @@ def tile_list_session_memory_blend_kernel(
                     out=dst, lhsT=w2_c[:, cols].bitcast(FP8X4), lhsT_scale=w2_s[:, cols],
                     rhs=h_c[:].bitcast(FP8X4), rhs_scale=h_s[:], start=True, stop=True,
                 )
-            for u in range(N // P):
-                src = banks[bank_ids[u // per_bank]][:, (u % per_bank) * width : (u % per_bank + 1) * width]
-                nc.scalar.activation(y[:, u, :], src, ACT.Identity, bias=bias[:, u : u + 1])
+            if on_vector:
+                nc.vector.tensor_tensor(
+                    out=y[:],
+                    in0=banks[bank_ids[0]][:].rearrange("p (u n) -> p u n", n=width),
+                    in1=bias[:].unsqueeze(2).to_broadcast([P, N // P, width]),
+                    op=ALU.add,
+                )
+            else:
+                for u in range(N // P):
+                    src = banks[bank_ids[u // per_bank]][:, (u % per_bank) * width : (u % per_bank + 1) * width]
+                    nc.scalar.activation(y[:, u, :], src, ACT.Identity, bias=bias[:, u : u + 1])
             nc.sync.dma_start(out=out.rearrange("(u p) j -> p u j", p=P)[:, :, start : start + width], in_=y[:])
 
         for t in range(PACK):
             gate_pass(t, 0, t, 0)
+        for t in range(PACK):
+            old_pass(4 + t, 0, t, 0)
+        for t in range(PACK):
+            cast_wn_scalar(0, t)
+        quantize_wn(0)
+        gather_words(1, 0)
         gather_words(1, 1)
-        w2_raw = tile([P, PACK, N], F32, "w2_raw", "slot_tab1")
-        w2_view = w2.rearrange("(g t i) n -> t g i n", t=PACK, i=RUN)
+        bias = tile([P, N // P], F32, "bias", "slot_tab1")
+        with nc.allow_non_contiguous_dma(reason="one bias value for each partition"):
+            nc.sync.dma_start(out=bias[:], in_=bo.rearrange("(u p) -> p u", p=P))
+        gate_pass(0, 0, 0, 1)
         for t in range(PACK):
-            nc.sync.dma_start(out=w2_raw[:, t, :], in_=w2_view[t])
-        cast_wn_gpsimd(0)
+            if t + 1 < PACK:
+                gate_pass(t + 1, 0, t + 1, 1)
+            old_pass(4 + t, 0, t, 1)
+        cast_wn_gpsimd(1, 2)
+        cast_wn_gpsimd(1, 3)
+        sigmoid(0, 0, 0)
+        sigmoid(1, 0, 1)
+        sigmoid(2, 0, 2)
+        cast_wn_scalar(1, 0)
+        sigmoid(3, 0, 3)
+        cast_wn_scalar(1, 1)
         for t in range(PACK):
-            gate_pass(t, 0, t, 1)
-            for a in range(PASSES):
-                old_pass(4 + t, 0, t, a)
-            sigmoid(t, 0, t)
             old_part(4 + t, 0, t)
 
         def second_half(t, gate_bank, old_bank):
@@ -273,42 +296,39 @@ def tile_list_session_memory_blend_kernel(
             sigmoid(gate_bank, 1, t)
             old_part(old_bank, 1, t)
 
-        for t in range(PACK):
-            cast_wn_scalar(1, t)
-        quantize_wn(0)
-        second_half(0, 0, 4)
         quantize_wn(1)
+        second_half(0, 0, 4)
         second_half(1, 1, 5)
+        new_passes(0, [3, 7])
         cast_w2(0)
+        second_half(2, 2, 6)
         cast_w2(1)
-        new_passes(0, [2, 6])
-        new_passes(1, [3, 7])
-        new_part(0, [2, 6], 0)
-        new_part(0, [2, 6], 1)
-        new_part(1, [3, 7], 0)
+        new_passes(1, [0, 4])
+        new_part(0, [3, 7], 0)
+        new_part(0, [3, 7], 1)
+        new_part(1, [0, 4], 0)
         blend(0)
-        new_part(1, [3, 7], 1)
-        second_half(2, 0, 4)
+        new_part(1, [0, 4], 1)
         nc.vector.quantize_mx(out=w2_c[:].bitcast(FP8X4), scales=w2_s[:], in_=w2_bf[:])
         quantize_h(0)
-        blend(1)
         second_half(3, 1, 5)
+        new_passes(2, [3, 7])
         predict(0, [2, 6])
+        blend(1)
+        new_part(2, [3, 7], 0)
         quantize_h(1)
-        new_passes(2, [0, 4])
-        predict(1, [3, 7])
         new_passes(3, [1])
         new_passes(4, [5])
-        new_part(2, [0, 4], 0)
-        new_part(2, [0, 4], 1)
+        predict(1, [0, 4])
+        new_part(2, [3, 7], 1)
         new_part(3, [1], 0)
         blend(2)
         new_part(4, [5], 0)
         quantize_h(2)
-        blend(3)
         predict(2, [2, 6])
+        blend(3)
         blend(4)
         quantize_h(3)
         predict(3, [3])
         quantize_h(4)
-        predict(4, [7])
+        predict(4, [7], True)

@@ -21,6 +21,7 @@ PACK = 4
 PASSES = K // (P * PACK)
 HALF = 512
 RUN = 4
+WARM_PASSES = 2
 CHUNKS = [(0, 256), (256, 256), (512, 256), (768, 128), (896, 128)]
 
 
@@ -30,7 +31,7 @@ def tile_list_session_memory_blend_kernel(
     nc = tc.nc
     with ExitStack() as ctx:
         keep = ctx.enter_context(tc.tile_pool(name="keep", bufs=1))
-        ring = ctx.enter_context(tc.tile_pool(name="ring", bufs=3))
+        ring = ctx.enter_context(tc.tile_pool(name="ring", bufs=5))
         psum = ctx.enter_context(tc.psum_pool(name="psum", bufs=1))
 
         def tile(shape, dtype, name, tag=""):
@@ -39,11 +40,11 @@ def tile_list_session_memory_blend_kernel(
         offsets = keep.tile([P, S // 16], U16, name="offsets")
         tab_w = [tile([P, T], U32, "tab_w%d" % a, "slot_tab%d" % a) for a in range(PASSES)]
         tab_s = tile([P, T], U8, "tab_s")
-        wg_raw = tile([P, PASSES, H], I32, "wg_raw")
-        wo_raw = tile([P, PASSES, 2 * H], U8, "wo_raw")
-        wn_raw = [tile([P, PACK, H], F32, "wn_raw%d" % a) for a in range(PASSES)]
         warm_in = tile([P, 1], F32, "warm_in")
         warm_out = tile([P, 1], F32, "warm_out")
+        wg_raw = tile([P, PASSES, H], I32, "wg_raw")
+        wo_raw = tile([P, PASSES, H // 2], I32, "wo_raw")
+        wn_raw = [tile([P, PACK, H], F32, "wn_raw%d" % a) for a in range(PASSES)]
         ws_raw = tile([P, 4, H], U8, "ws_raw")
         wg_s = tile([P, PASSES, H], U8, "wg_s")
         wo_s = tile([P, PASSES, H], U8, "wo_s")
@@ -62,9 +63,9 @@ def tile_list_session_memory_blend_kernel(
         keepold = [tile([P, PACK, HALF], F32, "keepold%d" % h) for h in range(2)]
         banks = [psum.tile([P, 512], F32, name="bank%d" % b) for b in range(8)]
 
-        nc.gpsimd.memset(tab_s[:].bitcast(I32), 0)
-        nc.gpsimd.memset(warm_in[:], 0.0)
-        nc.vector.memset(ws_raw[:].rearrange("p a c -> p (a c)").bitcast(I32), 0)
+        nc.vector.memset(tab_s[:].bitcast(I32), 0)
+        nc.gpsimd.memset(ws_raw[:].rearrange("p a c -> p (a c)").bitcast(I32), 0)
+        nc.vector.memset(warm_in[:], 0.0)
         nc.vector.memset(v_s1[:].bitcast(I32), 0)
 
         def load_table(a):
@@ -88,7 +89,7 @@ def tile_list_session_memory_blend_kernel(
         nc.sync.dma_start(offsets[:], offs)
         load_table(0)
         for q in range(4):
-            nc.sync.dma_start(
+            nc.scalar.dma_start(
                 out=tab_s[32 * q : 32 * q + 8, :].bitcast(I32),
                 in_=tab_scales[:, 4 * q : 4 * q + 4, :].bitcast(I32),
             )
@@ -96,9 +97,9 @@ def tile_list_session_memory_blend_kernel(
         load_weight_scales(nc.scalar, 2, wo_scales)
         nc.scalar.activation(warm_out[:], warm_in[:], ACT.Sigmoid)
         nc.sync.dma_start(out=wg_raw[:], in_=wg_words.rearrange("a p c i -> p a (c i)").bitcast(I32))
-        nc.sync.dma_start(out=wo_raw[:].bitcast(I32), in_=wo_words.rearrange("a p c -> p a c").bitcast(I32))
-        load_wn(0)
+        nc.sync.dma_start(out=wo_raw[:], in_=wo_words.rearrange("a p c -> p a c").bitcast(I32))
         load_table(1)
+        load_wn(0)
         load_wn(1)
 
         def gather_words(a, h):
@@ -118,15 +119,25 @@ def tile_list_session_memory_blend_kernel(
             nc.scalar.dma_start(
                 out=v_s1[32 * q : 32 * q + 4, :].bitcast(I32), in_=v_s[32 * q + 4 : 32 * q + 8, :].bitcast(I32)
             )
+        for w in range(WARM_PASSES):
+            nc.tensor.matmul_mx(
+                out=banks[7][:], lhsT=v_w[0][:, 0:P].bitcast(FP8X4), lhsT_scale=v_s[:, 0:P],
+                rhs=v_w[0][:, 0:HALF].bitcast(FP8X4), rhs_scale=v_s[:, 0:HALF], start=True, stop=True,
+            )
         permute(wg[:], wg_raw[:], RUN)
         permute(wg_s[:].bitcast(I32), ws_raw[:, 0:2, :].bitcast(I32), RUN // 4)
-        permute(wo[:].bitcast(I32), wo_raw[:].bitcast(I32), RUN // 2)
+        permute(wo[:].bitcast(I32), wo_raw[:], RUN // 2)
         permute(wo_s[:].bitcast(I32), ws_raw[:, 2:4, :].bitcast(I32), RUN // 4)
+        gather_words(1, 0)
         gather_words(0, 1)
         w2_raw = tile([P, PACK, N], F32, "w2_raw", "slot_tab0")
         w2_view = w2.rearrange("(g t i) n -> t g i n", t=PACK, i=RUN)
         for t in range(PACK):
             nc.sync.dma_start(out=w2_raw[:, t, :], in_=w2_view[t])
+        gather_words(1, 1)
+        bias = tile([P, N // P], F32, "bias", "slot_tab1")
+        with nc.allow_non_contiguous_dma(reason="one bias value for each partition"):
+            nc.sync.dma_start(out=bias[:], in_=bo.rearrange("(u p) -> p u", p=P))
 
         def moving(a, start, width, shifted):
             cols = slice(start, start + width)
@@ -176,42 +187,59 @@ def tile_list_session_memory_blend_kernel(
             dst, src = cast_views(a, t)
             nc.scalar.activation(dst, src, ACT.Copy)
 
+        def cast_wn_vector(a, t):
+            dst, src = cast_views(a, t)
+            nc.vector.tensor_copy(out=dst, in_=src)
+
         def quantize_wn(a):
             nc.vector.quantize_mx(out=wn_c[a][:].bitcast(FP8X4), scales=wn_s[a][:], in_=wn_bf[a][:])
 
-        def cast_w2(part):
-            cols = slice(part * 256, (part + 1) * 256)
-            nc.scalar.activation(
-                w2_bf[:, part * 1024 : (part + 1) * 1024].rearrange("p (c i t) -> p c t i", i=4, t=PACK),
-                w2_raw[:, :, cols].rearrange("p t (c i) -> p c t i", i=4),
-                ACT.Copy,
-            )
+        def w2_views(part, run):
+            dst = w2_bf[:, part * 512 : (part + 1) * 512].rearrange("p (c i t) -> p c t i", i=run, t=PACK)
+            src = w2_raw[:, :, part * P : (part + 1) * P].rearrange("p t (c i) -> p c t i", i=run)
+            return dst, src
+
+        def cast_w2_scalar(part):
+            dst, src = w2_views(part, 4)
+            nc.scalar.activation(dst, src, ACT.Copy)
+
+        def cast_w2_vector(part):
+            dst, src = w2_views(part, 4)
+            nc.vector.tensor_copy(out=dst, in_=src)
+
+        def cast_w2_gpsimd(part):
+            dst, src = w2_views(part, 1)
+            nc.gpsimd.tensor_scalar(out=dst, in0=src, scalar1=1.0, scalar2=0.0, op0=ALU.mult, op1=ALU.add)
+
+        def quantize_w2():
+            nc.vector.quantize_mx(out=w2_c[:].bitcast(FP8X4), scales=w2_s[:], in_=w2_bf[:])
 
         state = {}
 
-        def new_passes(c, bank_ids):
+        def new_passes(bank, c, k):
             start, width = CHUNKS[c]
-            per_bank = PACK // len(bank_ids)
-            for t in range(PACK):
-                dst = banks[bank_ids[t // per_bank]][:, (t % per_bank) * width : (t % per_bank + 1) * width]
+            per_bank = 512 // width
+            for j in range(per_bank):
+                t = k * per_bank + j
                 cols = slice(t * P, (t + 1) * P)
                 for a in range(PASSES):
                     codes, scales = moving(a, start, width, False)
                     nc.tensor.matmul_mx(
-                        out=dst, lhsT=wn_c[a][:, cols].bitcast(FP8X4), lhsT_scale=wn_s[a][:, cols],
+                        out=banks[bank][:, j * width : (j + 1) * width],
+                        lhsT=wn_c[a][:, cols].bitcast(FP8X4), lhsT_scale=wn_s[a][:, cols],
                         rhs=codes, rhs_scale=scales, start=(a == 0), stop=(a == PASSES - 1),
                     )
 
-        def new_part(c, bank_ids, k):
+        def new_part(bank, c, k):
             start, width = CHUNKS[c]
             h, off = divmod(start, HALF)
-            per_bank = PACK // len(bank_ids)
-            if k == 0:
+            per_bank = 512 // width
+            if ("new", c) not in state:
                 state["new", c] = ring.tile([P, PACK, width], F32, name="gated_new", align_bytes=64)
             ts = slice(k * per_bank, (k + 1) * per_bank)
             nc.vector.tensor_tensor(
                 out=state["new", c][:, ts, :],
-                in0=banks[bank_ids[k]][:].rearrange("p (t n) -> p t n", n=width),
+                in0=banks[bank][:].rearrange("p (t n) -> p t n", n=width),
                 in1=sig[h][:, ts, off : off + width],
                 op=ALU.mult,
             )
@@ -228,6 +256,28 @@ def tile_list_session_memory_blend_kernel(
                 op=ALU.subtract,
             )
 
+        def blend_gpsimd(c, k):
+            start, width = CHUNKS[c]
+            h, off = divmod(start, HALF)
+            if ("ht", c) not in state:
+                state["ht", c] = ring.tile([P, PACK, width], BF16, name="h_rows", align_bytes=64)
+            ts = slice(2 * k, 2 * k + 2)
+            nc.gpsimd.tensor_tensor(
+                out=state["ht", c][:, ts, :],
+                in0=state["new", c][:, ts, :],
+                in1=keepold[h][:, ts, off : off + width],
+                op=ALU.subtract,
+            )
+
+        def interleave(c):
+            start, width = CHUNKS[c]
+            h_bf = ring.tile([P, PACK * width], BF16, name="h_bf", align_bytes=64)
+            state["h", c] = h_bf
+            nc.scalar.copy(
+                h_bf[:].rearrange("p (c i t) -> p c t i", i=4, t=PACK),
+                state["ht", c][:].rearrange("p t (c i) -> p c t i", i=4),
+            )
+
         def quantize_h(c):
             start, width = CHUNKS[c]
             h_c = ring.tile([P, width], U32, name="h_c", align_bytes=64)
@@ -235,100 +285,162 @@ def tile_list_session_memory_blend_kernel(
             state["hq", c] = (h_c, h_s)
             nc.vector.quantize_mx(out=h_c[:].bitcast(FP8X4), scales=h_s[:], in_=state["h", c][:])
 
-        def predict(c, bank_ids, on_vector=False):
+        def predict(bank, c, k):
             start, width = CHUNKS[c]
-            per_bank = PACK // len(bank_ids)
+            per_bank = 512 // width
             h_c, h_s = state["hq", c]
-            y = ring.tile([P, N // P, width], F32, name="y", align_bytes=64)
-            for u in range(N // P):
-                dst = banks[bank_ids[u // per_bank]][:, (u % per_bank) * width : (u % per_bank + 1) * width]
+            for j in range(per_bank):
+                u = k * per_bank + j
                 cols = slice(u * P, (u + 1) * P)
                 nc.tensor.matmul_mx(
-                    out=dst, lhsT=w2_c[:, cols].bitcast(FP8X4), lhsT_scale=w2_s[:, cols],
+                    out=banks[bank][:, j * width : (j + 1) * width],
+                    lhsT=w2_c[:, cols].bitcast(FP8X4), lhsT_scale=w2_s[:, cols],
                     rhs=h_c[:].bitcast(FP8X4), rhs_scale=h_s[:], start=True, stop=True,
                 )
-            if on_vector:
-                nc.vector.tensor_tensor(
-                    out=y[:],
-                    in0=banks[bank_ids[0]][:].rearrange("p (u n) -> p u n", n=width),
-                    in1=bias[:].unsqueeze(2).to_broadcast([P, N // P, width]),
-                    op=ALU.add,
+
+        def result_tile(c):
+            if ("y", c) not in state:
+                state["y", c] = ring.tile([P, N // P, CHUNKS[c][1]], F32, name="y", align_bytes=64)
+            return state["y", c]
+
+        def evacuate_vector(bank, c, k):
+            start, width = CHUNKS[c]
+            per_bank = 512 // width
+            us = slice(k * per_bank, (k + 1) * per_bank)
+            nc.vector.tensor_tensor(
+                out=result_tile(c)[:, us, :],
+                in0=banks[bank][:].rearrange("p (u n) -> p u n", n=width),
+                in1=bias[:, us].unsqueeze(2).to_broadcast([P, per_bank, width]),
+                op=ALU.add,
+            )
+
+        def evacuate_scalar(bank, c, k):
+            start, width = CHUNKS[c]
+            per_bank = 512 // width
+            for j in range(per_bank):
+                u = k * per_bank + j
+                nc.scalar.activation(
+                    result_tile(c)[:, u, :], banks[bank][:, j * width : (j + 1) * width], ACT.Identity,
+                    bias=bias[:, u : u + 1],
                 )
-            else:
-                for u in range(N // P):
-                    src = banks[bank_ids[u // per_bank]][:, (u % per_bank) * width : (u % per_bank + 1) * width]
-                    nc.scalar.activation(y[:, u, :], src, ACT.Identity, bias=bias[:, u : u + 1])
-            nc.sync.dma_start(out=out.rearrange("(u p) j -> p u j", p=P)[:, :, start : start + width], in_=y[:])
 
-        for t in range(PACK):
-            gate_pass(t, 0, t, 0)
-        for t in range(PACK):
-            old_pass(4 + t, 0, t, 0)
-        for t in range(PACK):
-            cast_wn_scalar(0, t)
-        quantize_wn(0)
-        gather_words(1, 0)
-        gather_words(1, 1)
-        bias = tile([P, N // P], F32, "bias", "slot_tab1")
-        with nc.allow_non_contiguous_dma(reason="one bias value for each partition"):
-            nc.sync.dma_start(out=bias[:], in_=bo.rearrange("(u p) -> p u", p=P))
+        def store(c):
+            start, width = CHUNKS[c]
+            nc.sync.dma_start(
+                out=out.rearrange("(u p) j -> p u j", p=P)[:, :, start : start + width], in_=result_tile(c)[:]
+            )
+
+        gate_pass(0, 0, 0, 0)
+        gate_pass(1, 0, 1, 0)
+        gate_pass(2, 0, 2, 0)
+        gate_pass(3, 0, 3, 0)
+        cast_wn_scalar(0, 2)
+        cast_wn_scalar(0, 3)
+        cast_wn_vector(0, 0)
+        cast_wn_vector(0, 1)
         gate_pass(0, 0, 0, 1)
-        for t in range(PACK):
-            if t + 1 < PACK:
-                gate_pass(t + 1, 0, t + 1, 1)
-            old_pass(4 + t, 0, t, 1)
-        cast_wn_gpsimd(1, 2)
-        cast_wn_gpsimd(1, 3)
+        old_pass(4, 0, 0, 0)
+        old_pass(4, 0, 0, 1)
+        gate_pass(1, 0, 1, 1)
+        old_pass(5, 0, 1, 0)
+        old_pass(5, 0, 1, 1)
+        gate_pass(2, 0, 2, 1)
+        old_pass(6, 0, 2, 0)
+        old_pass(6, 0, 2, 1)
+        gate_pass(3, 0, 3, 1)
+        old_pass(7, 0, 3, 0)
+        old_pass(7, 0, 3, 1)
+        quantize_wn(0)
         sigmoid(0, 0, 0)
+        old_part(4, 0, 0)
         sigmoid(1, 0, 1)
-        sigmoid(2, 0, 2)
-        cast_wn_scalar(1, 0)
-        sigmoid(3, 0, 3)
+        old_part(5, 0, 1)
+        cast_wn_gpsimd(1, 3)
+        cast_wn_scalar(1, 2)
+        cast_wn_vector(1, 0)
         cast_wn_scalar(1, 1)
-        for t in range(PACK):
-            old_part(4 + t, 0, t)
-
-        def second_half(t, gate_bank, old_bank):
-            for a in range(PASSES):
-                gate_pass(gate_bank, 1, t, a)
-            for a in range(PASSES):
-                old_pass(old_bank, 1, t, a)
-            sigmoid(gate_bank, 1, t)
-            old_part(old_bank, 1, t)
-
+        gate_pass(0, 1, 0, 0)
+        gate_pass(0, 1, 0, 1)
+        gate_pass(4, 1, 1, 0)
+        gate_pass(4, 1, 1, 1)
+        sigmoid(2, 0, 2)
+        sigmoid(3, 0, 3)
         quantize_wn(1)
-        second_half(0, 0, 4)
-        second_half(1, 1, 5)
-        new_passes(0, [3, 7])
-        cast_w2(0)
-        second_half(2, 2, 6)
-        cast_w2(1)
-        new_passes(1, [0, 4])
-        new_part(0, [3, 7], 0)
-        new_part(0, [3, 7], 1)
-        new_part(1, [0, 4], 0)
-        blend(0)
-        new_part(1, [0, 4], 1)
-        nc.vector.quantize_mx(out=w2_c[:].bitcast(FP8X4), scales=w2_s[:], in_=w2_bf[:])
+        old_part(6, 0, 2)
+        old_part(7, 0, 3)
+        new_passes(1, 0, 0)
+        new_passes(5, 0, 1)
+        cast_w2_scalar(0)
+        cast_w2_scalar(1)
+        cast_w2_scalar(2)
+        cast_w2_gpsimd(3)
+        new_passes(2, 1, 0)
+        new_passes(3, 1, 1)
+        new_part(1, 0, 0)
+        blend_gpsimd(0, 0)
+        new_part(5, 0, 1)
+        blend_gpsimd(0, 1)
+        quantize_w2()
+        sigmoid(0, 1, 0)
+        sigmoid(4, 1, 1)
+        gate_pass(6, 1, 2, 0)
+        gate_pass(6, 1, 2, 1)
+        gate_pass(7, 1, 3, 0)
+        gate_pass(7, 1, 3, 1)
+        new_part(2, 1, 0)
+        blend_gpsimd(1, 0)
+        new_part(3, 1, 1)
+        blend_gpsimd(1, 1)
+        old_pass(1, 1, 0, 0)
+        old_pass(1, 1, 0, 1)
+        old_part(1, 1, 0)
+        old_pass(5, 1, 1, 0)
+        old_pass(5, 1, 1, 1)
+        old_part(5, 1, 1)
+        old_pass(0, 1, 2, 0)
+        old_pass(0, 1, 2, 1)
+        sigmoid(6, 1, 2)
+        old_part(0, 1, 2)
+        old_pass(4, 1, 3, 0)
+        old_pass(4, 1, 3, 1)
+        sigmoid(7, 1, 3)
+        old_part(4, 1, 3)
+        interleave(0)
+        new_passes(2, 2, 0)
+        new_passes(3, 2, 1)
+        new_part(2, 2, 0)
+        new_part(3, 2, 1)
+        new_passes(1, 3, 0)
+        new_passes(5, 4, 0)
         quantize_h(0)
-        second_half(3, 1, 5)
-        new_passes(2, [3, 7])
-        predict(0, [2, 6])
-        blend(1)
-        new_part(2, [3, 7], 0)
-        quantize_h(1)
-        new_passes(3, [1])
-        new_passes(4, [5])
-        predict(1, [0, 4])
-        new_part(2, [3, 7], 1)
-        new_part(3, [1], 0)
+        interleave(1)
+        predict(6, 0, 0)
+        predict(0, 0, 1)
+        evacuate_scalar(6, 0, 0)
+        evacuate_scalar(0, 0, 1)
+        store(0)
         blend(2)
-        new_part(4, [5], 0)
+        quantize_h(1)
+        predict(7, 1, 0)
+        predict(4, 1, 1)
+        new_part(1, 3, 0)
         quantize_h(2)
-        predict(2, [2, 6])
+        evacuate_vector(7, 1, 0)
+        evacuate_scalar(4, 1, 1)
+        store(1)
+        predict(2, 2, 0)
+        predict(3, 2, 1)
         blend(3)
-        blend(4)
+        new_part(5, 4, 0)
+        evacuate_scalar(2, 2, 0)
+        evacuate_scalar(3, 2, 1)
+        store(2)
         quantize_h(3)
-        predict(3, [3])
+        predict(6, 3, 0)
+        blend(4)
         quantize_h(4)
-        predict(4, [7], True)
+        evacuate_vector(6, 3, 0)
+        store(3)
+        predict(0, 4, 0)
+        evacuate_vector(0, 4, 0)
+        store(4)

@@ -1,6 +1,7 @@
 from contextlib import ExitStack
 
 import concourse.mybir as mybir
+from concourse.masks import make_identity
 
 K, H, N, T, S = 1024, 512, 512, 2048, 1024
 FLOPS = 2 * S * H * (3 * K + N)
@@ -19,10 +20,11 @@ ACT = mybir.ActivationFunctionType
 P = 128
 PACK = 4
 PASSES = K // (P * PACK)
-HALF = 512
-RUN = 4
-WARM_PASSES = 2
-CHUNKS = [(0, 256), (256, 256), (512, 256), (768, 128), (896, 128)]
+BLOCKS = S // P
+PIECE = 256
+LINE = 4
+GROUPS = [(0, 2), (2, 2), (4, 2), (6, 1), (7, 1)]
+SHIFTED_ROWS = 112
 
 
 def tile_list_session_memory_blend_kernel(
@@ -31,53 +33,61 @@ def tile_list_session_memory_blend_kernel(
     nc = tc.nc
     with ExitStack() as ctx:
         keep = ctx.enter_context(tc.tile_pool(name="keep", bufs=1))
-        ring = ctx.enter_context(tc.tile_pool(name="ring", bufs=5))
         psum = ctx.enter_context(tc.psum_pool(name="psum", bufs=1))
 
-        def tile(shape, dtype, name, tag=""):
-            return keep.tile(shape, dtype, name=name, tag=tag, align_bytes=64)
+        def tile(shape, dtype, name):
+            return keep.tile(shape, dtype, name=name, align_bytes=64)
 
         offsets = keep.tile([P, S // 16], U16, name="offsets")
-        tab_w = [tile([P, T], U32, "tab_w%d" % a, "slot_tab%d" % a) for a in range(PASSES)]
+        tab_w = [tile([P, T], U32, "tab_w%d" % a) for a in range(PASSES)]
         tab_s = tile([P, T], U8, "tab_s")
         warm_in = tile([P, 1], F32, "warm_in")
         warm_out = tile([P, 1], F32, "warm_out")
-        wg_raw = tile([P, PASSES, H], I32, "wg_raw")
-        wo_raw = tile([P, PASSES, H // 2], I32, "wo_raw")
-        wn_raw = [tile([P, PACK, H], F32, "wn_raw%d" % a) for a in range(PASSES)]
-        ws_raw = tile([P, 4, H], U8, "ws_raw")
+        ident = tile([P, P], F32, "ident")
+        wg = [tile([P, H], I32, "wg%d" % a) for a in range(PASSES)]
+        wo = tile([P, PASSES, 2 * H], U8, "wo")
         wg_s = tile([P, PASSES, H], U8, "wg_s")
         wo_s = tile([P, PASSES, H], U8, "wo_s")
-        wg = tile([P, PASSES, H], I32, "wg")
-        wo = tile([P, PASSES, 2 * H], U8, "wo")
+        wn_raw = [tile([P, PACK, H], F32, "wn_raw%d" % a) for a in range(PASSES)]
         wn_bf = [tile([P, PACK * H], BF16, "wn_bf%d" % a) for a in range(PASSES)]
         wn_c = [tile([P, H], U32, "wn_c%d" % a) for a in range(PASSES)]
         wn_s = [tile([P, H], U8, "wn_s%d" % a) for a in range(PASSES)]
+        w2_raw = tile([P, PACK, N], F32, "w2_raw")
         w2_bf = tile([P, PACK * N], BF16, "w2_bf")
         w2_c = tile([P, N], U32, "w2_c")
         w2_s = tile([P, N], U8, "w2_s")
+        bias = tile([P, N // P], F32, "bias")
         v_w = [tile([P, S], U32, "v_w%d" % a) for a in range(PASSES)]
         v_s = tile([P, S], U8, "v_s")
         v_s1 = tile([P, S], U8, "v_s1")
-        sig = [tile([P, PACK, HALF], F32, "sig%d" % h) for h in range(2)]
-        keepold = [tile([P, PACK, HALF], F32, "keepold%d" % h) for h in range(2)]
+        sig = [tile([P, H], F32, "sig%d" % b) for b in range(BLOCKS)]
+        old_part = [tile([P, H], F32, "old_part%d" % b) for b in range(BLOCKS)]
+        new_part = [tile([P, H], F32, "new_part%d" % b) for b in range(BLOCKS)]
+        h_rows = [tile([P, H], BF16, "h_rows%d" % b) for b in range(BLOCKS)]
+        h_bf = [tile([P, n * H], BF16, "h_bf%d" % b) for b, n in GROUPS]
+        h_c = [tile([P, n * P], U32, "h_c%d" % b) for b, n in GROUPS]
+        h_s = [tile([P, n * P], U8, "h_s%d" % b) for b, n in GROUPS]
+        y = [tile([P, N // P, n * P], F32, "y%d" % b) for b, n in GROUPS]
         banks = [psum.tile([P, 512], F32, name="bank%d" % b) for b in range(8)]
 
-        nc.vector.memset(tab_s[:].bitcast(I32), 0)
-        nc.gpsimd.memset(ws_raw[:].rearrange("p a c -> p (a c)").bitcast(I32), 0)
+        nc.gpsimd.memset(tab_s[:].bitcast(I32), 0)
+        nc.gpsimd.memset(wo_s[:].rearrange("p a c -> p (a c)").bitcast(I32), 0)
         nc.vector.memset(warm_in[:], 0.0)
+        nc.vector.memset(wg_s[:].rearrange("p a c -> p (a c)").bitcast(I32), 0)
         nc.vector.memset(v_s1[:].bitcast(I32), 0)
 
         def load_table(a):
             nc.sync.dma_start(
-                out=tab_w[a][:].bitcast(I32),
-                in_=tab_words[a].rearrange("p t i -> p (t i)").bitcast(I32),
+                out=tab_w[a][:].bitcast(I32), in_=tab_words[a].rearrange("p t i -> p (t i)").bitcast(I32)
             )
 
-        def load_weight_scales(queue, first, src):
+        def load_wg(a):
+            nc.sync.dma_start(out=wg[a][:], in_=wg_words[a].rearrange("p c i -> p (c i)").bitcast(I32))
+
+        def load_weight_scales(queue, dst, src):
             for q in range(4):
                 queue.dma_start(
-                    out=ws_raw[32 * q : 32 * q + 4, first : first + 2, :].bitcast(I32),
+                    out=dst[32 * q : 32 * q + 4, :, :].bitcast(I32),
                     in_=src[:, 4 * q : 4 * q + 4, :].rearrange("a r c -> r a c").bitcast(I32),
                 )
 
@@ -87,360 +97,209 @@ def tile_list_session_memory_blend_kernel(
             )
 
         nc.sync.dma_start(offsets[:], offs)
-        load_table(0)
+        with nc.allow_non_contiguous_dma(reason="one bias value for each partition"):
+            nc.sync.dma_start(out=bias[:], in_=bo.rearrange("(u p) -> p u", p=P))
         for q in range(4):
-            nc.scalar.dma_start(
+            nc.sync.dma_start(
                 out=tab_s[32 * q : 32 * q + 8, :].bitcast(I32),
                 in_=tab_scales[:, 4 * q : 4 * q + 4, :].bitcast(I32),
             )
-        load_weight_scales(nc.scalar, 0, wg_scales)
-        load_weight_scales(nc.scalar, 2, wo_scales)
+        load_table(0)
+        load_wg(0)
         nc.scalar.activation(warm_out[:], warm_in[:], ACT.Sigmoid)
-        nc.sync.dma_start(out=wg_raw[:], in_=wg_words.rearrange("a p c i -> p a (c i)").bitcast(I32))
-        nc.sync.dma_start(out=wo_raw[:], in_=wo_words.rearrange("a p c -> p a c").bitcast(I32))
+        load_weight_scales(nc.sync, wg_s, wg_scales)
         load_table(1)
+        nc.vector.tensor_copy(out=v_s[:], in_=tab_s[:].indirect(offsets[:]))
+        nc.sync.dma_start(
+            out=v_s1[0:SHIFTED_ROWS, :].bitcast(I32), in_=v_s[4 : 4 + SHIFTED_ROWS, :].bitcast(I32)
+        )
+        nc.sync.dma_start(out=wo[:].bitcast(I32), in_=wo_words.rearrange("a p c -> p a c").bitcast(I32))
+        load_weight_scales(nc.sync, wo_s, wo_scales)
+        load_wg(1)
+        make_identity(nc, ident[:])
         load_wn(0)
         load_wn(1)
 
-        def gather_words(a, h):
+        def gather_words(a, c):
             nc.vector.tensor_copy(
-                out=v_w[a][:, h * HALF : (h + 1) * HALF], in_=tab_w[a][:].indirect(offsets[:, 32 * h : 32 * h + 32])
+                out=v_w[a][:, c * PIECE : (c + 1) * PIECE],
+                in_=tab_w[a][:].indirect(offsets[:, c * PIECE // 16 : (c + 1) * PIECE // 16]),
             )
 
-        def permute(dst, src, words):
-            nc.vector.tensor_copy(
-                out=dst.rearrange("p a (t g i) -> p a t g i", t=PACK, i=words),
-                in_=src.rearrange("p a (g t i) -> p a t g i", t=PACK, i=words),
-            )
-
-        gather_words(0, 0)
-        nc.vector.tensor_copy(out=v_s[:], in_=tab_s[:].indirect(offsets[:]))
-        for q in range(4):
-            nc.scalar.dma_start(
-                out=v_s1[32 * q : 32 * q + 4, :].bitcast(I32), in_=v_s[32 * q + 4 : 32 * q + 8, :].bitcast(I32)
-            )
-        for w in range(WARM_PASSES):
-            nc.tensor.matmul_mx(
-                out=banks[7][:], lhsT=v_w[0][:, 0:P].bitcast(FP8X4), lhsT_scale=v_s[:, 0:P],
-                rhs=v_w[0][:, 0:HALF].bitcast(FP8X4), rhs_scale=v_s[:, 0:HALF], start=True, stop=True,
-            )
-        permute(wg[:], wg_raw[:], RUN)
-        permute(wg_s[:].bitcast(I32), ws_raw[:, 0:2, :].bitcast(I32), RUN // 4)
-        permute(wo[:].bitcast(I32), wo_raw[:], RUN // 2)
-        permute(wo_s[:].bitcast(I32), ws_raw[:, 2:4, :].bitcast(I32), RUN // 4)
-        gather_words(1, 0)
-        gather_words(0, 1)
-        w2_raw = tile([P, PACK, N], F32, "w2_raw", "slot_tab0")
-        w2_view = w2.rearrange("(g t i) n -> t g i n", t=PACK, i=RUN)
-        for t in range(PACK):
-            nc.sync.dma_start(out=w2_raw[:, t, :], in_=w2_view[t])
-        gather_words(1, 1)
-        bias = tile([P, N // P], F32, "bias", "slot_tab1")
-        with nc.allow_non_contiguous_dma(reason="one bias value for each partition"):
-            nc.sync.dma_start(out=bias[:], in_=bo.rearrange("(u p) -> p u", p=P))
-
-        def moving(a, start, width, shifted):
-            cols = slice(start, start + width)
-            codes = v_w[a][:, cols].bitcast(FP8X4)
+        def project(bank, b, a, codes, scales, shifted):
+            cols = slice(b * P, (b + 1) * P)
             if a == 0:
-                return codes, v_s[:, cols]
-            if shifted:
-                return codes, v_s1[:, cols]
-            return codes, v_s[4:P, cols]
-
-        def gate_pass(bank, h, t, a):
-            codes, scales = moving(a, h * HALF, HALF, False)
-            cols = slice(t * P, (t + 1) * P)
+                v_scales = v_s[:, cols]
+            elif shifted:
+                v_scales = v_s1[:, cols]
+            else:
+                v_scales = v_s[4:P, cols]
             nc.tensor.matmul_mx(
-                out=banks[bank][:], lhsT=wg[:, a, cols].bitcast(FP8X4), lhsT_scale=wg_s[:, a, cols],
+                out=banks[bank][:], lhsT=v_w[a][:, cols].bitcast(FP8X4), lhsT_scale=v_scales,
                 rhs=codes, rhs_scale=scales, start=(a == 0), stop=(a == PASSES - 1),
             )
 
-        def old_pass(bank, h, t, a):
-            codes, scales = moving(a, h * HALF, HALF, True)
-            nc.tensor.matmul_mx(
-                out=banks[bank][:], lhsT=wo[:, a, 2 * t * P : 2 * (t + 1) * P].bitcast(FP4X4),
-                lhsT_scale=wo_s[:, a, t * P : (t + 1) * P],
-                rhs=codes, rhs_scale=scales, start=(a == 0), stop=(a == PASSES - 1),
-            )
+        def gate_pass(b, a):
+            project(b, b, a, wg[a][:].bitcast(FP8X4), wg_s[:, a, :], False)
 
-        def sigmoid(bank, h, t):
-            nc.scalar.activation(sig[h][:, t, :], banks[bank][:], ACT.Sigmoid)
+        def old_passes(b):
+            for a in range(PASSES):
+                project(b, b, a, wo[:, a, :].bitcast(FP4X4), wo_s[:, a, :], True)
 
-        def old_part(bank, h, t):
+        def new_passes(b):
+            for a in range(PASSES):
+                project(b % 4, b, a, wn_c[a][:].bitcast(FP8X4), wn_s[a][:], False)
+
+        def sigmoid(b):
+            nc.scalar.activation(sig[b][:], banks[b][:], ACT.Sigmoid)
+
+        def weigh_old(b):
             nc.vector.scalar_tensor_tensor(
-                out=keepold[h][:, t, :], in0=sig[h][:, t, :], scalar=1.0, in1=banks[bank][:],
-                op0=ALU.subtract, op1=ALU.mult,
+                out=old_part[b][:], in0=sig[b][:], scalar=1.0, in1=banks[b][:], op0=ALU.subtract, op1=ALU.mult
             )
 
-        def cast_views(a, t):
-            dst = wn_bf[a][:, t * 512 : (t + 1) * 512].rearrange("p (g i j) -> p g j i", i=RUN, j=PACK)
-            src = wn_raw[a][:].rearrange("p j (g t i) -> p t g j i", t=PACK, i=RUN)[:, t]
-            return dst, src
+        def weigh_new(b):
+            nc.vector.tensor_tensor(out=new_part[b][:], in0=banks[b % 4][:], in1=sig[b][:], op=ALU.mult)
 
-        def cast_wn_gpsimd(a, t):
-            dst = wn_bf[a][:, t * 512 : (t + 1) * 512].rearrange("p (g i j) -> p g i j", i=RUN, j=PACK)
-            src = wn_raw[a][:].rearrange("p j (g t i) -> p t g i j", t=PACK, i=RUN)[:, t]
-            nc.gpsimd.tensor_scalar(out=dst, in0=src, scalar1=1.0, scalar2=0.0, op0=ALU.mult, op1=ALU.add)
+        def round_views(dst, src, part, run):
+            cols = slice(part * P, (part + 1) * P)
+            to = dst[:, part * PACK * P : (part + 1) * PACK * P].rearrange("p (c i j) -> p c j i", i=run, j=PACK)
+            return to, src[:, :, cols].rearrange("p j (c i) -> p c j i", i=run)
 
-        def cast_wn_scalar(a, t):
-            dst, src = cast_views(a, t)
-            nc.scalar.activation(dst, src, ACT.Copy)
+        def round_scalar(dst, src, part):
+            to, frm = round_views(dst, src, part, LINE)
+            nc.scalar.activation(to, frm, ACT.Copy)
 
-        def cast_wn_vector(a, t):
-            dst, src = cast_views(a, t)
-            nc.vector.tensor_copy(out=dst, in_=src)
+        def round_vector(dst, src, part):
+            to, frm = round_views(dst, src, part, LINE)
+            nc.vector.tensor_copy(out=to, in_=frm)
 
-        def quantize_wn(a):
-            nc.vector.quantize_mx(out=wn_c[a][:].bitcast(FP8X4), scales=wn_s[a][:], in_=wn_bf[a][:])
+        def round_gpsimd(dst, src, part):
+            to, frm = round_views(dst, src, part, 1)
+            nc.gpsimd.tensor_scalar(out=to, in0=frm, scalar1=1.0, scalar2=0.0, op0=ALU.mult, op1=ALU.add)
 
-        def w2_views(part, run):
-            dst = w2_bf[:, part * 512 : (part + 1) * 512].rearrange("p (c i t) -> p c t i", i=run, t=PACK)
-            src = w2_raw[:, :, part * P : (part + 1) * P].rearrange("p t (c i) -> p c t i", i=run)
-            return dst, src
+        def quantize(codes, scales, values):
+            nc.vector.quantize_mx(out=codes.bitcast(FP8X4), scales=scales, in_=values)
 
-        def cast_w2_scalar(part):
-            dst, src = w2_views(part, 4)
-            nc.scalar.activation(dst, src, ACT.Copy)
+        def blend(engine, b):
+            engine.tensor_tensor(
+                out=h_rows[b][:].rearrange("p (u g j) -> p u g j", u=2, j=16),
+                in0=new_part[b][:].rearrange("p (g u j) -> p u g j", u=2, j=16),
+                in1=old_part[b][:].rearrange("p (g u j) -> p u g j", u=2, j=16),
+                op=ALU.subtract,
+            )
 
-        def cast_w2_vector(part):
-            dst, src = w2_views(part, 4)
-            nc.vector.tensor_copy(out=dst, in_=src)
+        def turn_bank(g):
+            return banks[4 + 3 * (g % 2)][:, 0 : 2 * P * GROUPS[g][1]]
 
-        def cast_w2_gpsimd(part):
-            dst, src = w2_views(part, 1)
-            nc.gpsimd.tensor_scalar(out=dst, in0=src, scalar1=1.0, scalar2=0.0, op0=ALU.mult, op1=ALU.add)
-
-        def quantize_w2():
-            nc.vector.quantize_mx(out=w2_c[:].bitcast(FP8X4), scales=w2_s[:], in_=w2_bf[:])
-
-        state = {}
-
-        def new_passes(bank, c, k):
-            start, width = CHUNKS[c]
-            per_bank = 512 // width
-            for j in range(per_bank):
-                t = k * per_bank + j
-                cols = slice(t * P, (t + 1) * P)
-                for a in range(PASSES):
-                    codes, scales = moving(a, start, width, False)
-                    nc.tensor.matmul_mx(
-                        out=banks[bank][:, j * width : (j + 1) * width],
-                        lhsT=wn_c[a][:, cols].bitcast(FP8X4), lhsT_scale=wn_s[a][:, cols],
-                        rhs=codes, rhs_scale=scales, start=(a == 0), stop=(a == PASSES - 1),
+        def turn(g):
+            first, count = GROUPS[g]
+            for k in range(count):
+                words = h_rows[first + k][:].bitcast(F32)
+                for u in range(2):
+                    nc.tensor.transpose(
+                        turn_bank(g)[:, (2 * k + u) * P : (2 * k + u + 1) * P], words[:, u * P : (u + 1) * P], ident[:]
                     )
 
-        def new_part(bank, c, k):
-            start, width = CHUNKS[c]
-            h, off = divmod(start, HALF)
-            per_bank = 512 // width
-            if ("new", c) not in state:
-                state["new", c] = ring.tile([P, PACK, width], F32, name="gated_new", align_bytes=64)
-            ts = slice(k * per_bank, (k + 1) * per_bank)
-            nc.vector.tensor_tensor(
-                out=state["new", c][:, ts, :],
-                in0=banks[bank][:].rearrange("p (t n) -> p t n", n=width),
-                in1=sig[h][:, ts, off : off + width],
-                op=ALU.mult,
-            )
-
-        def blend(c):
-            start, width = CHUNKS[c]
-            h, off = divmod(start, HALF)
-            h_bf = ring.tile([P, PACK * width], BF16, name="h_bf", align_bytes=64)
-            state["h", c] = h_bf
-            nc.vector.tensor_tensor(
-                out=h_bf[:].rearrange("p (c i t) -> p c t i", i=2, t=PACK),
-                in0=state["new", c][:].rearrange("p t (c i) -> p c t i", i=2),
-                in1=keepold[h][:, :, off : off + width].rearrange("p t (c i) -> p c t i", i=2),
-                op=ALU.subtract,
-            )
-
-        def blend_gpsimd(c, k):
-            start, width = CHUNKS[c]
-            h, off = divmod(start, HALF)
-            if ("ht", c) not in state:
-                state["ht", c] = ring.tile([P, PACK, width], BF16, name="h_rows", align_bytes=64)
-            ts = slice(2 * k, 2 * k + 2)
-            nc.gpsimd.tensor_tensor(
-                out=state["ht", c][:, ts, :],
-                in0=state["new", c][:, ts, :],
-                in1=keepold[h][:, ts, off : off + width],
-                op=ALU.subtract,
-            )
-
-        def interleave(c):
-            start, width = CHUNKS[c]
-            h_bf = ring.tile([P, PACK * width], BF16, name="h_bf", align_bytes=64)
-            state["h", c] = h_bf
+        def weave(g):
             nc.scalar.copy(
-                h_bf[:].rearrange("p (c i t) -> p c t i", i=4, t=PACK),
-                state["ht", c][:].rearrange("p t (c i) -> p c t i", i=4),
+                h_bf[g][:].bitcast(F32).rearrange("p (k e u) -> p k e u", e=P, u=2),
+                turn_bank(g).rearrange("p (k u e) -> p k e u", e=P, u=2),
             )
 
-        def quantize_h(c):
-            start, width = CHUNKS[c]
-            h_c = ring.tile([P, width], U32, name="h_c", align_bytes=64)
-            h_s = ring.tile([P, width], U8, name="h_s", align_bytes=64)
-            state["hq", c] = (h_c, h_s)
-            nc.vector.quantize_mx(out=h_c[:].bitcast(FP8X4), scales=h_s[:], in_=state["h", c][:])
+        def quantize_h(g):
+            quantize(h_c[g][:], h_s[g][:], h_bf[g][:])
 
-        def predict(bank, c, k):
-            start, width = CHUNKS[c]
-            per_bank = 512 // width
-            h_c, h_s = state["hq", c]
-            for j in range(per_bank):
-                u = k * per_bank + j
+        def sums(g, u):
+            width = GROUPS[g][1] * P
+            if width == 2 * P:
+                return banks[5 + u // 2][:, (u % 2) * width : (u % 2 + 1) * width]
+            return banks[2 * (g - 3) + u // 2][:, (u % 2) * width : (u % 2 + 1) * width]
+
+        def predict(g):
+            for u in range(N // P):
                 cols = slice(u * P, (u + 1) * P)
                 nc.tensor.matmul_mx(
-                    out=banks[bank][:, j * width : (j + 1) * width],
-                    lhsT=w2_c[:, cols].bitcast(FP8X4), lhsT_scale=w2_s[:, cols],
-                    rhs=h_c[:].bitcast(FP8X4), rhs_scale=h_s[:], start=True, stop=True,
+                    out=sums(g, u), lhsT=w2_c[:, cols].bitcast(FP8X4), lhsT_scale=w2_s[:, cols],
+                    rhs=h_c[g][:].bitcast(FP8X4), rhs_scale=h_s[g][:], start=True, stop=True,
                 )
 
-        def result_tile(c):
-            if ("y", c) not in state:
-                state["y", c] = ring.tile([P, N // P, CHUNKS[c][1]], F32, name="y", align_bytes=64)
-            return state["y", c]
+        def add_bias_scalar(g, us):
+            for u in us:
+                nc.scalar.activation(y[g][:, u, :], sums(g, u), ACT.Identity, bias=bias[:, u : u + 1])
 
-        def evacuate_vector(bank, c, k):
-            start, width = CHUNKS[c]
-            per_bank = 512 // width
-            us = slice(k * per_bank, (k + 1) * per_bank)
-            nc.vector.tensor_tensor(
-                out=result_tile(c)[:, us, :],
-                in0=banks[bank][:].rearrange("p (u n) -> p u n", n=width),
-                in1=bias[:, us].unsqueeze(2).to_broadcast([P, per_bank, width]),
-                op=ALU.add,
-            )
-
-        def evacuate_scalar(bank, c, k):
-            start, width = CHUNKS[c]
-            per_bank = 512 // width
-            for j in range(per_bank):
-                u = k * per_bank + j
-                nc.scalar.activation(
-                    result_tile(c)[:, u, :], banks[bank][:, j * width : (j + 1) * width], ACT.Identity,
-                    bias=bias[:, u : u + 1],
+        def add_bias_vector(g, us):
+            for u in us:
+                nc.vector.tensor_scalar(
+                    out=y[g][:, u, :], in0=sums(g, u), scalar1=bias[:, u : u + 1], scalar2=None, op0=ALU.add
                 )
 
-        def store(c):
-            start, width = CHUNKS[c]
+        def store(g):
+            first, count = GROUPS[g]
             nc.sync.dma_start(
-                out=out.rearrange("(u p) j -> p u j", p=P)[:, :, start : start + width], in_=result_tile(c)[:]
+                out=out.rearrange("(u p) j -> p u j", p=P)[:, :, first * P : (first + count) * P], in_=y[g][:]
             )
 
-        gate_pass(0, 0, 0, 0)
-        gate_pass(1, 0, 1, 0)
-        gate_pass(2, 0, 2, 0)
-        gate_pass(3, 0, 3, 0)
-        cast_wn_scalar(0, 2)
-        cast_wn_scalar(0, 3)
-        cast_wn_vector(0, 0)
-        cast_wn_vector(0, 1)
-        gate_pass(0, 0, 0, 1)
-        old_pass(4, 0, 0, 0)
-        old_pass(4, 0, 0, 1)
-        gate_pass(1, 0, 1, 1)
-        old_pass(5, 0, 1, 0)
-        old_pass(5, 0, 1, 1)
-        gate_pass(2, 0, 2, 1)
-        old_pass(6, 0, 2, 0)
-        old_pass(6, 0, 2, 1)
-        gate_pass(3, 0, 3, 1)
-        old_pass(7, 0, 3, 0)
-        old_pass(7, 0, 3, 1)
-        quantize_wn(0)
-        sigmoid(0, 0, 0)
-        old_part(4, 0, 0)
-        sigmoid(1, 0, 1)
-        old_part(5, 0, 1)
-        cast_wn_gpsimd(1, 3)
-        cast_wn_scalar(1, 2)
-        cast_wn_vector(1, 0)
-        cast_wn_scalar(1, 1)
-        gate_pass(0, 1, 0, 0)
-        gate_pass(0, 1, 0, 1)
-        gate_pass(4, 1, 1, 0)
-        gate_pass(4, 1, 1, 1)
-        sigmoid(2, 0, 2)
-        sigmoid(3, 0, 3)
-        quantize_wn(1)
-        old_part(6, 0, 2)
-        old_part(7, 0, 3)
-        new_passes(1, 0, 0)
-        new_passes(5, 0, 1)
-        cast_w2_scalar(0)
-        cast_w2_scalar(1)
-        cast_w2_scalar(2)
-        cast_w2_gpsimd(3)
-        new_passes(2, 1, 0)
-        new_passes(3, 1, 1)
-        new_part(1, 0, 0)
-        blend_gpsimd(0, 0)
-        new_part(5, 0, 1)
-        blend_gpsimd(0, 1)
-        quantize_w2()
-        sigmoid(0, 1, 0)
-        sigmoid(4, 1, 1)
-        gate_pass(6, 1, 2, 0)
-        gate_pass(6, 1, 2, 1)
-        gate_pass(7, 1, 3, 0)
-        gate_pass(7, 1, 3, 1)
-        new_part(2, 1, 0)
-        blend_gpsimd(1, 0)
-        new_part(3, 1, 1)
-        blend_gpsimd(1, 1)
-        old_pass(1, 1, 0, 0)
-        old_pass(1, 1, 0, 1)
-        old_part(1, 1, 0)
-        old_pass(5, 1, 1, 0)
-        old_pass(5, 1, 1, 1)
-        old_part(5, 1, 1)
-        old_pass(0, 1, 2, 0)
-        old_pass(0, 1, 2, 1)
-        sigmoid(6, 1, 2)
-        old_part(0, 1, 2)
-        old_pass(4, 1, 3, 0)
-        old_pass(4, 1, 3, 1)
-        sigmoid(7, 1, 3)
-        old_part(4, 1, 3)
-        interleave(0)
-        new_passes(2, 2, 0)
-        new_passes(3, 2, 1)
-        new_part(2, 2, 0)
-        new_part(3, 2, 1)
-        new_passes(1, 3, 0)
-        new_passes(5, 4, 0)
-        quantize_h(0)
-        interleave(1)
-        predict(6, 0, 0)
-        predict(0, 0, 1)
-        evacuate_scalar(6, 0, 0)
-        evacuate_scalar(0, 0, 1)
-        store(0)
-        blend(2)
-        quantize_h(1)
-        predict(7, 1, 0)
-        predict(4, 1, 1)
-        new_part(1, 3, 0)
-        quantize_h(2)
-        evacuate_vector(7, 1, 0)
-        evacuate_scalar(4, 1, 1)
-        store(1)
-        predict(2, 2, 0)
-        predict(3, 2, 1)
-        blend(3)
-        new_part(5, 4, 0)
-        evacuate_scalar(2, 2, 0)
-        evacuate_scalar(3, 2, 1)
-        store(2)
-        quantize_h(3)
-        predict(6, 3, 0)
-        blend(4)
-        quantize_h(4)
-        evacuate_vector(6, 3, 0)
-        store(3)
-        predict(0, 4, 0)
-        evacuate_vector(0, 4, 0)
-        store(4)
+        for c in range(S // PIECE):
+            gather_words(0, c)
+            gate_pass(2 * c, 0)
+            gate_pass(2 * c + 1, 0)
+        w2_view = w2.rearrange("(g u i e) n -> u g i (e n)", u=2, i=8, e=2)
+        for u in range(2):
+            nc.sync.dma_start(out=w2_raw[:, 2 * u : 2 * u + 2, :].rearrange("p e n -> p (e n)"), in_=w2_view[u])
+        for c in range(S // PIECE):
+            gather_words(1, c)
+
+        lag = 2
+        for b in range(BLOCKS + lag):
+            if b < BLOCKS:
+                gate_pass(b, 1)
+                sigmoid(b)
+            if b >= lag:
+                old_passes(b - lag)
+                weigh_old(b - lag)
+            if b == 5:
+                round_gpsimd(wn_bf[0], wn_raw[0], 0)
+                round_gpsimd(wn_bf[0], wn_raw[0], 1)
+                round_gpsimd(wn_bf[0], wn_raw[0], 2)
+                round_scalar(wn_bf[0], wn_raw[0], 3)
+            if b == 7:
+                quantize(wn_c[0][:], wn_s[0][:], wn_bf[0][:])
+                round_gpsimd(wn_bf[1], wn_raw[1], 0)
+                round_gpsimd(wn_bf[1], wn_raw[1], 1)
+                round_scalar(wn_bf[1], wn_raw[1], 2)
+                round_scalar(wn_bf[1], wn_raw[1], 3)
+            if b == 8:
+                quantize(wn_c[1][:], wn_s[1][:], wn_bf[1][:])
+        round_scalar(w2_bf, w2_raw, 0)
+        round_scalar(w2_bf, w2_raw, 1)
+        round_gpsimd(w2_bf, w2_raw, 2)
+        round_gpsimd(w2_bf, w2_raw, 3)
+
+        for pair in range(BLOCKS // 2):
+            for b in (2 * pair, 2 * pair + 1):
+                new_passes(b)
+                weigh_new(b)
+            if pair == 0:
+                quantize(w2_c[:], w2_s[:], w2_bf[:])
+            else:
+                quantize_h(pair - 1)
+                predict(pair - 1)
+            blend(nc.vector, 2 * pair)
+            blend(nc.vector, 2 * pair + 1)
+            if pair > 0:
+                add_bias_scalar(pair - 1, range(4))
+                store(pair - 1)
+            if pair < 3:
+                turn(pair)
+                weave(pair)
+        for g in (3, 4):
+            turn(g)
+            weave(g)
+        for g in (3, 4):
+            quantize_h(g)
+            predict(g)
+        for g in (3, 4):
+            add_bias_scalar(g, (0, 1))
+            add_bias_vector(g, (2, 3))
+            store(g)

@@ -21,9 +21,9 @@ P = 128
 PACK = 4
 PASSES = K // (P * PACK)
 BLOCKS = S // P
-PIECE = 256
 LINE = 4
 GROUPS = [(0, 2), (2, 2), (4, 2), (6, 1), (7, 1)]
+SUM_BANKS = [(5, 6), (5, 6), (0, 1), (5, 6), (2, 3)]
 SHIFTED_ROWS = 112
 
 
@@ -35,8 +35,8 @@ def tile_list_session_memory_blend_kernel(
         keep = ctx.enter_context(tc.tile_pool(name="keep", bufs=1))
         psum = ctx.enter_context(tc.psum_pool(name="psum", bufs=1))
 
-        def tile(shape, dtype, name):
-            return keep.tile(shape, dtype, name=name, align_bytes=64)
+        def tile(shape, dtype, name, tag=""):
+            return keep.tile(shape, dtype, name=name, tag=tag, align_bytes=64)
 
         offsets = keep.tile([P, S // 16], U16, name="offsets")
         tab_w = [tile([P, T], U32, "tab_w%d" % a) for a in range(PASSES)]
@@ -49,7 +49,7 @@ def tile_list_session_memory_blend_kernel(
         wg_s = tile([P, PASSES, H], U8, "wg_s")
         wo_s = tile([P, PASSES, H], U8, "wo_s")
         wn_raw = [tile([P, PACK, H], F32, "wn_raw%d" % a) for a in range(PASSES)]
-        wn_bf = [tile([P, PACK * H], BF16, "wn_bf%d" % a) for a in range(PASSES)]
+        wn_bf = [tile([P, PACK * H], BF16, "wn_bf%d" % a, "rounded%d" % a) for a in range(PASSES)]
         wn_c = [tile([P, H], U32, "wn_c%d" % a) for a in range(PASSES)]
         wn_s = [tile([P, H], U8, "wn_s%d" % a) for a in range(PASSES)]
         w2_raw = tile([P, PACK, N], F32, "w2_raw")
@@ -61,7 +61,7 @@ def tile_list_session_memory_blend_kernel(
         v_s = tile([P, S], U8, "v_s")
         v_s1 = tile([P, S], U8, "v_s1")
         sig = [tile([P, H], F32, "sig%d" % b) for b in range(BLOCKS)]
-        old_part = [tile([P, H], F32, "old_part%d" % b) for b in range(BLOCKS)]
+        old_part = {}
         new_part = [tile([P, H], F32, "new_part%d" % b) for b in range(BLOCKS)]
         h_rows = [tile([P, H], BF16, "h_rows%d" % b) for b in range(BLOCKS)]
         h_bf = [tile([P, n * H], BF16, "h_bf%d" % b) for b, n in GROUPS]
@@ -120,10 +120,10 @@ def tile_list_session_memory_blend_kernel(
         load_wn(0)
         load_wn(1)
 
-        def gather_words(a, c):
+        def gather_words(a, first, count):
             nc.vector.tensor_copy(
-                out=v_w[a][:, c * PIECE : (c + 1) * PIECE],
-                in_=tab_w[a][:].indirect(offsets[:, c * PIECE // 16 : (c + 1) * PIECE // 16]),
+                out=v_w[a][:, first * P : (first + count) * P],
+                in_=tab_w[a][:].indirect(offsets[:, first * P // 16 : (first + count) * P // 16]),
             )
 
         def project(bank, b, a, codes, scales, shifted):
@@ -154,6 +154,7 @@ def tile_list_session_memory_blend_kernel(
             nc.scalar.activation(sig[b][:], banks[b][:], ACT.Sigmoid)
 
         def weigh_old(b):
+            old_part[b] = tile([P, H], F32, "old_part%d" % b, "rounded1" if b == 7 else "")
             nc.vector.scalar_tensor_tensor(
                 out=old_part[b][:], in0=sig[b][:], scalar=1.0, in1=banks[b][:], op0=ALU.subtract, op1=ALU.mult
             )
@@ -181,11 +182,11 @@ def tile_list_session_memory_blend_kernel(
         def quantize(codes, scales, values):
             nc.vector.quantize_mx(out=codes.bitcast(FP8X4), scales=scales, in_=values)
 
-        def blend(engine, b):
+        def blend(engine, b, halves=slice(0, 2)):
             engine.tensor_tensor(
-                out=h_rows[b][:].rearrange("p (u g j) -> p u g j", u=2, j=16),
-                in0=new_part[b][:].rearrange("p (g u j) -> p u g j", u=2, j=16),
-                in1=old_part[b][:].rearrange("p (g u j) -> p u g j", u=2, j=16),
+                out=h_rows[b][:].rearrange("p (u g j) -> p u g j", u=2, j=16)[:, halves],
+                in0=new_part[b][:].rearrange("p (g u j) -> p u g j", u=2, j=16)[:, halves],
+                in1=old_part[b][:].rearrange("p (g u j) -> p u g j", u=2, j=16)[:, halves],
                 op=ALU.subtract,
             )
 
@@ -212,9 +213,7 @@ def tile_list_session_memory_blend_kernel(
 
         def sums(g, u):
             width = GROUPS[g][1] * P
-            if width == 2 * P:
-                return banks[5 + u // 2][:, (u % 2) * width : (u % 2 + 1) * width]
-            return banks[2 * (g - 3) + u // 2][:, (u % 2) * width : (u % 2 + 1) * width]
+            return banks[SUM_BANKS[g][u // 2]][:, (u % 2) * width : (u % 2 + 1) * width]
 
         def predict(g):
             for u in range(N // P):
@@ -228,11 +227,14 @@ def tile_list_session_memory_blend_kernel(
             for u in us:
                 nc.scalar.activation(y[g][:, u, :], sums(g, u), ACT.Identity, bias=bias[:, u : u + 1])
 
-        def add_bias_vector(g, us):
-            for u in us:
-                nc.vector.tensor_scalar(
-                    out=y[g][:, u, :], in0=sums(g, u), scalar1=bias[:, u : u + 1], scalar2=None, op0=ALU.add
-                )
+        def add_bias_vector(g):
+            width = GROUPS[g][1] * P
+            nc.vector.tensor_tensor(
+                out=y[g][:, 2:4, :],
+                in0=banks[SUM_BANKS[g][1]][:, 0 : 2 * width].rearrange("p (u n) -> p u n", u=2),
+                in1=bias[:, 2:4].unsqueeze(2).to_broadcast([P, 2, width]),
+                op=ALU.add,
+            )
 
         def store(g):
             first, count = GROUPS[g]
@@ -240,15 +242,15 @@ def tile_list_session_memory_blend_kernel(
                 out=out.rearrange("(u p) j -> p u j", p=P)[:, :, first * P : (first + count) * P], in_=y[g][:]
             )
 
-        for c in range(S // PIECE):
-            gather_words(0, c)
-            gate_pass(2 * c, 0)
-            gate_pass(2 * c + 1, 0)
+        for first, count in ((0, 2), (2, 2), (4, 4)):
+            gather_words(0, first, count)
+            for b in range(first, first + count):
+                gate_pass(b, 0)
         w2_view = w2.rearrange("(g u i e) n -> u g i (e n)", u=2, i=8, e=2)
         for u in range(2):
             nc.sync.dma_start(out=w2_raw[:, 2 * u : 2 * u + 2, :].rearrange("p e n -> p (e n)"), in_=w2_view[u])
-        for c in range(S // PIECE):
-            gather_words(1, c)
+        for first, count in ((0, 2), (2, 2), (4, 4)):
+            gather_words(1, first, count)
 
         lag = 2
         for b in range(BLOCKS + lag):
@@ -258,48 +260,71 @@ def tile_list_session_memory_blend_kernel(
             if b >= lag:
                 old_passes(b - lag)
                 weigh_old(b - lag)
-            if b == 5:
-                round_gpsimd(wn_bf[0], wn_raw[0], 0)
-                round_gpsimd(wn_bf[0], wn_raw[0], 1)
+            if b == 3:
+                round_scalar(wn_bf[0], wn_raw[0], 0)
+                round_scalar(wn_bf[0], wn_raw[0], 1)
                 round_gpsimd(wn_bf[0], wn_raw[0], 2)
-                round_scalar(wn_bf[0], wn_raw[0], 3)
-            if b == 7:
-                quantize(wn_c[0][:], wn_s[0][:], wn_bf[0][:])
+                round_gpsimd(wn_bf[0], wn_raw[0], 3)
+            if b == 5:
                 round_gpsimd(wn_bf[1], wn_raw[1], 0)
-                round_gpsimd(wn_bf[1], wn_raw[1], 1)
+                round_scalar(wn_bf[1], wn_raw[1], 1)
                 round_scalar(wn_bf[1], wn_raw[1], 2)
-                round_scalar(wn_bf[1], wn_raw[1], 3)
+            if b == 6:
+                quantize(wn_c[0][:], wn_s[0][:], wn_bf[0][:])
+            if b == 7:
+                round_vector(wn_bf[1], wn_raw[1], 3)
             if b == 8:
                 quantize(wn_c[1][:], wn_s[1][:], wn_bf[1][:])
-        round_scalar(w2_bf, w2_raw, 0)
-        round_scalar(w2_bf, w2_raw, 1)
-        round_gpsimd(w2_bf, w2_raw, 2)
-        round_gpsimd(w2_bf, w2_raw, 3)
+        for part in range(4):
+            round_scalar(w2_bf, w2_raw, part)
 
-        for pair in range(BLOCKS // 2):
-            for b in (2 * pair, 2 * pair + 1):
-                new_passes(b)
-                weigh_new(b)
-            if pair == 0:
-                quantize(w2_c[:], w2_s[:], w2_bf[:])
+        def finish(g):
+            predict(g)
+            if g < 2:
+                add_bias_scalar(g, range(4))
             else:
-                quantize_h(pair - 1)
-                predict(pair - 1)
-            blend(nc.vector, 2 * pair)
-            blend(nc.vector, 2 * pair + 1)
-            if pair > 0:
-                add_bias_scalar(pair - 1, range(4))
-                store(pair - 1)
-            if pair < 3:
-                turn(pair)
-                weave(pair)
-        for g in (3, 4):
+                add_bias_scalar(g, (0, 1))
+                add_bias_vector(g)
+            store(g)
+
+        def weigh_new_block(b):
+            new_passes(b)
+            weigh_new(b)
+
+        def turn_and_weave(g):
             turn(g)
             weave(g)
-        for g in (3, 4):
-            quantize_h(g)
-            predict(g)
-        for g in (3, 4):
-            add_bias_scalar(g, (0, 1))
-            add_bias_vector(g, (2, 3))
-            store(g)
+
+        weigh_new_block(0)
+        blend(nc.gpsimd, 0)
+        weigh_new_block(1)
+        weigh_new_block(2)
+        blend(nc.vector, 1)
+        turn_and_weave(0)
+        blend(nc.vector, 2)
+        quantize(w2_c[:], w2_s[:], w2_bf[:])
+        weigh_new_block(3)
+        blend(nc.gpsimd, 3)
+        weigh_new_block(4)
+        weigh_new_block(5)
+        turn_and_weave(1)
+        quantize_h(0)
+        finish(0)
+        blend(nc.vector, 4)
+        blend(nc.vector, 5)
+        turn_and_weave(2)
+        quantize_h(1)
+        finish(1)
+        weigh_new_block(6)
+        blend(nc.gpsimd, 6, slice(0, 1))
+        weigh_new_block(7)
+        blend(nc.vector, 6, slice(1, 2))
+        turn_and_weave(3)
+        blend(nc.vector, 7)
+        turn_and_weave(4)
+        quantize_h(2)
+        quantize_h(3)
+        quantize_h(4)
+        finish(2)
+        finish(3)
+        finish(4)

@@ -1,7 +1,6 @@
 from contextlib import ExitStack
 
 import concourse.mybir as mybir
-from concourse.masks import make_identity
 
 K, H, N, T, S = 1024, 512, 512, 2048, 1024
 FLOPS = 2 * S * H * (3 * K + N)
@@ -21,9 +20,11 @@ P = 128
 PACK = 4
 PASSES = K // (P * PACK)
 BLOCKS = S // P
-LINE = 4
+RUN = 4
+HELD = 3
+PIECES = [(0, 2), (2, 2), (4, 4)]
 GROUPS = [(0, 2), (2, 2), (4, 2), (6, 1), (7, 1)]
-SUM_BANKS = [(5, 6), (5, 6), (0, 1), (5, 6), (2, 3)]
+SUM_BANKS = [(4, 5), (6, 7), (4, 5), (0, 1), (2, 3)]
 SHIFTED_ROWS = 112
 
 
@@ -33,23 +34,30 @@ def tile_list_session_memory_blend_kernel(
     nc = tc.nc
     with ExitStack() as ctx:
         keep = ctx.enter_context(tc.tile_pool(name="keep", bufs=1))
+        shared = ctx.enter_context(tc.tile_pool(name="shared", bufs=1))
         psum = ctx.enter_context(tc.psum_pool(name="psum", bufs=1))
 
-        def tile(shape, dtype, name, tag=""):
-            return keep.tile(shape, dtype, name=name, tag=tag, align_bytes=64)
+        def tile(shape, dtype, name):
+            return keep.tile(shape, dtype, name=name, align_bytes=64)
+
+        def placed(shape, dtype, name, offset):
+            return shared.tile(shape, dtype, name=name, align_bytes=64, offset=offset)
 
         offsets = keep.tile([P, S // 16], U16, name="offsets")
         tab_w = [tile([P, T], U32, "tab_w%d" % a) for a in range(PASSES)]
         tab_s = tile([P, T], U8, "tab_s")
         warm_in = tile([P, 1], F32, "warm_in")
         warm_out = tile([P, 1], F32, "warm_out")
-        ident = tile([P, P], F32, "ident")
+        wg_raw = [placed([P, H], I32, "wg_raw0", 10240), placed([P, H], I32, "wg_raw1", 14848)]
+        wg_s_raw = placed([P, PASSES * H], U8, "wg_s_raw", 12288)
+        wo_s_raw = tile([P, PASSES * H], U8, "wo_s_raw")
+        wo_raw = tile([P, PASSES * H // 2], I32, "wo_raw")
         wg = [tile([P, H], I32, "wg%d" % a) for a in range(PASSES)]
-        wo = tile([P, PASSES, 2 * H], U8, "wo")
-        wg_s = tile([P, PASSES, H], U8, "wg_s")
-        wo_s = tile([P, PASSES, H], U8, "wo_s")
+        wo = tile([P, PASSES * 2 * H], U8, "wo")
+        wg_s = tile([P, PASSES * H], U8, "wg_s")
+        wo_s = tile([P, PASSES * H], U8, "wo_s")
         wn_raw = [tile([P, PACK, H], F32, "wn_raw%d" % a) for a in range(PASSES)]
-        wn_bf = [tile([P, PACK * H], BF16, "wn_bf%d" % a, "rounded%d" % a) for a in range(PASSES)]
+        wn_bf = [tile([P, PACK * H], BF16, "wn_bf0"), placed([P, 10 * H], BF16, "wn_bf1", 0)[:, 0 : PACK * H]]
         wn_c = [tile([P, H], U32, "wn_c%d" % a) for a in range(PASSES)]
         wn_s = [tile([P, H], U8, "wn_s%d" % a) for a in range(PASSES)]
         w2_raw = tile([P, PACK, N], F32, "w2_raw")
@@ -57,13 +65,19 @@ def tile_list_session_memory_blend_kernel(
         w2_c = tile([P, N], U32, "w2_c")
         w2_s = tile([P, N], U8, "w2_s")
         bias = tile([P, N // P], F32, "bias")
-        v_w = [tile([P, S], U32, "v_w%d" % a) for a in range(PASSES)]
+        v_w = {
+            (0, 0): tile([P, 2 * P], U32, "v_w00"),
+            (0, 2): placed([P, 2 * P], U32, "v_w02", 12800),
+            (0, 4): placed([P, 4 * P], U32, "v_w04", 10752),
+            (1, 0): tile([P, 2 * P], U32, "v_w10"),
+            (1, 2): placed([P, 2 * P], U32, "v_w12", 15872),
+            (1, 4): placed([P, 4 * P], U32, "v_w14", 13824),
+        }
         v_s = tile([P, S], U8, "v_s")
         v_s1 = tile([P, S], U8, "v_s1")
         sig = [tile([P, H], F32, "sig%d" % b) for b in range(BLOCKS)]
         old_part = {}
         new_part = [tile([P, H], F32, "new_part%d" % b) for b in range(BLOCKS)]
-        h_rows = [tile([P, H], BF16, "h_rows%d" % b) for b in range(BLOCKS)]
         h_bf = [tile([P, n * H], BF16, "h_bf%d" % b) for b, n in GROUPS]
         h_c = [tile([P, n * P], U32, "h_c%d" % b) for b, n in GROUPS]
         h_s = [tile([P, n * P], U8, "h_s%d" % b) for b, n in GROUPS]
@@ -71,9 +85,9 @@ def tile_list_session_memory_blend_kernel(
         banks = [psum.tile([P, 512], F32, name="bank%d" % b) for b in range(8)]
 
         nc.gpsimd.memset(tab_s[:].bitcast(I32), 0)
-        nc.gpsimd.memset(wo_s[:].rearrange("p a c -> p (a c)").bitcast(I32), 0)
+        nc.gpsimd.memset(wo_s_raw[:].bitcast(I32), 0)
         nc.vector.memset(warm_in[:], 0.0)
-        nc.vector.memset(wg_s[:].rearrange("p a c -> p (a c)").bitcast(I32), 0)
+        nc.vector.memset(wg_s_raw[:].bitcast(I32), 0)
         nc.vector.memset(v_s1[:].bitcast(I32), 0)
 
         def load_table(a):
@@ -82,12 +96,12 @@ def tile_list_session_memory_blend_kernel(
             )
 
         def load_wg(a):
-            nc.sync.dma_start(out=wg[a][:], in_=wg_words[a].rearrange("p c i -> p (c i)").bitcast(I32))
+            nc.sync.dma_start(out=wg_raw[a][:], in_=wg_words[a].rearrange("p c i -> p (c i)").bitcast(I32))
 
-        def load_weight_scales(queue, dst, src):
+        def load_weight_scales(dst, src):
             for q in range(4):
-                queue.dma_start(
-                    out=dst[32 * q : 32 * q + 4, :, :].bitcast(I32),
+                nc.sync.dma_start(
+                    out=dst[32 * q : 32 * q + 4, :].bitcast(I32).rearrange("r (a c) -> r a c", a=PASSES),
                     in_=src[:, 4 * q : 4 * q + 4, :].rearrange("a r c -> r a c").bitcast(I32),
                 )
 
@@ -107,26 +121,37 @@ def tile_list_session_memory_blend_kernel(
         load_table(0)
         load_wg(0)
         nc.scalar.activation(warm_out[:], warm_in[:], ACT.Sigmoid)
-        load_weight_scales(nc.sync, wg_s, wg_scales)
+        load_weight_scales(wg_s_raw, wg_scales)
         load_table(1)
         nc.vector.tensor_copy(out=v_s[:], in_=tab_s[:].indirect(offsets[:]))
         nc.sync.dma_start(
             out=v_s1[0:SHIFTED_ROWS, :].bitcast(I32), in_=v_s[4 : 4 + SHIFTED_ROWS, :].bitcast(I32)
         )
-        nc.sync.dma_start(out=wo[:].bitcast(I32), in_=wo_words.rearrange("a p c -> p a c").bitcast(I32))
-        load_weight_scales(nc.sync, wo_s, wo_scales)
+        nc.sync.dma_start(
+            out=wo_raw[:].rearrange("p (a c) -> p a c", a=PASSES), in_=wo_words.rearrange("a p c -> p a c").bitcast(I32)
+        )
+        load_weight_scales(wo_s_raw, wo_scales)
         load_wg(1)
-        make_identity(nc, ident[:])
         load_wn(0)
         load_wn(1)
+        w2_view = w2.rearrange("(g t i) n -> t g i n", t=PACK, i=RUN)
+        for t in range(PACK):
+            nc.sync.dma_start(out=w2_raw[:, t, :], in_=w2_view[t])
 
         def gather_words(a, first, count):
             nc.vector.tensor_copy(
-                out=v_w[a][:, first * P : (first + count) * P],
+                out=v_w[a, first][:],
                 in_=tab_w[a][:].indirect(offsets[:, first * P // 16 : (first + count) * P // 16]),
             )
 
-        def project(bank, b, a, codes, scales, shifted):
+        def permute(dst, src, passes, words):
+            nc.vector.tensor_copy(
+                out=dst.rearrange("p (a t g i) -> p a t g i", a=passes, t=PACK, i=words),
+                in_=src.rearrange("p (a g t i) -> p a t g i", a=passes, t=PACK, i=words),
+            )
+
+        def project(bank, b, a, codes, width, dtype, scales, shifted):
+            first = max(f for f, count in PIECES if f <= b)
             cols = slice(b * P, (b + 1) * P)
             if a == 0:
                 v_scales = v_s[:, cols]
@@ -134,79 +159,75 @@ def tile_list_session_memory_blend_kernel(
                 v_scales = v_s1[:, cols]
             else:
                 v_scales = v_s[4:P, cols]
-            nc.tensor.matmul_mx(
-                out=banks[bank][:], lhsT=v_w[a][:, cols].bitcast(FP8X4), lhsT_scale=v_scales,
-                rhs=codes, rhs_scale=scales, start=(a == 0), stop=(a == PASSES - 1),
-            )
+            for t in range(PACK):
+                nc.tensor.matmul_mx(
+                    out=banks[bank][:, t * P : (t + 1) * P],
+                    lhsT=codes[:, t * width : (t + 1) * width].bitcast(dtype), lhsT_scale=scales[:, t * P : (t + 1) * P],
+                    rhs=v_w[a, first][:, (b - first) * P : (b - first + 1) * P].bitcast(FP8X4), rhs_scale=v_scales,
+                    start=(a == 0 and t == 0), stop=(a == PASSES - 1 and t == PACK - 1),
+                )
 
         def gate_pass(b, a):
-            project(b, b, a, wg[a][:].bitcast(FP8X4), wg_s[:, a, :], False)
+            project(b, b, a, wg[a], P, FP8X4, wg_s[:, a * H : (a + 1) * H], False)
 
         def old_passes(b):
             for a in range(PASSES):
-                project(b, b, a, wo[:, a, :].bitcast(FP4X4), wo_s[:, a, :], True)
+                project(b, b, a, wo[:, 2 * a * H : 2 * (a + 1) * H], 2 * P, FP4X4, wo_s[:, a * H : (a + 1) * H], True)
 
         def new_passes(b):
             for a in range(PASSES):
-                project(b % 4, b, a, wn_c[a][:].bitcast(FP8X4), wn_s[a][:], False)
+                project(b % 4, b, a, wn_c[a], P, FP8X4, wn_s[a], False)
+
+        def woven(bank):
+            return banks[bank][:].rearrange("p (t e) -> p e t", t=PACK)
+
+        def by_event(values):
+            return values[:].rearrange("p (e t) -> p e t", t=PACK)
 
         def sigmoid(b):
-            nc.scalar.activation(sig[b][:], banks[b][:], ACT.Sigmoid)
+            nc.scalar.activation(by_event(sig[b]), woven(b), ACT.Sigmoid)
 
         def weigh_old(b):
-            old_part[b] = tile([P, H], F32, "old_part%d" % b, "rounded1" if b == 7 else "")
+            if b < HELD:
+                old_part[b] = tile([P, H], F32, "old_part%d" % b)
+            else:
+                old_part[b] = placed([P, H], F32, "old_part%d" % b, 4 * H * (b - HELD))
             nc.vector.scalar_tensor_tensor(
-                out=old_part[b][:], in0=sig[b][:], scalar=1.0, in1=banks[b][:], op0=ALU.subtract, op1=ALU.mult
+                out=by_event(old_part[b]), in0=by_event(sig[b]), scalar=1.0, in1=woven(b),
+                op0=ALU.subtract, op1=ALU.mult,
             )
 
         def weigh_new(b):
-            nc.vector.tensor_tensor(out=new_part[b][:], in0=banks[b % 4][:], in1=sig[b][:], op=ALU.mult)
+            new_passes(b)
+            nc.vector.tensor_tensor(out=by_event(new_part[b]), in0=woven(b % 4), in1=by_event(sig[b]), op=ALU.mult)
 
-        def round_views(dst, src, part, run):
-            cols = slice(part * P, (part + 1) * P)
-            to = dst[:, part * PACK * P : (part + 1) * PACK * P].rearrange("p (c i j) -> p c j i", i=run, j=PACK)
-            return to, src[:, :, cols].rearrange("p j (c i) -> p c j i", i=run)
+        def round_wn_scalar(a, t):
+            nc.scalar.activation(
+                wn_bf[a][:, t * H : (t + 1) * H].rearrange("p (g i j) -> p g j i", i=RUN, j=PACK),
+                wn_raw[a][:].rearrange("p j (g t i) -> p t g j i", t=PACK, i=RUN)[:, t],
+                ACT.Copy,
+            )
 
-        def round_scalar(dst, src, part):
-            to, frm = round_views(dst, src, part, LINE)
-            nc.scalar.activation(to, frm, ACT.Copy)
+        def round_wn_vector(a):
+            nc.vector.tensor_copy(
+                out=wn_bf[a].rearrange("p (t g i j) -> p t g j i", t=PACK, i=RUN, j=PACK),
+                in_=wn_raw[a][:].rearrange("p j (g t i) -> p t g j i", t=PACK, i=RUN),
+            )
 
-        def round_vector(dst, src, part):
-            to, frm = round_views(dst, src, part, LINE)
-            nc.vector.tensor_copy(out=to, in_=frm)
-
-        def round_gpsimd(dst, src, part):
-            to, frm = round_views(dst, src, part, 1)
-            nc.gpsimd.tensor_scalar(out=to, in0=frm, scalar1=1.0, scalar2=0.0, op0=ALU.mult, op1=ALU.add)
+        def round_w2(part):
+            nc.scalar.activation(
+                w2_bf[:, part * N : (part + 1) * N].rearrange("p (c i t) -> p c t i", i=RUN, t=PACK),
+                w2_raw[:, :, part * P : (part + 1) * P].rearrange("p t (c i) -> p c t i", i=RUN),
+                ACT.Copy,
+            )
 
         def quantize(codes, scales, values):
             nc.vector.quantize_mx(out=codes.bitcast(FP8X4), scales=scales, in_=values)
 
-        def blend(engine, b, halves=slice(0, 2)):
-            engine.tensor_tensor(
-                out=h_rows[b][:].rearrange("p (u g j) -> p u g j", u=2, j=16)[:, halves],
-                in0=new_part[b][:].rearrange("p (g u j) -> p u g j", u=2, j=16)[:, halves],
-                in1=old_part[b][:].rearrange("p (g u j) -> p u g j", u=2, j=16)[:, halves],
-                op=ALU.subtract,
-            )
-
-        def turn_bank(g):
-            return banks[4 + 3 * (g % 2)][:, 0 : 2 * P * GROUPS[g][1]]
-
-        def turn(g):
-            first, count = GROUPS[g]
-            for k in range(count):
-                words = h_rows[first + k][:].bitcast(F32)
-                for u in range(2):
-                    nc.tensor.transpose(
-                        turn_bank(g)[:, (2 * k + u) * P : (2 * k + u + 1) * P], words[:, u * P : (u + 1) * P], ident[:]
-                    )
-
-        def weave(g):
-            nc.scalar.copy(
-                h_bf[g][:].bitcast(F32).rearrange("p (k e u) -> p k e u", e=P, u=2),
-                turn_bank(g).rearrange("p (k u e) -> p k e u", e=P, u=2),
-            )
+        def blend(engine, b):
+            g = max(k for k, (first, count) in enumerate(GROUPS) if first <= b)
+            at = (b - GROUPS[g][0]) * H
+            engine.tensor_tensor(out=h_bf[g][:, at : at + H], in0=new_part[b][:], in1=old_part[b][:], op=ALU.subtract)
 
         def quantize_h(g):
             quantize(h_c[g][:], h_s[g][:], h_bf[g][:])
@@ -236,95 +257,81 @@ def tile_list_session_memory_blend_kernel(
                 op=ALU.add,
             )
 
-        def store(g):
-            first, count = GROUPS[g]
-            nc.sync.dma_start(
-                out=out.rearrange("(u p) j -> p u j", p=P)[:, :, first * P : (first + count) * P], in_=y[g][:]
-            )
-
-        for first, count in ((0, 2), (2, 2), (4, 4)):
-            gather_words(0, first, count)
-            for b in range(first, first + count):
-                gate_pass(b, 0)
-        w2_view = w2.rearrange("(g u i e) n -> u g i (e n)", u=2, i=8, e=2)
-        for u in range(2):
-            nc.sync.dma_start(out=w2_raw[:, 2 * u : 2 * u + 2, :].rearrange("p e n -> p (e n)"), in_=w2_view[u])
-        for first, count in ((0, 2), (2, 2), (4, 4)):
-            gather_words(1, first, count)
-
-        lag = 2
-        for b in range(BLOCKS + lag):
-            if b < BLOCKS:
-                gate_pass(b, 1)
-                sigmoid(b)
-            if b >= lag:
-                old_passes(b - lag)
-                weigh_old(b - lag)
-            if b == 3:
-                round_scalar(wn_bf[0], wn_raw[0], 0)
-                round_scalar(wn_bf[0], wn_raw[0], 1)
-                round_gpsimd(wn_bf[0], wn_raw[0], 2)
-                round_gpsimd(wn_bf[0], wn_raw[0], 3)
-            if b == 5:
-                round_gpsimd(wn_bf[1], wn_raw[1], 0)
-                round_scalar(wn_bf[1], wn_raw[1], 1)
-                round_scalar(wn_bf[1], wn_raw[1], 2)
-            if b == 6:
-                quantize(wn_c[0][:], wn_s[0][:], wn_bf[0][:])
-            if b == 7:
-                round_vector(wn_bf[1], wn_raw[1], 3)
-            if b == 8:
-                quantize(wn_c[1][:], wn_s[1][:], wn_bf[1][:])
-        for part in range(4):
-            round_scalar(w2_bf, w2_raw, part)
-
         def finish(g):
+            first, count = GROUPS[g]
             predict(g)
-            if g < 2:
+            if count == 2:
                 add_bias_scalar(g, range(4))
             else:
                 add_bias_scalar(g, (0, 1))
                 add_bias_vector(g)
-            store(g)
+            nc.sync.dma_start(
+                out=out.rearrange("(u p) j -> p u j", p=P)[:, :, first * P : (first + count) * P], in_=y[g][:]
+            )
 
-        def weigh_new_block(b):
-            new_passes(b)
-            weigh_new(b)
+        gather_words(0, 0, 2)
+        permute(wg[0][:], wg_raw[0][:], 1, RUN)
+        permute(wg_s[:].bitcast(I32), wg_s_raw[:].bitcast(I32), PASSES, RUN // 4)
+        gather_words(0, 2, 2)
+        gather_words(0, 4, 4)
+        for b in range(BLOCKS):
+            gate_pass(b, 0)
+        gather_words(1, 0, 2)
+        permute(wg[1][:], wg_raw[1][:], 1, RUN)
+        permute(wo[:].bitcast(I32), wo_raw[:], PASSES, RUN // 2)
+        permute(wo_s[:].bitcast(I32), wo_s_raw[:].bitcast(I32), PASSES, RUN // 4)
+        gather_words(1, 2, 2)
+        gather_words(1, 4, 4)
 
-        def turn_and_weave(g):
-            turn(g)
-            weave(g)
+        lag = 2
+        for b in range(BLOCKS):
+            gate_pass(b, 1)
+            sigmoid(b)
+            if b >= lag:
+                old_passes(b - lag)
+            if lag <= b < lag + HELD:
+                weigh_old(b - lag)
+            if b == 2:
+                for t in range(PACK):
+                    round_wn_scalar(0, t)
+            if b == 4:
+                quantize(wn_c[0][:], wn_s[0][:], wn_bf[0][:])
+        round_wn_vector(1)
+        quantize(wn_c[1][:], wn_s[1][:], wn_bf[1])
+        for part in range(4):
+            round_w2(part)
 
-        weigh_new_block(0)
+        weigh_old(3)
+        weigh_new(0)
         blend(nc.gpsimd, 0)
-        weigh_new_block(1)
-        weigh_new_block(2)
-        blend(nc.vector, 1)
-        turn_and_weave(0)
-        blend(nc.vector, 2)
+        weigh_old(4)
+        weigh_new(1)
+        blend(nc.gpsimd, 1)
+        weigh_old(5)
+        weigh_new(2)
+        old_passes(6)
+        old_passes(7)
         quantize(w2_c[:], w2_s[:], w2_bf[:])
-        weigh_new_block(3)
-        blend(nc.gpsimd, 3)
-        weigh_new_block(4)
-        weigh_new_block(5)
-        turn_and_weave(1)
         quantize_h(0)
+        blend(nc.vector, 2)
         finish(0)
-        blend(nc.vector, 4)
-        blend(nc.vector, 5)
-        turn_and_weave(2)
+        weigh_new(3)
+        blend(nc.gpsimd, 3)
+        weigh_old(6)
+        weigh_new(4)
+        blend(nc.gpsimd, 4)
+        weigh_old(7)
+        weigh_new(5)
         quantize_h(1)
+        blend(nc.vector, 5)
         finish(1)
-        weigh_new_block(6)
-        blend(nc.gpsimd, 6, slice(0, 1))
-        weigh_new_block(7)
-        blend(nc.vector, 6, slice(1, 2))
-        turn_and_weave(3)
-        blend(nc.vector, 7)
-        turn_and_weave(4)
+        weigh_new(6)
         quantize_h(2)
+        finish(2)
+        weigh_new(7)
+        blend(nc.vector, 6)
+        blend(nc.vector, 7)
         quantize_h(3)
         quantize_h(4)
-        finish(2)
         finish(3)
         finish(4)

@@ -84,11 +84,11 @@ def tile_list_session_memory_blend_kernel(
         y = [tile([P, N // P, n * P], F32, "y%d" % b) for b, n in GROUPS]
         banks = [psum.tile([P, 512], F32, name="bank%d" % b) for b in range(8)]
 
-        nc.gpsimd.memset(tab_s[:].bitcast(I32), 0)
-        nc.gpsimd.memset(wo_s_raw[:].bitcast(I32), 0)
+        nc.vector.memset(tab_s[:].bitcast(I32), 0)
         nc.vector.memset(warm_in[:], 0.0)
         nc.vector.memset(wg_s_raw[:].bitcast(I32), 0)
-        nc.vector.memset(v_s1[:].bitcast(I32), 0)
+        nc.vector.memset(wo_s_raw[:].bitcast(I32), 0)
+        nc.vector.memset(v_s1[96:P, :].bitcast(I32), 0)
 
         def load_table(a):
             nc.sync.dma_start(
@@ -259,15 +259,16 @@ def tile_list_session_memory_blend_kernel(
 
         def finish(g):
             first, count = GROUPS[g]
+            rows = out.rearrange("(u p) j -> p u j", p=P)[:, :, first * P : (first + count) * P]
             predict(g)
+            add_bias_scalar(g, (0, 1))
             if count == 2:
-                add_bias_scalar(g, range(4))
+                nc.sync.dma_start(out=rows[:, 0:2, :], in_=y[g][:, 0:2, :])
+                add_bias_scalar(g, (2, 3))
+                nc.sync.dma_start(out=rows[:, 2:4, :], in_=y[g][:, 2:4, :])
             else:
-                add_bias_scalar(g, (0, 1))
                 add_bias_vector(g)
-            nc.sync.dma_start(
-                out=out.rearrange("(u p) j -> p u j", p=P)[:, :, first * P : (first + count) * P], in_=y[g][:]
-            )
+                nc.sync.dma_start(out=rows, in_=y[g][:])
 
         gather_words(0, 0, 2)
         permute(wg[0][:], wg_raw[0][:], 1, RUN)

@@ -21,11 +21,13 @@ PACK = 4
 PASSES = K // (P * PACK)
 BLOCKS = S // P
 RUN = 4
-HELD = 3
-PIECES = [(0, 2), (2, 2), (4, 4)]
+PIECES = [(0, 4), (4, 4)]
 GROUPS = [(0, 2), (2, 2), (4, 2), (6, 1), (7, 1)]
-SUM_BANKS = [(4, 5), (6, 7), (4, 5), (0, 1), (2, 3)]
-SHIFTED_ROWS = 112
+SUM_BANKS = [(0, 1), (2, 3), (0, 1), (4, 5), (2, 3)]
+ROWS = 16
+EARLY = 4
+OLD_AT = {3: 28672, 5: 2048, 6: 4096, 7: 6144}
+NEW_AT = {4: 8192, 5: 10240, 6: 16384, 7: 18432}
 
 
 def tile_list_session_memory_blend_kernel(
@@ -46,18 +48,19 @@ def tile_list_session_memory_blend_kernel(
         offsets = keep.tile([P, S // 16], U16, name="offsets")
         tab_w = [tile([P, T], U32, "tab_w%d" % a) for a in range(PASSES)]
         tab_s = tile([P, T], U8, "tab_s")
+        picked_s = tile([P, S], U8, "picked_s")
+        wg_s_raw = tile([P, H], U8, "wg_s_raw")
+        wo_s_raw = tile([P, H], U8, "wo_s_raw")
+        rows_s = tile([P, S + 2 * H], U8, "rows_s")
+        planes = [tile([P, S + 2 * H], U8, "planes%d" % a) for a in range(PASSES)]
         warm_in = tile([P, 1], F32, "warm_in")
         warm_out = tile([P, 1], F32, "warm_out")
-        wg_raw = [placed([P, H], I32, "wg_raw0", 10240), placed([P, H], I32, "wg_raw1", 14848)]
-        wg_s_raw = placed([P, PASSES * H], U8, "wg_s_raw", 12288)
-        wo_s_raw = tile([P, PASSES * H], U8, "wo_s_raw")
+        wg_raw = tile([P, PASSES * H], I32, "wg_raw")
         wo_raw = tile([P, PASSES * H // 2], I32, "wo_raw")
-        wg = [tile([P, H], I32, "wg%d" % a) for a in range(PASSES)]
+        wg = tile([P, PASSES * H], I32, "wg")
         wo = tile([P, PASSES * 2 * H], U8, "wo")
-        wg_s = tile([P, PASSES * H], U8, "wg_s")
-        wo_s = tile([P, PASSES * H], U8, "wo_s")
-        wn_raw = [tile([P, PACK, H], F32, "wn_raw%d" % a) for a in range(PASSES)]
-        wn_bf = [tile([P, PACK * H], BF16, "wn_bf0"), placed([P, 10 * H], BF16, "wn_bf1", 0)[:, 0 : PACK * H]]
+        wn_raw = [tile([P, PACK, H], F32, "wn_raw0"), placed([P, PACK, H], F32, "wn_raw1", 20480)]
+        wn_bf = [tile([P, PACK * H], BF16, "wn_bf0"), placed([P, PACK * H], BF16, "wn_bf1", 28672)]
         wn_c = [tile([P, H], U32, "wn_c%d" % a) for a in range(PASSES)]
         wn_s = [tile([P, H], U8, "wn_s%d" % a) for a in range(PASSES)]
         w2_raw = tile([P, PACK, N], F32, "w2_raw")
@@ -65,78 +68,74 @@ def tile_list_session_memory_blend_kernel(
         w2_c = tile([P, N], U32, "w2_c")
         w2_s = tile([P, N], U8, "w2_s")
         bias = tile([P, N // P], F32, "bias")
-        v_w = {
-            (0, 0): tile([P, 2 * P], U32, "v_w00"),
-            (0, 2): placed([P, 2 * P], U32, "v_w02", 12800),
-            (0, 4): placed([P, 4 * P], U32, "v_w04", 10752),
-            (1, 0): tile([P, 2 * P], U32, "v_w10"),
-            (1, 2): placed([P, 2 * P], U32, "v_w12", 15872),
-            (1, 4): placed([P, 4 * P], U32, "v_w14", 13824),
-        }
-        v_s = tile([P, S], U8, "v_s")
-        v_s1 = tile([P, S], U8, "v_s1")
-        sig = [tile([P, H], F32, "sig%d" % b) for b in range(BLOCKS)]
-        old_part = {}
-        new_part = [tile([P, H], F32, "new_part%d" % b) for b in range(BLOCKS)]
-        h_bf = [tile([P, n * H], BF16, "h_bf%d" % b) for b, n in GROUPS]
+        v_w = {(a, f): tile([P, n * P], U32, "v_w%d%d" % (a, f)) for a in range(PASSES) for f, n in PIECES}
+        sig = [
+            placed([P, H], F32, "sig%d" % b, 20480 + 4 * H * (b - 5)) if b >= 5 else tile([P, H], F32, "sig%d" % b)
+            for b in range(BLOCKS)
+        ]
+        old_part = [
+            placed([P, H], F32, "old_part%d" % b, OLD_AT[b]) if b in OLD_AT else tile([P, H], F32, "old_part%d" % b)
+            for b in range(BLOCKS)
+        ]
+        new_part = [
+            placed([P, H], F32, "new_part%d" % b, NEW_AT[b]) if b in NEW_AT else tile([P, H], F32, "new_part%d" % b)
+            for b in range(BLOCKS)
+        ]
+        h_bf = [
+            placed([P, 20 * H], BF16, "h_bf0", 0)[:, 0 : 2 * H],
+            placed([P, 8 * H], BF16, "h_bf2", 12288)[:, 0 : 2 * H],
+            placed([P, 2 * H], BF16, "h_bf4", 14336)[:],
+        ] + [tile([P, n * H], BF16, "h_bf%d" % b)[:] for b, n in GROUPS[3:]]
         h_c = [tile([P, n * P], U32, "h_c%d" % b) for b, n in GROUPS]
         h_s = [tile([P, n * P], U8, "h_s%d" % b) for b, n in GROUPS]
         y = [tile([P, N // P, n * P], F32, "y%d" % b) for b, n in GROUPS]
         banks = [psum.tile([P, 512], F32, name="bank%d" % b) for b in range(8)]
 
-        nc.vector.memset(tab_s[:].bitcast(I32), 0)
+        nc.vector.memset(tab_s[32:64, :].bitcast(I32), 0)
+        nc.vector.memset(tab_s[64:P, :].bitcast(I32), 0)
         nc.vector.memset(warm_in[:], 0.0)
-        nc.vector.memset(wg_s_raw[:].bitcast(I32), 0)
-        nc.vector.memset(wo_s_raw[:].bitcast(I32), 0)
-        nc.vector.memset(v_s1[96:P, :].bitcast(I32), 0)
+        for a in range(PASSES):
+            nc.gpsimd.memset(planes[a][:].bitcast(I32), 0)
+
+        def load_rows(queue, dst, src):
+            queue.dma_start(out=dst[0 : PASSES * ROWS, :].bitcast(I32), in_=src.rearrange("a q c -> (a q) c").bitcast(I32))
 
         def load_table(a):
             nc.sync.dma_start(
                 out=tab_w[a][:].bitcast(I32), in_=tab_words[a].rearrange("p t i -> p (t i)").bitcast(I32)
             )
 
-        def load_wg(a):
-            nc.sync.dma_start(out=wg_raw[a][:], in_=wg_words[a].rearrange("p c i -> p (c i)").bitcast(I32))
+        def load_wg():
+            nc.sync.dma_start(
+                out=wg_raw[:].rearrange("p (a c) -> p a c", a=PASSES),
+                in_=wg_words.rearrange("a p c i -> p a (c i)").bitcast(I32),
+            )
 
-        def load_weight_scales(dst, src):
+        def load_wo():
+            nc.sync.dma_start(
+                out=wo_raw[:].rearrange("p (a c) -> p a c", a=PASSES),
+                in_=wo_words.rearrange("a p c -> p a c").bitcast(I32),
+            )
+
+        def load_wn(a, first, count):
+            rows = wn[a * 512 : (a + 1) * 512, :].rearrange("(p j) c -> p j c", j=PACK)
+            nc.sync.dma_start(out=wn_raw[a][:, first : first + count, :], in_=rows[:, first : first + count, :])
+
+        def load_w2():
+            w2_view = w2.rearrange("(g t i) n -> t g i n", t=PACK, i=RUN)
+            for t in range(PACK):
+                nc.sync.dma_start(out=w2_raw[:, t, :], in_=w2_view[t])
+
+        def load_bias():
+            with nc.allow_non_contiguous_dma(reason="one bias value for each partition"):
+                nc.sync.dma_start(out=bias[:], in_=bo.rearrange("(u p) -> p u", p=P))
+
+        def spread(a):
             for q in range(4):
+                first = ROWS * a + 4 * q
                 nc.sync.dma_start(
-                    out=dst[32 * q : 32 * q + 4, :].bitcast(I32).rearrange("r (a c) -> r a c", a=PASSES),
-                    in_=src[:, 4 * q : 4 * q + 4, :].rearrange("a r c -> r a c").bitcast(I32),
+                    out=planes[a][32 * q : 32 * q + 4, :].bitcast(I32), in_=rows_s[first : first + 4, :].bitcast(I32)
                 )
-
-        def load_wn(a):
-            nc.sync.dma_start(
-                out=wn_raw[a][:], in_=wn[a * 512 : (a + 1) * 512, :].rearrange("(p j) c -> p j c", j=PACK)
-            )
-
-        nc.sync.dma_start(offsets[:], offs)
-        with nc.allow_non_contiguous_dma(reason="one bias value for each partition"):
-            nc.sync.dma_start(out=bias[:], in_=bo.rearrange("(u p) -> p u", p=P))
-        for q in range(4):
-            nc.sync.dma_start(
-                out=tab_s[32 * q : 32 * q + 8, :].bitcast(I32),
-                in_=tab_scales[:, 4 * q : 4 * q + 4, :].bitcast(I32),
-            )
-        load_table(0)
-        load_wg(0)
-        nc.scalar.activation(warm_out[:], warm_in[:], ACT.Sigmoid)
-        load_weight_scales(wg_s_raw, wg_scales)
-        load_table(1)
-        nc.vector.tensor_copy(out=v_s[:], in_=tab_s[:].indirect(offsets[:]))
-        nc.sync.dma_start(
-            out=v_s1[0:SHIFTED_ROWS, :].bitcast(I32), in_=v_s[4 : 4 + SHIFTED_ROWS, :].bitcast(I32)
-        )
-        nc.sync.dma_start(
-            out=wo_raw[:].rearrange("p (a c) -> p a c", a=PASSES), in_=wo_words.rearrange("a p c -> p a c").bitcast(I32)
-        )
-        load_weight_scales(wo_s_raw, wo_scales)
-        load_wg(1)
-        load_wn(0)
-        load_wn(1)
-        w2_view = w2.rearrange("(g t i) n -> t g i n", t=PACK, i=RUN)
-        for t in range(PACK):
-            nc.sync.dma_start(out=w2_raw[:, t, :], in_=w2_view[t])
 
         def gather_words(a, first, count):
             nc.vector.tensor_copy(
@@ -150,33 +149,30 @@ def tile_list_session_memory_blend_kernel(
                 in_=src.rearrange("p (a g t i) -> p a t g i", a=passes, t=PACK, i=words),
             )
 
-        def project(bank, b, a, codes, width, dtype, scales, shifted):
+        def project(bank, b, a, codes, width, dtype, scales):
             first = max(f for f, count in PIECES if f <= b)
-            cols = slice(b * P, (b + 1) * P)
-            if a == 0:
-                v_scales = v_s[:, cols]
-            elif shifted:
-                v_scales = v_s1[:, cols]
-            else:
-                v_scales = v_s[4:P, cols]
             for t in range(PACK):
                 nc.tensor.matmul_mx(
                     out=banks[bank][:, t * P : (t + 1) * P],
                     lhsT=codes[:, t * width : (t + 1) * width].bitcast(dtype), lhsT_scale=scales[:, t * P : (t + 1) * P],
-                    rhs=v_w[a, first][:, (b - first) * P : (b - first + 1) * P].bitcast(FP8X4), rhs_scale=v_scales,
+                    rhs=v_w[a, first][:, (b - first) * P : (b - first + 1) * P].bitcast(FP8X4),
+                    rhs_scale=planes[a][:, b * P : (b + 1) * P],
                     start=(a == 0 and t == 0), stop=(a == PASSES - 1 and t == PACK - 1),
                 )
 
         def gate_pass(b, a):
-            project(b, b, a, wg[a], P, FP8X4, wg_s[:, a * H : (a + 1) * H], False)
+            project(b, b, a, wg[:, a * H : (a + 1) * H], P, FP8X4, planes[a][:, S : S + H])
 
         def old_passes(b):
             for a in range(PASSES):
-                project(b, b, a, wo[:, 2 * a * H : 2 * (a + 1) * H], 2 * P, FP4X4, wo_s[:, a * H : (a + 1) * H], True)
+                project(b, b, a, wo[:, 2 * a * H : 2 * (a + 1) * H], 2 * P, FP4X4, planes[a][:, S + H : S + 2 * H])
+
+        def new_bank(b):
+            return EARLY + b % EARLY
 
         def new_passes(b):
             for a in range(PASSES):
-                project(b % 4, b, a, wn_c[a], P, FP8X4, wn_s[a], False)
+                project(new_bank(b), b, a, wn_c[a], P, FP8X4, wn_s[a])
 
         def woven(bank):
             return banks[bank][:].rearrange("p (t e) -> p e t", t=PACK)
@@ -188,18 +184,15 @@ def tile_list_session_memory_blend_kernel(
             nc.scalar.activation(by_event(sig[b]), woven(b), ACT.Sigmoid)
 
         def weigh_old(b):
-            if b < HELD:
-                old_part[b] = tile([P, H], F32, "old_part%d" % b)
-            else:
-                old_part[b] = placed([P, H], F32, "old_part%d" % b, 4 * H * (b - HELD))
             nc.vector.scalar_tensor_tensor(
                 out=by_event(old_part[b]), in0=by_event(sig[b]), scalar=1.0, in1=woven(b),
                 op0=ALU.subtract, op1=ALU.mult,
             )
 
         def weigh_new(b):
-            new_passes(b)
-            nc.vector.tensor_tensor(out=by_event(new_part[b]), in0=woven(b % 4), in1=by_event(sig[b]), op=ALU.mult)
+            nc.vector.tensor_tensor(
+                out=by_event(new_part[b]), in0=woven(new_bank(b)), in1=by_event(sig[b]), op=ALU.mult
+            )
 
         def round_wn_scalar(a, t):
             nc.scalar.activation(
@@ -208,10 +201,11 @@ def tile_list_session_memory_blend_kernel(
                 ACT.Copy,
             )
 
-        def round_wn_vector(a):
+        def round_wn_vector(a, first, count):
+            tiles = slice(first, first + count)
             nc.vector.tensor_copy(
-                out=wn_bf[a].rearrange("p (t g i j) -> p t g j i", t=PACK, i=RUN, j=PACK),
-                in_=wn_raw[a][:].rearrange("p j (g t i) -> p t g j i", t=PACK, i=RUN),
+                out=wn_bf[a][:].rearrange("p (t g i j) -> p t g j i", t=PACK, i=RUN, j=PACK)[:, tiles],
+                in_=wn_raw[a][:].rearrange("p j (g t i) -> p t g j i", t=PACK, i=RUN)[:, tiles],
             )
 
         def round_w2(part):
@@ -230,7 +224,7 @@ def tile_list_session_memory_blend_kernel(
             engine.tensor_tensor(out=h_bf[g][:, at : at + H], in0=new_part[b][:], in1=old_part[b][:], op=ALU.subtract)
 
         def quantize_h(g):
-            quantize(h_c[g][:], h_s[g][:], h_bf[g][:])
+            quantize(h_c[g][:], h_s[g][:], h_bf[g])
 
         def sums(g, u):
             width = GROUPS[g][1] * P
@@ -270,67 +264,103 @@ def tile_list_session_memory_blend_kernel(
                 add_bias_vector(g)
                 nc.sync.dma_start(out=rows, in_=y[g][:])
 
-        gather_words(0, 0, 2)
-        permute(wg[0][:], wg_raw[0][:], 1, RUN)
-        permute(wg_s[:].bitcast(I32), wg_s_raw[:].bitcast(I32), PASSES, RUN // 4)
-        gather_words(0, 2, 2)
-        gather_words(0, 4, 4)
+        rows32 = slice(0, PASSES * ROWS)
+        nc.sync.dma_start(offsets[:], offs)
+        load_rows(nc.sync, tab_s, tab_scales)
+        load_rows(nc.sync, wg_s_raw, wg_scales)
+        load_rows(nc.sync, wo_s_raw, wo_scales)
+        load_wg()
+        load_table(0)
+        load_table(1)
+        nc.scalar.activation(warm_out[:], warm_in[:], ACT.Sigmoid)
+        nc.vector.tensor_copy(out=picked_s[:], in_=tab_s[:].indirect(offsets[:]))
+        permute(rows_s[rows32, S : S + H].bitcast(I32), wg_s_raw[rows32, :].bitcast(I32), 1, RUN // 4)
+        permute(rows_s[rows32, S + H : S + 2 * H].bitcast(I32), wo_s_raw[rows32, :].bitcast(I32), 1, RUN // 4)
+        nc.vector.tensor_copy(out=rows_s[rows32, 0:S].bitcast(I32), in_=picked_s[rows32, :].bitcast(I32))
+        permute(wg[:, 0:H], wg_raw[:, 0:H], 1, RUN)
+        permute(wg[:, H : 2 * H], wg_raw[:, H : 2 * H], 1, RUN)
+        spread(0)
+        load_wo()
+        load_wn(0, 0, 2)
+        spread(1)
+        load_wn(0, 2, 2)
+        load_wn(1, 0, PACK)
+        load_w2()
+        load_bias()
+        for k in range(5):
+            nc.tensor.matmul_mx(
+                out=banks[7][:], lhsT=wg[:, 0:P].bitcast(FP8X4), lhsT_scale=tab_s[:, 0:P],
+                rhs=wg[:, 0:H].bitcast(FP8X4), rhs_scale=tab_s[:, 0:H], start=True, stop=True,
+            )
+
+        for first, count in PIECES:
+            gather_words(0, first, count)
         for b in range(BLOCKS):
             gate_pass(b, 0)
-        gather_words(1, 0, 2)
-        permute(wg[1][:], wg_raw[1][:], 1, RUN)
+        for first, count in PIECES:
+            gather_words(1, first, count)
         permute(wo[:].bitcast(I32), wo_raw[:], PASSES, RUN // 2)
-        permute(wo_s[:].bitcast(I32), wo_s_raw[:].bitcast(I32), PASSES, RUN // 4)
-        gather_words(1, 2, 2)
-        gather_words(1, 4, 4)
+        round_wn_vector(0, 0, PACK)
+        quantize(wn_c[0][:], wn_s[0][:], wn_bf[0][:])
 
-        lag = 2
-        for b in range(BLOCKS):
+        for b in range(EARLY + 1):
             gate_pass(b, 1)
             sigmoid(b)
-            if b >= lag:
-                old_passes(b - lag)
-            if lag <= b < lag + HELD:
-                weigh_old(b - lag)
-            if b == 2:
-                for t in range(PACK):
-                    round_wn_scalar(0, t)
-            if b == 4:
-                quantize(wn_c[0][:], wn_s[0][:], wn_bf[0][:])
-        round_wn_vector(1)
-        quantize(wn_c[1][:], wn_s[1][:], wn_bf[1])
+        for b in range(3):
+            old_passes(b)
+        round_wn_scalar(1, 2)
+        round_wn_scalar(1, 3)
+        for b in range(EARLY + 1, BLOCKS):
+            gate_pass(b, 1)
+            sigmoid(b)
+        old_passes(3)
+        weigh_old(0)
+        round_wn_vector(1, 0, 2)
+        weigh_old(1)
+        quantize(wn_c[1][:], wn_s[1][:], wn_bf[1][:])
+        weigh_old(2)
         for part in range(4):
             round_w2(part)
 
-        weigh_old(3)
+        new_passes(0)
         weigh_new(0)
         blend(nc.gpsimd, 0)
-        weigh_old(4)
+        weigh_old(3)
+        new_passes(1)
         weigh_new(1)
         blend(nc.gpsimd, 1)
-        weigh_old(5)
+        new_passes(2)
         weigh_new(2)
-        old_passes(6)
-        old_passes(7)
+        old_passes(4)
+        weigh_old(4)
+        new_passes(3)
+        weigh_new(3)
         quantize(w2_c[:], w2_s[:], w2_bf[:])
         quantize_h(0)
-        blend(nc.vector, 2)
-        finish(0)
-        weigh_new(3)
+        blend(nc.gpsimd, 2)
         blend(nc.gpsimd, 3)
-        weigh_old(6)
+        old_passes(5)
+        weigh_old(5)
+        new_passes(4)
         weigh_new(4)
-        blend(nc.gpsimd, 4)
-        weigh_old(7)
+        old_passes(6)
+        weigh_old(6)
+        finish(0)
+        new_passes(5)
         weigh_new(5)
+        old_passes(7)
+        weigh_old(7)
         quantize_h(1)
-        blend(nc.vector, 5)
-        finish(1)
+        blend(nc.gpsimd, 4)
+        new_passes(6)
         weigh_new(6)
+        new_passes(7)
+        finish(1)
+        weigh_new(7)
+        blend(nc.vector, 5)
+        blend(nc.vector, 6)
         quantize_h(2)
         finish(2)
-        weigh_new(7)
-        blend(nc.vector, 6)
         blend(nc.vector, 7)
         quantize_h(3)
         quantize_h(4)

@@ -22,12 +22,12 @@ PASSES = K // (P * PACK)
 BLOCKS = S // P
 RUN = 4
 PIECES = [(0, 4), (4, 4)]
-GROUPS = [(0, 2), (2, 2), (4, 2), (6, 1), (7, 1)]
-SUM_BANKS = [(0, 1), (2, 3), (0, 1), (4, 5), (2, 3)]
+GROUPS = [(0, 2), (2, 2), (4, 2), (6, 2)]
+SUM_BANKS = [(4, 5), (6, 7), (4, 5), (6, 7)]
 ROWS = 16
 EARLY = 4
-OLD_AT = {3: 28672, 5: 2048, 6: 4096, 7: 6144}
-NEW_AT = {4: 8192, 5: 10240, 6: 16384, 7: 18432}
+HALF = S // 2
+WIDE = 2 * P
 
 
 def tile_list_session_memory_blend_kernel(
@@ -55,12 +55,12 @@ def tile_list_session_memory_blend_kernel(
         planes = [tile([P, S + 2 * H], U8, "planes%d" % a) for a in range(PASSES)]
         warm_in = tile([P, 1], F32, "warm_in")
         warm_out = tile([P, 1], F32, "warm_out")
-        wg_raw = tile([P, PASSES * H], I32, "wg_raw")
+        wg_raw = [tile([P, H], I32, "wg_raw0"), placed([P, H], I32, "wg_raw1", 32768)]
         wo_raw = tile([P, PASSES * H // 2], I32, "wo_raw")
         wg = tile([P, PASSES * H], I32, "wg")
         wo = tile([P, PASSES * 2 * H], U8, "wo")
         wn_raw = [tile([P, PACK, H], F32, "wn_raw0"), placed([P, PACK, H], F32, "wn_raw1", 20480)]
-        wn_bf = [tile([P, PACK * H], BF16, "wn_bf0"), placed([P, PACK * H], BF16, "wn_bf1", 28672)]
+        wn_bf = [tile([P, PACK * H], BF16, "wn_bf0"), tile([P, PACK * H], BF16, "wn_bf1")]
         wn_c = [tile([P, H], U32, "wn_c%d" % a) for a in range(PASSES)]
         wn_s = [tile([P, H], U8, "wn_s%d" % a) for a in range(PASSES)]
         w2_raw = tile([P, PACK, N], F32, "w2_raw")
@@ -68,25 +68,18 @@ def tile_list_session_memory_blend_kernel(
         w2_c = tile([P, N], U32, "w2_c")
         w2_s = tile([P, N], U8, "w2_s")
         bias = tile([P, N // P], F32, "bias")
-        v_w = {(a, f): tile([P, n * P], U32, "v_w%d%d" % (a, f)) for a in range(PASSES) for f, n in PIECES}
-        sig = [
-            placed([P, H], F32, "sig%d" % b, 20480 + 4 * H * (b - 5)) if b >= 5 else tile([P, H], F32, "sig%d" % b)
-            for b in range(BLOCKS)
-        ]
-        old_part = [
-            placed([P, H], F32, "old_part%d" % b, OLD_AT[b]) if b in OLD_AT else tile([P, H], F32, "old_part%d" % b)
-            for b in range(BLOCKS)
-        ]
-        new_part = [
-            placed([P, H], F32, "new_part%d" % b, NEW_AT[b]) if b in NEW_AT else tile([P, H], F32, "new_part%d" % b)
-            for b in range(BLOCKS)
-        ]
-        h_bf = [
-            placed([P, 20 * H], BF16, "h_bf0", 0)[:, 0 : 2 * H],
-            placed([P, 8 * H], BF16, "h_bf2", 12288)[:, 0 : 2 * H],
-            placed([P, 2 * H], BF16, "h_bf4", 14336)[:],
-        ] + [tile([P, n * H], BF16, "h_bf%d" % b)[:] for b, n in GROUPS[3:]]
-        h_c = [tile([P, n * P], U32, "h_c%d" % b) for b, n in GROUPS]
+        v_w = {(a, f): tile([P, n * P], U32, "v_w%d%d" % (a, f)) for a, f, n in [(0, 0, 4), (0, 4, 4), (1, 0, 4)]}
+        v_w[1, 4] = placed([P, 4 * P], U32, "v_w14", 32768)
+        sig = {
+            (0, 0): tile([P, 2, HALF], F32, "sig00"),
+            (0, 1): tile([P, 2, HALF], F32, "sig01"),
+            (1, 0): tile([P, 2, HALF], F32, "sig10"),
+            (1, 1): placed([P, 2, HALF], F32, "sig11", 20480),
+        }
+        old_part = [tile([P, PACK, HALF], F32, "old%d" % half) for half in range(2)]
+        new_part = [tile([P, PACK, WIDE], F32, "new%d" % g) for g in range(4)]
+        h_bf = [tile([P, 2 * H], BF16, "h_bf%d" % g)[:] for g in range(4)]
+        h_c = [tile([P, WIDE], U32, "h_c%d" % g) for g in range(4)]
         h_s = [tile([P, n * P], U8, "h_s%d" % b) for b, n in GROUPS]
         y = [tile([P, N // P, n * P], F32, "y%d" % b) for b, n in GROUPS]
         banks = [psum.tile([P, 512], F32, name="bank%d" % b) for b in range(8)]
@@ -105,11 +98,8 @@ def tile_list_session_memory_blend_kernel(
                 out=tab_w[a][:].bitcast(I32), in_=tab_words[a].rearrange("p t i -> p (t i)").bitcast(I32)
             )
 
-        def load_wg():
-            nc.sync.dma_start(
-                out=wg_raw[:].rearrange("p (a c) -> p a c", a=PASSES),
-                in_=wg_words.rearrange("a p c i -> p a (c i)").bitcast(I32),
-            )
+        def load_wg(a):
+            nc.sync.dma_start(out=wg_raw[a][:], in_=wg_words[a].rearrange("p c i -> p (c i)").bitcast(I32))
 
         def load_wo():
             nc.sync.dma_start(
@@ -149,49 +139,71 @@ def tile_list_session_memory_blend_kernel(
                 in_=src.rearrange("p (a g t i) -> p a t g i", a=passes, t=PACK, i=words),
             )
 
-        def project(bank, b, a, codes, width, dtype, scales):
-            first = max(f for f, count in PIECES if f <= b)
-            for t in range(PACK):
-                nc.tensor.matmul_mx(
-                    out=banks[bank][:, t * P : (t + 1) * P],
-                    lhsT=codes[:, t * width : (t + 1) * width].bitcast(dtype), lhsT_scale=scales[:, t * P : (t + 1) * P],
-                    rhs=v_w[a, first][:, (b - first) * P : (b - first + 1) * P].bitcast(FP8X4),
-                    rhs_scale=planes[a][:, b * P : (b + 1) * P],
-                    start=(a == 0 and t == 0), stop=(a == PASSES - 1 and t == PACK - 1),
-                )
-
-        def gate_pass(b, a):
-            project(b, b, a, wg[:, a * H : (a + 1) * H], P, FP8X4, planes[a][:, S : S + H])
-
-        def old_passes(b):
-            for a in range(PASSES):
-                project(b, b, a, wo[:, 2 * a * H : 2 * (a + 1) * H], 2 * P, FP4X4, planes[a][:, S + H : S + 2 * H])
-
-        def new_bank(b):
-            return EARLY + b % EARLY
-
-        def new_passes(b):
-            for a in range(PASSES):
-                project(new_bank(b), b, a, wn_c[a], P, FP8X4, wn_s[a])
-
-        def woven(bank):
-            return banks[bank][:].rearrange("p (t e) -> p e t", t=PACK)
-
-        def by_event(values):
-            return values[:].rearrange("p (e t) -> p e t", t=PACK)
-
-        def sigmoid(b):
-            nc.scalar.activation(by_event(sig[b]), woven(b), ACT.Sigmoid)
-
-        def weigh_old(b):
-            nc.vector.scalar_tensor_tensor(
-                out=by_event(old_part[b]), in0=by_event(sig[b]), scalar=1.0, in1=woven(b),
-                op0=ALU.subtract, op1=ALU.mult,
+        def gate_pass(half, t, a):
+            nc.tensor.matmul_mx(
+                out=banks[PACK * half + t][:],
+                lhsT=wg[:, a * H + t * P : a * H + (t + 1) * P].bitcast(FP8X4),
+                lhsT_scale=planes[a][:, S + t * P : S + (t + 1) * P],
+                rhs=v_w[a, PACK * half][:].bitcast(FP8X4), rhs_scale=planes[a][:, half * HALF : (half + 1) * HALF],
+                start=(a == 0), stop=(a == PASSES - 1),
             )
 
-        def weigh_new(b):
+        def old_passes(half, t):
+            for a in range(PASSES):
+                at = a * H + t * P
+                nc.tensor.matmul_mx(
+                    out=banks[PACK * half + t][:],
+                    lhsT=wo[:, 2 * at : 2 * (at + P)].bitcast(FP4X4),
+                    lhsT_scale=planes[a][:, S + H + t * P : S + H + (t + 1) * P],
+                    rhs=v_w[a, PACK * half][:].bitcast(FP8X4),
+                    rhs_scale=planes[a][:, half * HALF : (half + 1) * HALF],
+                    start=(a == 0), stop=(a == PASSES - 1),
+                )
+
+        def new_bank(g, u):
+            return banks[2 * (g % 2) + u][:].rearrange("p (t e) -> p t e", t=2)
+
+        def in_half(g):
+            return slice((g % 2) * WIDE, (g % 2 + 1) * WIDE)
+
+        def new_passes(g, u):
+            for a in range(PASSES):
+                for k in range(2):
+                    cols = slice((2 * u + k) * P, (2 * u + k + 1) * P)
+                    nc.tensor.matmul_mx(
+                        out=new_bank(g, u)[:, k, :],
+                        lhsT=wn_c[a][:, cols].bitcast(FP8X4), lhsT_scale=wn_s[a][:, cols],
+                        rhs=v_w[a, PACK * (g // 2)][:, in_half(g)].bitcast(FP8X4),
+                        rhs_scale=planes[a][:, g * WIDE : (g + 1) * WIDE],
+                        start=(a == 0 and k == 0), stop=(a == PASSES - 1 and k == 1),
+                    )
+
+        def sigmoid(half, t):
+            nc.scalar.activation(sig[half, t // 2][:, t % 2, :], banks[PACK * half + t][:], ACT.Sigmoid)
+
+        def weigh_old(half, t):
+            nc.vector.scalar_tensor_tensor(
+                out=old_part[half][:, t, :], in0=sig[half, t // 2][:, t % 2, :], scalar=1.0,
+                in1=banks[PACK * half + t][:], op0=ALU.subtract, op1=ALU.mult,
+            )
+
+        def weigh_new(g, u):
             nc.vector.tensor_tensor(
-                out=by_event(new_part[b]), in0=woven(new_bank(b)), in1=by_event(sig[b]), op=ALU.mult
+                out=new_part[g][:, 2 * u : 2 * u + 2, :], in0=new_bank(g, u), in1=sig[g // 2, u][:, :, in_half(g)], op=ALU.mult
+            )
+
+        def parts(b):
+            new = new_part[b // 2][:, :, (b % 2) * P : (b % 2 + 1) * P]
+            old = old_part[b // PACK][:, :, (b % PACK) * P : (b % PACK + 1) * P]
+            return new, old, h_bf[b // 2][:, (b % 2) * H : (b % 2 + 1) * H]
+
+        def blend_woven(b):
+            new, old, woven = parts(b)
+            nc.vector.tensor_tensor(
+                out=woven.rearrange("p (c i t) -> p c t i", i=2, t=PACK),
+                in0=new.rearrange("p t (c i) -> p c t i", i=2),
+                in1=old.rearrange("p t (c i) -> p c t i", i=2),
+                op=ALU.subtract,
             )
 
         def round_wn_scalar(a, t):
@@ -217,11 +229,6 @@ def tile_list_session_memory_blend_kernel(
 
         def quantize(codes, scales, values):
             nc.vector.quantize_mx(out=codes.bitcast(FP8X4), scales=scales, in_=values)
-
-        def blend(engine, b):
-            g = max(k for k, (first, count) in enumerate(GROUPS) if first <= b)
-            at = (b - GROUPS[g][0]) * H
-            engine.tensor_tensor(out=h_bf[g][:, at : at + H], in0=new_part[b][:], in1=old_part[b][:], op=ALU.subtract)
 
         def quantize_h(g):
             quantize(h_c[g][:], h_s[g][:], h_bf[g])
@@ -256,20 +263,21 @@ def tile_list_session_memory_blend_kernel(
             rows = out.rearrange("(u p) j -> p u j", p=P)[:, :, first * P : (first + count) * P]
             predict(g)
             add_bias_scalar(g, (0, 1))
-            if count == 2:
+            if g < len(GROUPS) - 1:
                 nc.sync.dma_start(out=rows[:, 0:2, :], in_=y[g][:, 0:2, :])
                 add_bias_scalar(g, (2, 3))
                 nc.sync.dma_start(out=rows[:, 2:4, :], in_=y[g][:, 2:4, :])
             else:
                 add_bias_vector(g)
-                nc.sync.dma_start(out=rows, in_=y[g][:])
+                nc.sync.dma_start(out=rows[:, 0:2, :], in_=y[g][:, 0:2, :])
+                nc.sync.dma_start(out=rows[:, 2:4, :], in_=y[g][:, 2:4, :])
 
         rows32 = slice(0, PASSES * ROWS)
         nc.sync.dma_start(offsets[:], offs)
         load_rows(nc.sync, tab_s, tab_scales)
         load_rows(nc.sync, wg_s_raw, wg_scales)
         load_rows(nc.sync, wo_s_raw, wo_scales)
-        load_wg()
+        load_wg(0)
         load_table(0)
         load_table(1)
         nc.scalar.activation(warm_out[:], warm_in[:], ACT.Sigmoid)
@@ -277,9 +285,9 @@ def tile_list_session_memory_blend_kernel(
         permute(rows_s[rows32, S : S + H].bitcast(I32), wg_s_raw[rows32, :].bitcast(I32), 1, RUN // 4)
         permute(rows_s[rows32, S + H : S + 2 * H].bitcast(I32), wo_s_raw[rows32, :].bitcast(I32), 1, RUN // 4)
         nc.vector.tensor_copy(out=rows_s[rows32, 0:S].bitcast(I32), in_=picked_s[rows32, :].bitcast(I32))
-        permute(wg[:, 0:H], wg_raw[:, 0:H], 1, RUN)
-        permute(wg[:, H : 2 * H], wg_raw[:, H : 2 * H], 1, RUN)
+        permute(wg[:, 0:H], wg_raw[0][:], 1, RUN)
         spread(0)
+        load_wg(1)
         load_wo()
         load_wn(0, 0, 2)
         spread(1)
@@ -289,80 +297,59 @@ def tile_list_session_memory_blend_kernel(
         load_bias()
         for k in range(5):
             nc.tensor.matmul_mx(
-                out=banks[7][:], lhsT=wg[:, 0:P].bitcast(FP8X4), lhsT_scale=tab_s[:, 0:P],
-                rhs=wg[:, 0:H].bitcast(FP8X4), rhs_scale=tab_s[:, 0:H], start=True, stop=True,
+                out=banks[7][:], lhsT=wg_raw[0][:, 0:P].bitcast(FP8X4), lhsT_scale=picked_s[:, 0:P],
+                rhs=wg_raw[0][:].bitcast(FP8X4), rhs_scale=picked_s[:, 0:H], start=True, stop=True,
             )
 
         for first, count in PIECES:
             gather_words(0, first, count)
-        for b in range(BLOCKS):
-            gate_pass(b, 0)
-        for first, count in PIECES:
-            gather_words(1, first, count)
+        for half in range(2):
+            for t in range(PACK):
+                gate_pass(half, t, 0)
+        gather_words(1, 0, 4)
+        permute(wg[:, H : 2 * H], wg_raw[1][:], 1, RUN)
+        gather_words(1, 4, 4)
         permute(wo[:].bitcast(I32), wo_raw[:], PASSES, RUN // 2)
         round_wn_vector(0, 0, PACK)
         quantize(wn_c[0][:], wn_s[0][:], wn_bf[0][:])
 
-        for b in range(EARLY + 1):
-            gate_pass(b, 1)
-            sigmoid(b)
-        for b in range(3):
-            old_passes(b)
+        for t in range(PACK):
+            gate_pass(0, t, 1)
+            sigmoid(0, t)
+        for t in range(PACK):
+            gate_pass(1, t, 1)
+        sigmoid(1, 0)
+        sigmoid(1, 1)
+        for t in range(PACK):
+            old_passes(0, t)
         round_wn_scalar(1, 2)
         round_wn_scalar(1, 3)
-        for b in range(EARLY + 1, BLOCKS):
-            gate_pass(b, 1)
-            sigmoid(b)
-        old_passes(3)
-        weigh_old(0)
+        sigmoid(1, 2)
+        sigmoid(1, 3)
+        for t in range(PACK):
+            old_passes(1, t)
+        weigh_old(0, 0)
+        weigh_old(0, 1)
         round_wn_vector(1, 0, 2)
-        weigh_old(1)
+        weigh_old(0, 2)
         quantize(wn_c[1][:], wn_s[1][:], wn_bf[1][:])
-        weigh_old(2)
+        weigh_old(0, 3)
+        for t in range(PACK):
+            weigh_old(1, t)
         for part in range(4):
             round_w2(part)
 
-        new_passes(0)
-        weigh_new(0)
-        blend(nc.gpsimd, 0)
-        weigh_old(3)
-        new_passes(1)
-        weigh_new(1)
-        blend(nc.gpsimd, 1)
-        new_passes(2)
-        weigh_new(2)
-        old_passes(4)
-        weigh_old(4)
-        new_passes(3)
-        weigh_new(3)
-        quantize(w2_c[:], w2_s[:], w2_bf[:])
-        quantize_h(0)
-        blend(nc.gpsimd, 2)
-        blend(nc.gpsimd, 3)
-        old_passes(5)
-        weigh_old(5)
-        new_passes(4)
-        weigh_new(4)
-        old_passes(6)
-        weigh_old(6)
-        finish(0)
-        new_passes(5)
-        weigh_new(5)
-        old_passes(7)
-        weigh_old(7)
-        quantize_h(1)
-        blend(nc.gpsimd, 4)
-        new_passes(6)
-        weigh_new(6)
-        new_passes(7)
-        finish(1)
-        weigh_new(7)
-        blend(nc.vector, 5)
-        blend(nc.vector, 6)
-        quantize_h(2)
-        finish(2)
-        blend(nc.vector, 7)
+        for g in range(4):
+            new_passes(g, 0)
+            weigh_new(g, 0)
+            if g > 0:
+                quantize_h(g - 1)
+                finish(g - 1)
+            new_passes(g, 1)
+            weigh_new(g, 1)
+            if g == 0:
+                quantize(w2_c[:], w2_s[:], w2_bf[:])
+            blend_woven(2 * g)
+            blend_woven(2 * g + 1)
         quantize_h(3)
-        quantize_h(4)
         finish(3)
-        finish(4)

@@ -23,7 +23,9 @@ BLOCKS = S // P
 RUN = 4
 PIECES = [(0, 4), (4, 4)]
 GROUPS = [(0, 2), (2, 2), (4, 2), (6, 2)]
-SUM_BANKS = [(4, 5), (6, 7), (4, 5), (6, 7)]
+SUM_BANKS = [(4, 5), (6, 7), (2, 3)]
+NEW_BANKS = [0, 2, 0, 4]
+LAST_BANKS = [0, 1, 6, 7]
 ROWS = 16
 EARLY = 4
 HALF = S // 2
@@ -55,11 +57,11 @@ def tile_list_session_memory_blend_kernel(
         planes = [tile([P, S + 2 * H], U8, "planes%d" % a) for a in range(PASSES)]
         warm_in = tile([P, 1], F32, "warm_in")
         warm_out = tile([P, 1], F32, "warm_out")
-        wg_raw = [tile([P, H], I32, "wg_raw0"), placed([P, H], I32, "wg_raw1", 32768)]
-        wo_raw = tile([P, PASSES * H // 2], I32, "wo_raw")
+        wg_raw = [tile([P, H], I32, "wg_raw0"), tile([P, H], I32, "wg_raw1")]
+        wo_raw = placed([P, PASSES * H // 2], I32, "wo_raw", 32768)
         wg = tile([P, PASSES * H], I32, "wg")
         wo = tile([P, PASSES * 2 * H], U8, "wo")
-        wn_raw = [tile([P, PACK, H], F32, "wn_raw0"), placed([P, PACK, H], F32, "wn_raw1", 20480)]
+        wn_raw = [placed([P, PACK, H], F32, "wn_raw0", 40960), tile([P, PACK, H], F32, "wn_raw1")]
         wn_bf = [tile([P, PACK * H], BF16, "wn_bf0"), tile([P, PACK * H], BF16, "wn_bf1")]
         wn_c = [tile([P, H], U32, "wn_c%d" % a) for a in range(PASSES)]
         wn_s = [tile([P, H], U8, "wn_s%d" % a) for a in range(PASSES)]
@@ -74,14 +76,15 @@ def tile_list_session_memory_blend_kernel(
             (0, 0): tile([P, 2, HALF], F32, "sig00"),
             (0, 1): tile([P, 2, HALF], F32, "sig01"),
             (1, 0): tile([P, 2, HALF], F32, "sig10"),
-            (1, 1): placed([P, 2, HALF], F32, "sig11", 20480),
+            (1, 1): tile([P, 2, HALF], F32, "sig11"),
         }
-        old_part = [tile([P, PACK, HALF], F32, "old%d" % half) for half in range(2)]
+        old_part = [placed([P, PACK, HALF], F32, "old0", 40960), tile([P, PACK, HALF], F32, "old1")]
         new_part = [tile([P, PACK, WIDE], F32, "new%d" % g) for g in range(4)]
         h_bf = [tile([P, 2 * H], BF16, "h_bf%d" % g)[:] for g in range(4)]
         h_c = [tile([P, WIDE], U32, "h_c%d" % g) for g in range(4)]
         h_s = [tile([P, n * P], U8, "h_s%d" % b) for b, n in GROUPS]
-        y = [tile([P, N // P, n * P], F32, "y%d" % b) for b, n in GROUPS]
+        y = [tile([P, N // P, n * P], F32, "y%d" % b) for b, n in GROUPS[:-1]]
+        last = [tile([P, WIDE], F32, "last%d" % u) for u in range(N // P)]
         banks = [psum.tile([P, 512], F32, name="bank%d" % b) for b in range(8)]
 
         nc.vector.memset(tab_s[32:64, :].bitcast(I32), 0)
@@ -161,7 +164,7 @@ def tile_list_session_memory_blend_kernel(
                 )
 
         def new_bank(g, u):
-            return banks[2 * (g % 2) + u][:].rearrange("p (t e) -> p t e", t=2)
+            return banks[NEW_BANKS[g] + u][:].rearrange("p (t e) -> p t e", t=2)
 
         def in_half(g):
             return slice((g % 2) * WIDE, (g % 2 + 1) * WIDE)
@@ -213,6 +216,13 @@ def tile_list_session_memory_blend_kernel(
                 ACT.Copy,
             )
 
+        def round_wn_gpsimd(a, t):
+            nc.gpsimd.tensor_scalar(
+                out=wn_bf[a][:, t * H : (t + 1) * H].rearrange("p (g i j) -> p g i j", i=RUN, j=PACK),
+                in0=wn_raw[a][:].rearrange("p j (g t i) -> p t g i j", t=PACK, i=RUN)[:, t],
+                scalar1=1.0, scalar2=0.0, op0=ALU.mult, op1=ALU.add,
+            )
+
         def round_wn_vector(a, first, count):
             tiles = slice(first, first + count)
             nc.vector.tensor_copy(
@@ -249,28 +259,35 @@ def tile_list_session_memory_blend_kernel(
             for u in us:
                 nc.scalar.activation(y[g][:, u, :], sums(g, u), ACT.Identity, bias=bias[:, u : u + 1])
 
-        def add_bias_vector(g):
-            width = GROUPS[g][1] * P
-            nc.vector.tensor_tensor(
-                out=y[g][:, 2:4, :],
-                in0=banks[SUM_BANKS[g][1]][:, 0 : 2 * width].rearrange("p (u n) -> p u n", u=2),
-                in1=bias[:, 2:4].unsqueeze(2).to_broadcast([P, 2, width]),
-                op=ALU.add,
-            )
-
         def finish(g):
             first, count = GROUPS[g]
             rows = out.rearrange("(u p) j -> p u j", p=P)[:, :, first * P : (first + count) * P]
             predict(g)
-            add_bias_scalar(g, (0, 1))
-            if g < len(GROUPS) - 1:
-                nc.sync.dma_start(out=rows[:, 0:2, :], in_=y[g][:, 0:2, :])
-                add_bias_scalar(g, (2, 3))
-                nc.sync.dma_start(out=rows[:, 2:4, :], in_=y[g][:, 2:4, :])
-            else:
-                add_bias_vector(g)
-                nc.sync.dma_start(out=rows[:, 0:2, :], in_=y[g][:, 0:2, :])
-                nc.sync.dma_start(out=rows[:, 2:4, :], in_=y[g][:, 2:4, :])
+            for us in ((0, 1), (2, 3)):
+                add_bias_scalar(g, us)
+                nc.sync.dma_start(out=rows[:, us[0] : us[1] + 1, :], in_=y[g][:, us[0] : us[1] + 1, :])
+
+        def finish_last():
+            g = len(GROUPS) - 1
+            rows = out.rearrange("(u p) j -> p u j", p=P)[:, :, S - WIDE : S]
+            for part in range(2):
+                quantize(
+                    h_c[g][:, part * P : (part + 1) * P], h_s[g][:, part * P : (part + 1) * P],
+                    h_bf[g][:, part * H : (part + 1) * H],
+                )
+            for u in range(N // P):
+                cols = slice(u * P, (u + 1) * P)
+                nc.tensor.matmul_mx(
+                    out=banks[LAST_BANKS[u]][:, 0:WIDE], lhsT=w2_c[:, cols].bitcast(FP8X4), lhsT_scale=w2_s[:, cols],
+                    rhs=h_c[g][:].bitcast(FP8X4), rhs_scale=h_s[g][:], start=True, stop=True,
+                )
+                if u % 2 == 0:
+                    nc.scalar.activation(last[u][:], banks[LAST_BANKS[u]][:, 0:WIDE], ACT.Identity, bias=bias[:, u : u + 1])
+                else:
+                    nc.vector.tensor_scalar(
+                        out=last[u][:], in0=banks[LAST_BANKS[u]][:, 0:WIDE], scalar1=bias[:, u : u + 1], scalar2=None, op0=ALU.add
+                    )
+                nc.sync.dma_start(out=rows[:, u, :], in_=last[u][:])
 
         rows32 = slice(0, PASSES * ROWS)
         nc.sync.dma_start(offsets[:], offs)
@@ -289,9 +306,8 @@ def tile_list_session_memory_blend_kernel(
         spread(0)
         load_wg(1)
         load_wo()
-        load_wn(0, 0, 2)
         spread(1)
-        load_wn(0, 2, 2)
+        load_wn(0, 0, PACK)
         load_wn(1, 0, PACK)
         load_w2()
         load_bias()
@@ -308,48 +324,41 @@ def tile_list_session_memory_blend_kernel(
                 gate_pass(half, t, 0)
         gather_words(1, 0, 4)
         permute(wg[:, H : 2 * H], wg_raw[1][:], 1, RUN)
-        gather_words(1, 4, 4)
         permute(wo[:].bitcast(I32), wo_raw[:], PASSES, RUN // 2)
+        gather_words(1, 4, 4)
         round_wn_vector(0, 0, PACK)
         quantize(wn_c[0][:], wn_s[0][:], wn_bf[0][:])
-
+        round_wn_gpsimd(1, 0)
+        round_wn_gpsimd(1, 1)
         for t in range(PACK):
             gate_pass(0, t, 1)
             sigmoid(0, t)
         for t in range(PACK):
-            gate_pass(1, t, 1)
-        sigmoid(1, 0)
-        sigmoid(1, 1)
-        for t in range(PACK):
             old_passes(0, t)
+            weigh_old(0, t)
+            gate_pass(1, t, 1)
+            sigmoid(1, t)
         round_wn_scalar(1, 2)
         round_wn_scalar(1, 3)
-        sigmoid(1, 2)
-        sigmoid(1, 3)
         for t in range(PACK):
             old_passes(1, t)
-        weigh_old(0, 0)
-        weigh_old(0, 1)
-        round_wn_vector(1, 0, 2)
-        weigh_old(0, 2)
+        weigh_old(1, 0)
+        weigh_old(1, 1)
         quantize(wn_c[1][:], wn_s[1][:], wn_bf[1][:])
-        weigh_old(0, 3)
-        for t in range(PACK):
-            weigh_old(1, t)
+        weigh_old(1, 2)
+        weigh_old(1, 3)
         for part in range(4):
             round_w2(part)
 
         for g in range(4):
-            new_passes(g, 0)
-            weigh_new(g, 0)
-            if g > 0:
-                quantize_h(g - 1)
-                finish(g - 1)
-            new_passes(g, 1)
-            weigh_new(g, 1)
+            for u in range(2):
+                new_passes(g, u)
+                weigh_new(g, u)
             if g == 0:
                 quantize(w2_c[:], w2_s[:], w2_bf[:])
+            else:
+                quantize_h(g - 1)
+                finish(g - 1)
             blend_woven(2 * g)
             blend_woven(2 * g + 1)
-        quantize_h(3)
-        finish(3)
+        finish_last()

@@ -24,8 +24,9 @@ RUN = 4
 PIECES = [(0, 4), (4, 4)]
 GROUPS = [(0, 2), (2, 2), (4, 2), (6, 2)]
 SUM_BANKS = [(4, 5), (6, 7), (2, 3)]
-NEW_BANKS = [0, 2, 0, 4]
-LAST_BANKS = [0, 1, 6, 7]
+NEW_BANKS = [(0, 1), (2, 3), (6, 7), (0, 1)]
+OLD_BANKS = [0, 1, 2, 3, 4, 5, 0, 2]
+LAST_BANKS = [4, 5, 0, 1]
 ROWS = 16
 EARLY = 4
 HALF = S // 2
@@ -61,7 +62,7 @@ def tile_list_session_memory_blend_kernel(
         wo_raw = placed([P, PASSES * H // 2], I32, "wo_raw", 32768)
         wg = tile([P, PASSES * H], I32, "wg")
         wo = tile([P, PASSES * 2 * H], U8, "wo")
-        wn_raw = [placed([P, PACK, H], F32, "wn_raw0", 40960), tile([P, PACK, H], F32, "wn_raw1")]
+        wn_raw = [placed([P, PACK, H], F32, "wn_raw0", 40960), placed([P, PACK, H], F32, "wn_raw1", 20480)]
         wn_bf = [tile([P, PACK * H], BF16, "wn_bf0"), tile([P, PACK * H], BF16, "wn_bf1")]
         wn_c = [tile([P, H], U32, "wn_c%d" % a) for a in range(PASSES)]
         wn_s = [tile([P, H], U8, "wn_s%d" % a) for a in range(PASSES)]
@@ -76,11 +77,14 @@ def tile_list_session_memory_blend_kernel(
             (0, 0): tile([P, 2, HALF], F32, "sig00"),
             (0, 1): tile([P, 2, HALF], F32, "sig01"),
             (1, 0): tile([P, 2, HALF], F32, "sig10"),
-            (1, 1): tile([P, 2, HALF], F32, "sig11"),
+            (1, 1): placed([P, 2, HALF], F32, "sig11", 20480),
         }
         old_part = [placed([P, PACK, HALF], F32, "old0", 40960), tile([P, PACK, HALF], F32, "old1")]
-        new_part = [tile([P, PACK, WIDE], F32, "new%d" % g) for g in range(4)]
-        h_bf = [tile([P, 2 * H], BF16, "h_bf%d" % g)[:] for g in range(4)]
+        new_part = [tile([P, PACK, WIDE], F32, "new%d" % g) for g in range(3)]
+        new_last = [tile([P, PACK, P], F32, "new_last%d" % part) for part in range(2)]
+        flat = [tile([P, PACK, P], BF16, "flat0"), placed([P, PACK, P], BF16, "flat1", 0)]
+        h_bf = [placed([P, 2 * H], BF16, "h_bf0", 0)[:]]
+        h_bf += [tile([P, 2 * H], BF16, "h_bf%d" % g)[:] for g in range(1, 4)]
         h_c = [tile([P, WIDE], U32, "h_c%d" % g) for g in range(4)]
         h_s = [tile([P, n * P], U8, "h_s%d" % b) for b, n in GROUPS]
         y = [tile([P, N // P, n * P], F32, "y%d" % b) for b, n in GROUPS[:-1]]
@@ -155,7 +159,7 @@ def tile_list_session_memory_blend_kernel(
             for a in range(PASSES):
                 at = a * H + t * P
                 nc.tensor.matmul_mx(
-                    out=banks[PACK * half + t][:],
+                    out=banks[OLD_BANKS[PACK * half + t]][:],
                     lhsT=wo[:, 2 * at : 2 * (at + P)].bitcast(FP4X4),
                     lhsT_scale=planes[a][:, S + H + t * P : S + H + (t + 1) * P],
                     rhs=v_w[a, PACK * half][:].bitcast(FP8X4),
@@ -164,7 +168,7 @@ def tile_list_session_memory_blend_kernel(
                 )
 
         def new_bank(g, u):
-            return banks[NEW_BANKS[g] + u][:].rearrange("p (t e) -> p t e", t=2)
+            return banks[NEW_BANKS[g][u]][:].rearrange("p (t e) -> p t e", t=2)
 
         def in_half(g):
             return slice((g % 2) * WIDE, (g % 2 + 1) * WIDE)
@@ -187,7 +191,7 @@ def tile_list_session_memory_blend_kernel(
         def weigh_old(half, t):
             nc.vector.scalar_tensor_tensor(
                 out=old_part[half][:, t, :], in0=sig[half, t // 2][:, t % 2, :], scalar=1.0,
-                in1=banks[PACK * half + t][:], op0=ALU.subtract, op1=ALU.mult,
+                in1=banks[OLD_BANKS[PACK * half + t]][:], op0=ALU.subtract, op1=ALU.mult,
             )
 
         def weigh_new(g, u):
@@ -195,13 +199,42 @@ def tile_list_session_memory_blend_kernel(
                 out=new_part[g][:, 2 * u : 2 * u + 2, :], in0=new_bank(g, u), in1=sig[g // 2, u][:, :, in_half(g)], op=ALU.mult
             )
 
-        def parts(b):
-            new = new_part[b // 2][:, :, (b % 2) * P : (b % 2 + 1) * P]
-            old = old_part[b // PACK][:, :, (b % PACK) * P : (b % PACK + 1) * P]
-            return new, old, h_bf[b // 2][:, (b % 2) * H : (b % 2 + 1) * H]
+        def parts(g, first, end):
+            at = (g % 2) * WIDE
+            return (
+                new_part[g][:, :, first:end] if g < 3 else new_last[first // P][:],
+                old_part[g // 2][:, :, at + first : at + end],
+                h_bf[g][:, PACK * first : PACK * end],
+            )
 
-        def blend_woven(b):
-            new, old, woven = parts(b)
+        def weigh_block(part):
+            bank = banks[NEW_BANKS[3][part]][:].rearrange("p (t e) -> p t e", t=PACK)
+            at = WIDE + part * P
+            for a in range(PASSES):
+                for t in range(PACK):
+                    cols = slice(t * P, (t + 1) * P)
+                    nc.tensor.matmul_mx(
+                        out=bank[:, t, :], lhsT=wn_c[a][:, cols].bitcast(FP8X4), lhsT_scale=wn_s[a][:, cols],
+                        rhs=v_w[a, PACK][:, at : at + P].bitcast(FP8X4),
+                        rhs_scale=planes[a][:, HALF + at : HALF + at + P],
+                        start=(a == 0 and t == 0), stop=(a == PASSES - 1 and t == PACK - 1),
+                    )
+            for u in range(2):
+                nc.vector.tensor_tensor(
+                    out=new_last[part][:, 2 * u : 2 * u + 2, :], in0=bank[:, 2 * u : 2 * u + 2, :],
+                    in1=sig[1, u][:, :, at : at + P], op=ALU.mult,
+                )
+
+        def blend_flat(g):
+            new, old, woven = parts(g, 0, P)
+            nc.gpsimd.tensor_tensor(out=flat[g][:], in0=new, in1=old, op=ALU.subtract)
+            nc.scalar.copy(
+                woven.rearrange("p (c i t) -> p c t i", i=RUN, t=PACK),
+                flat[g][:].rearrange("p t (c i) -> p c t i", i=RUN),
+            )
+
+        def blend_woven(g, first, end):
+            new, old, woven = parts(g, first, end)
             nc.vector.tensor_tensor(
                 out=woven.rearrange("p (c i t) -> p c t i", i=2, t=PACK),
                 in0=new.rearrange("p t (c i) -> p c t i", i=2),
@@ -335,30 +368,50 @@ def tile_list_session_memory_blend_kernel(
             sigmoid(0, t)
         for t in range(PACK):
             old_passes(0, t)
-            weigh_old(0, t)
             gate_pass(1, t, 1)
-            sigmoid(1, t)
+        sigmoid(1, 0)
+        sigmoid(1, 1)
         round_wn_scalar(1, 2)
         round_wn_scalar(1, 3)
-        for t in range(PACK):
+        sigmoid(1, 2)
+        sigmoid(1, 3)
+        for t in range(2):
             old_passes(1, t)
+        for t in range(PACK):
+            weigh_old(0, t)
+        quantize(wn_c[1][:], wn_s[1][:], wn_bf[1][:])
         weigh_old(1, 0)
         weigh_old(1, 1)
-        quantize(wn_c[1][:], wn_s[1][:], wn_bf[1][:])
-        weigh_old(1, 2)
-        weigh_old(1, 3)
         for part in range(4):
             round_w2(part)
 
-        for g in range(4):
+        def weigh_group(g):
             for u in range(2):
                 new_passes(g, u)
                 weigh_new(g, u)
-            if g == 0:
-                quantize(w2_c[:], w2_s[:], w2_bf[:])
-            else:
-                quantize_h(g - 1)
-                finish(g - 1)
-            blend_woven(2 * g)
-            blend_woven(2 * g + 1)
+
+        weigh_group(0)
+        blend_flat(0)
+        weigh_group(1)
+        old_passes(1, 2)
+        weigh_old(1, 2)
+        blend_woven(0, P, WIDE)
+        quantize(w2_c[:], w2_s[:], w2_bf[:])
+        quantize_h(0)
+        finish(0)
+        blend_flat(1)
+        weigh_group(2)
+        old_passes(1, 3)
+        weigh_old(1, 3)
+        blend_woven(1, P, WIDE)
+        blend_woven(2, 0, P)
+        quantize_h(1)
+        finish(1)
+        blend_woven(2, P, WIDE)
+        weigh_block(0)
+        quantize_h(2)
+        finish(2)
+        weigh_block(1)
+        blend_woven(3, 0, P)
+        blend_woven(3, P, WIDE)
         finish_last()

@@ -24,9 +24,9 @@ RUN = 4
 PIECES = [(0, 4), (4, 4)]
 GROUPS = [(0, 2), (2, 2), (4, 2), (6, 2)]
 SUM_BANKS = [(4, 5), (6, 7), (2, 3)]
-NEW_BANKS = [(0, 1), (2, 3), (6, 7), (0, 1)]
+NEW_BANKS = [(0, 1), (2, 3), (6, 7), (4, 5)]
 OLD_BANKS = [0, 1, 2, 3, 4, 5, 0, 2]
-LAST_BANKS = [4, 5, 0, 1]
+LAST_BANKS = [0, 1, 6, 7]
 ROWS = 16
 EARLY = 4
 HALF = S // 2
@@ -59,10 +59,10 @@ def tile_list_session_memory_blend_kernel(
         warm_in = tile([P, 1], F32, "warm_in")
         warm_out = tile([P, 1], F32, "warm_out")
         wg_raw = [tile([P, H], I32, "wg_raw0"), tile([P, H], I32, "wg_raw1")]
-        wo_raw = placed([P, PASSES * H // 2], I32, "wo_raw", 32768)
+        wo_raw = tile([P, PASSES * H // 2], I32, "wo_raw")
         wg = tile([P, PASSES * H], I32, "wg")
         wo = tile([P, PASSES * 2 * H], U8, "wo")
-        wn_raw = [placed([P, PACK, H], F32, "wn_raw0", 40960), placed([P, PACK, H], F32, "wn_raw1", 20480)]
+        wn_raw = [placed([P, PACK, H], F32, "wn_raw0", 40960), placed([P, 2 * PACK, H], F32, "wn_raw1", 20480)[:, 0:PACK, :]]
         wn_bf = [tile([P, PACK * H], BF16, "wn_bf0"), tile([P, PACK * H], BF16, "wn_bf1")]
         wn_c = [tile([P, H], U32, "wn_c%d" % a) for a in range(PASSES)]
         wn_s = [tile([P, H], U8, "wn_s%d" % a) for a in range(PASSES)]
@@ -72,14 +72,14 @@ def tile_list_session_memory_blend_kernel(
         w2_s = tile([P, N], U8, "w2_s")
         bias = tile([P, N // P], F32, "bias")
         v_w = {(a, f): tile([P, n * P], U32, "v_w%d%d" % (a, f)) for a, f, n in [(0, 0, 4), (0, 4, 4), (1, 0, 4)]}
-        v_w[1, 4] = placed([P, 4 * P], U32, "v_w14", 32768)
+        v_w[1, 4] = tile([P, 4 * P], U32, "v_w14")
         sig = {
             (0, 0): tile([P, 2, HALF], F32, "sig00"),
             (0, 1): tile([P, 2, HALF], F32, "sig01"),
             (1, 0): tile([P, 2, HALF], F32, "sig10"),
             (1, 1): placed([P, 2, HALF], F32, "sig11", 20480),
         }
-        old_part = [placed([P, PACK, HALF], F32, "old0", 40960), tile([P, PACK, HALF], F32, "old1")]
+        old_part = [placed([P, PACK, HALF], F32, "old0", 40960), placed([P, PACK, HALF], F32, "old1", 28672)]
         new_part = [tile([P, PACK, WIDE], F32, "new%d" % g) for g in range(3)]
         new_last = [tile([P, PACK, P], F32, "new_last%d" % part) for part in range(2)]
         flat = [tile([P, PACK, P], BF16, "flat0"), placed([P, PACK, P], BF16, "flat1", 0)]
@@ -140,8 +140,8 @@ def tile_list_session_memory_blend_kernel(
                 in_=tab_w[a][:].indirect(offsets[:, first * P // 16 : (first + count) * P // 16]),
             )
 
-        def permute(dst, src, passes, words):
-            nc.vector.tensor_copy(
+        def permute(engine, dst, src, passes, words):
+            engine.tensor_copy(
                 out=dst.rearrange("p (a t g i) -> p a t g i", a=passes, t=PACK, i=words),
                 in_=src.rearrange("p (a g t i) -> p a t g i", a=passes, t=PACK, i=words),
             )
@@ -332,10 +332,10 @@ def tile_list_session_memory_blend_kernel(
         load_table(1)
         nc.scalar.activation(warm_out[:], warm_in[:], ACT.Sigmoid)
         nc.vector.tensor_copy(out=picked_s[:], in_=tab_s[:].indirect(offsets[:]))
-        permute(rows_s[rows32, S : S + H].bitcast(I32), wg_s_raw[rows32, :].bitcast(I32), 1, RUN // 4)
-        permute(rows_s[rows32, S + H : S + 2 * H].bitcast(I32), wo_s_raw[rows32, :].bitcast(I32), 1, RUN // 4)
+        permute(nc.gpsimd, rows_s[rows32, S : S + H].bitcast(I32), wg_s_raw[rows32, :].bitcast(I32), 1, RUN // 4)
+        permute(nc.gpsimd, rows_s[rows32, S + H : S + 2 * H].bitcast(I32), wo_s_raw[rows32, :].bitcast(I32), 1, RUN // 4)
         nc.vector.tensor_copy(out=rows_s[rows32, 0:S].bitcast(I32), in_=picked_s[rows32, :].bitcast(I32))
-        permute(wg[:, 0:H], wg_raw[0][:], 1, RUN)
+        permute(nc.gpsimd, wg[:, 0:H], wg_raw[0][:], 1, RUN)
         spread(0)
         load_wg(1)
         load_wo()
@@ -356,11 +356,14 @@ def tile_list_session_memory_blend_kernel(
             for t in range(PACK):
                 gate_pass(half, t, 0)
         gather_words(1, 0, 4)
-        permute(wg[:, H : 2 * H], wg_raw[1][:], 1, RUN)
-        permute(wo[:].bitcast(I32), wo_raw[:], PASSES, RUN // 2)
+        permute(nc.gpsimd, wg[:, H : 2 * H], wg_raw[1][:], 1, RUN)
+        permute(nc.gpsimd, wo[:].bitcast(I32), wo_raw[:], PASSES, RUN // 2)
         gather_words(1, 4, 4)
-        round_wn_vector(0, 0, PACK)
-        quantize(wn_c[0][:], wn_s[0][:], wn_bf[0][:])
+        for first in (0, 2):
+            round_wn_vector(0, first, 2)
+        for first in (0, 2):
+            cols = slice(first * P, (first + 2) * P)
+            quantize(wn_c[0][:, cols], wn_s[0][:, cols], wn_bf[0][:, first * H : (first + 2) * H])
         round_wn_gpsimd(1, 0)
         round_wn_gpsimd(1, 1)
         for t in range(PACK):

@@ -23,10 +23,11 @@ BLOCKS = S // P
 RUN = 4
 PIECES = [(0, 4), (4, 4)]
 GROUPS = [(0, 2), (2, 2), (4, 2), (6, 2)]
-SUM_BANKS = [(4, 5), (6, 7), (2, 3)]
-NEW_BANKS = [(0, 1), (2, 3), (6, 7), (4, 5)]
+SUM_BANKS = [(6, 7), (0, 2), (4, 5)]
+NEW_BANKS = [(0, 1), (2, 3), (6, 7), (1, 3)]
 OLD_BANKS = [0, 1, 2, 3, 4, 5, 0, 2]
-LAST_BANKS = [0, 1, 6, 7]
+LAST_BANKS = [6, 7, 1, 3]
+TURN_BANKS = [4, 5]
 ROWS = 16
 EARLY = 4
 HALF = S // 2
@@ -59,7 +60,7 @@ def tile_list_session_memory_blend_kernel(
         warm_in = tile([P, 1], F32, "warm_in")
         warm_out = tile([P, 1], F32, "warm_out")
         wg_raw = [tile([P, H], I32, "wg_raw0"), tile([P, H], I32, "wg_raw1")]
-        wo_raw = tile([P, PASSES * H // 2], I32, "wo_raw")
+        wo_raw = placed([P, PASSES * H // 2], I32, "wo_raw", 0)
         wg = tile([P, PASSES * H], I32, "wg")
         wo = tile([P, PASSES * 2 * H], U8, "wo")
         wn_raw = [placed([P, PACK, H], F32, "wn_raw0", 40960), placed([P, 2 * PACK, H], F32, "wn_raw1", 20480)[:, 0:PACK, :]]
@@ -80,11 +81,16 @@ def tile_list_session_memory_blend_kernel(
             (1, 1): placed([P, 2, HALF], F32, "sig11", 20480),
         }
         old_part = [placed([P, PACK, HALF], F32, "old0", 40960), placed([P, PACK, HALF], F32, "old1", 28672)]
-        new_part = [tile([P, PACK, WIDE], F32, "new%d" % g) for g in range(3)]
+        new_part = [tile([P, PACK, WIDE], F32, "new%d" % g) for g in range(2)]
+        new_rows = [tile([P, H], F32, "new_rows%d" % b) for b in range(2)]
+        identity = placed([P, P], F32, "identity", 0)
+        ones = placed([P, 32], F32, "ones", 512)
+        ramp = tile([P, 32], F32, "ramp")
+        lane = tile([P, 32], F32, "lane")
         new_last = [tile([P, PACK, P], F32, "new_last%d" % part) for part in range(2)]
-        flat = [tile([P, PACK, P], BF16, "flat0"), placed([P, PACK, P], BF16, "flat1", 0)]
-        h_bf = [placed([P, 2 * H], BF16, "h_bf0", 0)[:]]
-        h_bf += [tile([P, 2 * H], BF16, "h_bf%d" % g)[:] for g in range(1, 4)]
+        flat = [tile([P, PACK, P], BF16, "flat%d" % g) for g in range(2)]
+        h_bf = [tile([P, 2 * H], BF16, "h_bf%d" % g)[:] for g in range(2)]
+        h_bf += [placed([P, 2 * H], BF16, "h_bf%d" % g, 4096)[:] for g in range(2, 4)]
         h_c = [tile([P, WIDE], U32, "h_c%d" % g) for g in range(4)]
         h_s = [tile([P, n * P], U8, "h_s%d" % b) for b, n in GROUPS]
         y = [tile([P, N // P, n * P], F32, "y%d" % b) for b, n in GROUPS[:-1]]
@@ -146,7 +152,28 @@ def tile_list_session_memory_blend_kernel(
                 in_=src.rearrange("p (a g t i) -> p a t g i", a=passes, t=PACK, i=words),
             )
 
+        def event_pass(bank, b, a, words, scales):
+            nc.tensor.matmul_mx(
+                out=banks[bank][:], lhsT=v_w[a, PACK][:, b * P : (b + 1) * P].bitcast(FP8X4),
+                lhsT_scale=planes[a][:, HALF + b * P : HALF + (b + 1) * P],
+                rhs=words, rhs_scale=scales, start=(a == 0), stop=(a == PASSES - 1),
+            )
+
         def gate_pass(half, t, a):
+            if half == 1 and t < 2:
+                event_pass(PACK + t, t, a, wg[:, a * H : (a + 1) * H].bitcast(FP8X4), planes[a][:, S : S + H])
+                return
+            if half == 1:
+                for k in range(2):
+                    at = (2 * (t - 2) + k) * P
+                    nc.tensor.matmul_mx(
+                        out=banks[PACK + t][:, k * WIDE : (k + 1) * WIDE],
+                        lhsT=wg[:, a * H + at : a * H + at + P].bitcast(FP8X4),
+                        lhsT_scale=planes[a][:, S + at : S + at + P],
+                        rhs=v_w[a, PACK][:, WIDE:HALF].bitcast(FP8X4), rhs_scale=planes[a][:, S - WIDE : S],
+                        start=(a == 0 and k == 0), stop=(a == PASSES - 1 and k == 1),
+                    )
+                return
             nc.tensor.matmul_mx(
                 out=banks[PACK * half + t][:],
                 lhsT=wg[:, a * H + t * P : a * H + (t + 1) * P].bitcast(FP8X4),
@@ -157,6 +184,27 @@ def tile_list_session_memory_blend_kernel(
 
         def old_passes(half, t):
             for a in range(PASSES):
+                if half == 1 and t < 2:
+                    event_pass(
+                        OLD_BANKS[PACK + t], t, a, wo[:, 2 * a * H : 2 * (a + 1) * H].bitcast(FP4X4),
+                        planes[a][:, S + H : S + 2 * H],
+                    )
+                    continue
+                if half == 1:
+                    for k in range(2):
+                        row = (2 * (t - 2) + k) * P
+                        for part in range(2):
+                            ev = WIDE + part * P
+                            nc.tensor.matmul_mx(
+                                out=banks[OLD_BANKS[PACK + t]][:, k * WIDE + part * P : k * WIDE + (part + 1) * P],
+                                lhsT=wo[:, 2 * (a * H + row) : 2 * (a * H + row + P)].bitcast(FP4X4),
+                                lhsT_scale=planes[a][:, S + H + row : S + H + row + P],
+                                rhs=v_w[a, PACK][:, ev : ev + P].bitcast(FP8X4),
+                                rhs_scale=planes[a][:, HALF + ev : HALF + ev + P],
+                                start=(a == 0 and k == 0 and part == 0),
+                                stop=(a == PASSES - 1 and k == 1 and part == 1),
+                            )
+                    continue
                 at = a * H + t * P
                 nc.tensor.matmul_mx(
                     out=banks[OLD_BANKS[PACK * half + t]][:],
@@ -201,13 +249,16 @@ def tile_list_session_memory_blend_kernel(
 
         def parts(g, first, end):
             at = (g % 2) * WIDE
+            if g == 3:
+                old = old_part[1][:, 2:4, :].rearrange("p u (k e) -> p (u k) e", k=2)[:, :, first:end]
+                return new_last[first // P][:], old, h_bf[g][:, PACK * first : PACK * end]
             return (
-                new_part[g][:, :, first:end] if g < 3 else new_last[first // P][:],
-                old_part[g // 2][:, :, at + first : at + end],
+                new_part[g][:, :, first:end],
+                old_part[0][:, :, at + first : at + end],
                 h_bf[g][:, PACK * first : PACK * end],
             )
 
-        def weigh_block(part):
+        def block_passes(part):
             bank = banks[NEW_BANKS[3][part]][:].rearrange("p (t e) -> p t e", t=PACK)
             at = WIDE + part * P
             for a in range(PASSES):
@@ -219,10 +270,13 @@ def tile_list_session_memory_blend_kernel(
                         rhs_scale=planes[a][:, HALF + at : HALF + at + P],
                         start=(a == 0 and t == 0), stop=(a == PASSES - 1 and t == PACK - 1),
                     )
+
+        def weigh_block(part):
+            bank = banks[NEW_BANKS[3][part]][:].rearrange("p (t e) -> p t e", t=PACK)
             for u in range(2):
                 nc.vector.tensor_tensor(
                     out=new_last[part][:, 2 * u : 2 * u + 2, :], in0=bank[:, 2 * u : 2 * u + 2, :],
-                    in1=sig[1, u][:, :, at : at + P], op=ALU.mult,
+                    in1=sig[1, 1][:, u, :].rearrange("p (k e) -> p k e", k=2)[:, :, part * P : (part + 1) * P], op=ALU.mult,
                 )
 
         def blend_flat(g):
@@ -231,6 +285,30 @@ def tile_list_session_memory_blend_kernel(
             nc.scalar.copy(
                 woven.rearrange("p (c i t) -> p c t i", i=RUN, t=PACK),
                 flat[g][:].rearrange("p t (c i) -> p c t i", i=RUN),
+            )
+
+        def weigh_rows(b):
+            bank = NEW_BANKS[2][b]
+            for a in range(PASSES):
+                event_pass(bank, b, a, wn_c[a][:].bitcast(FP8X4), wn_s[a][:])
+            nc.vector.scalar_tensor_tensor(
+                out=new_rows[b][:], in0=sig[1, 0][:, b, :], scalar=-1.0,
+                in1=banks[bank][:], op0=ALU.mult, op1=ALU.mult,
+            )
+
+        def turn(b, rows, first):
+            for t in range(PACK):
+                cols = slice(t * P, (t + 1) * P)
+                nc.tensor.matmul(
+                    banks[TURN_BANKS[b]][:, cols], rows[:, cols], identity[:],
+                    start=(first and t == 0), stop=(not first and t == PACK - 1), is_transpose=True,
+                )
+
+        def round_turned(b):
+            nc.scalar.activation(
+                h_bf[2][:, b * H : (b + 1) * H].rearrange("p (c i t) -> p c t i", i=2, t=PACK),
+                banks[TURN_BANKS[b]][:].rearrange("p (t c i) -> p c t i", i=2, t=PACK),
+                ACT.Copy, scale=-1.0,
             )
 
         def blend_woven(g, first, end):
@@ -359,6 +437,13 @@ def tile_list_session_memory_blend_kernel(
         permute(nc.gpsimd, wg[:, H : 2 * H], wg_raw[1][:], 1, RUN)
         permute(nc.gpsimd, wo[:].bitcast(I32), wo_raw[:], PASSES, RUN // 2)
         gather_words(1, 4, 4)
+        nc.vector.memset(ones[:], 1.0)
+        nc.vector.memset(identity[:], 0.0)
+        nc.vector.tensor_tensor_scan(ramp[:], ones[:], ones[:], 0.0, ALU.mult, ALU.add)
+        nc.vector.transpose(lane[:], ramp[:])
+        for q in range(4):
+            quad = slice(32 * q, 32 * q + 32)
+            nc.vector.tensor_tensor(out=identity[quad, quad], in0=ramp[quad, :], in1=lane[quad, :], op=ALU.is_equal)
         for first in (0, 2):
             round_wn_vector(0, first, 2)
         for first in (0, 2):
@@ -393,24 +478,30 @@ def tile_list_session_memory_blend_kernel(
                 new_passes(g, u)
                 weigh_new(g, u)
 
-        weigh_group(0)
-        blend_flat(0)
-        weigh_group(1)
+        for g in range(2):
+            weigh_group(g)
+            blend_flat(g)
+        weigh_rows(0)
+        weigh_rows(1)
         old_passes(1, 2)
         weigh_old(1, 2)
+        old_passes(1, 3)
+        block_passes(0)
+        for b in range(2):
+            turn(b, old_part[1][:, b, :], True)
+        turn(0, new_rows[0], False)
+        round_turned(0)
+        block_passes(1)
+        turn(1, new_rows[1], False)
+        round_turned(1)
         blend_woven(0, P, WIDE)
         quantize(w2_c[:], w2_s[:], w2_bf[:])
         quantize_h(0)
         finish(0)
-        blend_flat(1)
-        weigh_group(2)
-        old_passes(1, 3)
-        weigh_old(1, 3)
         blend_woven(1, P, WIDE)
-        blend_woven(2, 0, P)
+        weigh_old(1, 3)
         quantize_h(1)
         finish(1)
-        blend_woven(2, P, WIDE)
         weigh_block(0)
         quantize_h(2)
         finish(2)

@@ -1,6 +1,7 @@
 from contextlib import ExitStack
 
 import concourse.mybir as mybir
+from concourse.masks import make_identity
 
 K, H, N, T, S = 1024, 512, 512, 2048, 1024
 FLOPS = 2 * S * H * (3 * K + N)
@@ -23,11 +24,11 @@ BLOCKS = S // P
 RUN = 4
 PIECES = [(0, 4), (4, 4)]
 GROUPS = [(0, 2), (2, 2), (4, 2), (6, 2)]
-SUM_BANKS = [(6, 7), (0, 2), (4, 5)]
-NEW_BANKS = [(0, 1), (2, 3), (6, 7), (1, 3)]
-OLD_BANKS = [0, 1, 2, 3, 4, 5, 0, 2]
-LAST_BANKS = [6, 7, 1, 3]
-TURN_BANKS = [4, 5]
+SUM_BANKS = [(5, 7), (4, 0), (1, 2)]
+NEW_BANKS = [(0, 1), (2, 3), (6, 7), (3, 6)]
+OLD_BANKS = [7, 1, 2, 3, 4, 0, 1, 2]
+LAST_BANKS = [5, 7, 4, 0]
+TURN_BANKS = [4, 0]
 ROWS = 16
 EARLY = 4
 HALF = S // 2
@@ -59,15 +60,15 @@ def tile_list_session_memory_blend_kernel(
         planes = [tile([P, S + 2 * H], U8, "planes%d" % a) for a in range(PASSES)]
         warm_in = tile([P, 1], F32, "warm_in")
         warm_out = tile([P, 1], F32, "warm_out")
-        wg_raw = [tile([P, H], I32, "wg_raw0"), tile([P, H], I32, "wg_raw1")]
-        wo_raw = placed([P, PASSES * H // 2], I32, "wo_raw", 0)
+        wg_raw = [placed([P, H], I32, "wg_raw0", 0), tile([P, H], I32, "wg_raw1")]
+        wo_raw = tile([P, PASSES * H // 2], I32, "wo_raw")
         wg = tile([P, PASSES * H], I32, "wg")
         wo = tile([P, PASSES * 2 * H], U8, "wo")
-        wn_raw = [placed([P, PACK, H], F32, "wn_raw0", 40960), placed([P, 2 * PACK, H], F32, "wn_raw1", 20480)[:, 0:PACK, :]]
+        wn_raw = [tile([P, PACK, H], F32, "wn_raw0"), placed([P, 2 * PACK, H], F32, "wn_raw1", 20480)[:, 0:PACK, :]]
         wn_bf = [tile([P, PACK * H], BF16, "wn_bf0"), tile([P, PACK * H], BF16, "wn_bf1")]
         wn_c = [tile([P, H], U32, "wn_c%d" % a) for a in range(PASSES)]
         wn_s = [tile([P, H], U8, "wn_s%d" % a) for a in range(PASSES)]
-        w2_raw = tile([P, PACK, N], F32, "w2_raw")
+        w2_raw = placed([P, PACK, N], F32, "w2_raw", 40960)
         w2_bf = tile([P, PACK * N], BF16, "w2_bf")
         w2_c = tile([P, N], U32, "w2_c")
         w2_s = tile([P, N], U8, "w2_s")
@@ -80,17 +81,15 @@ def tile_list_session_memory_blend_kernel(
             (1, 0): tile([P, 2, HALF], F32, "sig10"),
             (1, 1): placed([P, 2, HALF], F32, "sig11", 20480),
         }
-        old_part = [placed([P, PACK, HALF], F32, "old0", 40960), placed([P, PACK, HALF], F32, "old1", 28672)]
+        old_wide = tile([P, PACK, HALF], F32, "old_wide")
+        old_rows = placed([P, 2, H], F32, "old_rows", 28672)
+        old_last = placed([P, 2, HALF], F32, "old_last", 40960)
         new_part = [tile([P, PACK, WIDE], F32, "new%d" % g) for g in range(2)]
         new_rows = [tile([P, H], F32, "new_rows%d" % b) for b in range(2)]
         identity = placed([P, P], F32, "identity", 0)
-        ones = placed([P, 32], F32, "ones", 512)
-        ramp = tile([P, 32], F32, "ramp")
-        lane = tile([P, 32], F32, "lane")
         new_last = [tile([P, PACK, P], F32, "new_last%d" % part) for part in range(2)]
         flat = [tile([P, PACK, P], BF16, "flat%d" % g) for g in range(2)]
-        h_bf = [tile([P, 2 * H], BF16, "h_bf%d" % g)[:] for g in range(2)]
-        h_bf += [placed([P, 2 * H], BF16, "h_bf%d" % g, 4096)[:] for g in range(2, 4)]
+        h_bf = [tile([P, 2 * H], BF16, "h_bf%d" % g)[:] for g in range(4)]
         h_c = [tile([P, WIDE], U32, "h_c%d" % g) for g in range(4)]
         h_s = [tile([P, n * P], U8, "h_s%d" % b) for b, n in GROUPS]
         y = [tile([P, N // P, n * P], F32, "y%d" % b) for b, n in GROUPS[:-1]]
@@ -238,7 +237,7 @@ def tile_list_session_memory_blend_kernel(
 
         def weigh_old(half, t):
             nc.vector.scalar_tensor_tensor(
-                out=old_part[half][:, t, :], in0=sig[half, t // 2][:, t % 2, :], scalar=1.0,
+                out=old_wide[:, t, :] if half == 0 else (old_rows, old_last)[t // 2][:, t % 2, :], in0=sig[half, t // 2][:, t % 2, :], scalar=1.0,
                 in1=banks[OLD_BANKS[PACK * half + t]][:], op0=ALU.subtract, op1=ALU.mult,
             )
 
@@ -250,11 +249,11 @@ def tile_list_session_memory_blend_kernel(
         def parts(g, first, end):
             at = (g % 2) * WIDE
             if g == 3:
-                old = old_part[1][:, 2:4, :].rearrange("p u (k e) -> p (u k) e", k=2)[:, :, first:end]
+                old = old_last[:].rearrange("p u (k e) -> p (u k) e", k=2)[:, :, first:end]
                 return new_last[first // P][:], old, h_bf[g][:, PACK * first : PACK * end]
             return (
                 new_part[g][:, :, first:end],
-                old_part[0][:, :, at + first : at + end],
+                old_wide[:, :, at + first : at + end],
                 h_bf[g][:, PACK * first : PACK * end],
             )
 
@@ -358,8 +357,8 @@ def tile_list_session_memory_blend_kernel(
             width = GROUPS[g][1] * P
             return banks[SUM_BANKS[g][u // 2]][:, (u % 2) * width : (u % 2 + 1) * width]
 
-        def predict(g):
-            for u in range(N // P):
+        def predict(g, us):
+            for u in us:
                 cols = slice(u * P, (u + 1) * P)
                 nc.tensor.matmul_mx(
                     out=sums(g, u), lhsT=w2_c[:, cols].bitcast(FP8X4), lhsT_scale=w2_s[:, cols],
@@ -370,13 +369,18 @@ def tile_list_session_memory_blend_kernel(
             for u in us:
                 nc.scalar.activation(y[g][:, u, :], sums(g, u), ACT.Identity, bias=bias[:, u : u + 1])
 
-        def finish(g):
+        def quantize_w2(k):
+            cols = slice(k * WIDE, (k + 1) * WIDE)
+            quantize(w2_c[:, cols], w2_s[:, cols], w2_bf[:, PACK * k * WIDE : PACK * (k + 1) * WIDE])
+
+        def finish(g, stores=((0, 1), (2, 3))):
             first, count = GROUPS[g]
             rows = out.rearrange("(u p) j -> p u j", p=P)[:, :, first * P : (first + count) * P]
-            predict(g)
-            for us in ((0, 1), (2, 3)):
+            for us in stores:
+                predict(g, us)
+            for us in stores:
                 add_bias_scalar(g, us)
-                nc.sync.dma_start(out=rows[:, us[0] : us[1] + 1, :], in_=y[g][:, us[0] : us[1] + 1, :])
+                nc.sync.dma_start(out=rows[:, us[0] : us[-1] + 1, :], in_=y[g][:, us[0] : us[-1] + 1, :])
 
         def finish_last():
             g = len(GROUPS) - 1
@@ -428,48 +432,47 @@ def tile_list_session_memory_blend_kernel(
                 rhs=wg_raw[0][:].bitcast(FP8X4), rhs_scale=picked_s[:, 0:H], start=True, stop=True,
             )
 
+        make_identity(nc, identity[:])
         for first, count in PIECES:
             gather_words(0, first, count)
         for half in range(2):
-            for t in range(PACK):
+            for t in range(PACK - half):
                 gate_pass(half, t, 0)
         gather_words(1, 0, 4)
         permute(nc.gpsimd, wg[:, H : 2 * H], wg_raw[1][:], 1, RUN)
         permute(nc.gpsimd, wo[:].bitcast(I32), wo_raw[:], PASSES, RUN // 2)
         gather_words(1, 4, 4)
-        nc.vector.memset(ones[:], 1.0)
-        nc.vector.memset(identity[:], 0.0)
-        nc.vector.tensor_tensor_scan(ramp[:], ones[:], ones[:], 0.0, ALU.mult, ALU.add)
-        nc.vector.transpose(lane[:], ramp[:])
-        for q in range(4):
-            quad = slice(32 * q, 32 * q + 32)
-            nc.vector.tensor_tensor(out=identity[quad, quad], in0=ramp[quad, :], in1=lane[quad, :], op=ALU.is_equal)
         for first in (0, 2):
             round_wn_vector(0, first, 2)
         for first in (0, 2):
             cols = slice(first * P, (first + 2) * P)
             quantize(wn_c[0][:, cols], wn_s[0][:, cols], wn_bf[0][:, first * H : (first + 2) * H])
-        round_wn_gpsimd(1, 0)
-        round_wn_gpsimd(1, 1)
+        round_wn_gpsimd(1, 2)
+        round_wn_gpsimd(1, 3)
         for t in range(PACK):
             gate_pass(0, t, 1)
             sigmoid(0, t)
-        for t in range(PACK):
+            if t == 1:
+                old_passes(0, 0)
+                weigh_old(0, 0)
+        for t in range(1, PACK):
+            gate_pass(1, t - 1, 1)
             old_passes(0, t)
-            gate_pass(1, t, 1)
         sigmoid(1, 0)
         sigmoid(1, 1)
-        round_wn_scalar(1, 2)
-        round_wn_scalar(1, 3)
+        round_wn_scalar(1, 0)
+        round_wn_scalar(1, 1)
+        old_passes(1, 0)
+        for a in range(PASSES):
+            gate_pass(1, PACK - 1, a)
         sigmoid(1, 2)
         sigmoid(1, 3)
-        for t in range(2):
-            old_passes(1, t)
-        for t in range(PACK):
+        for t in range(1, PACK):
             weigh_old(0, t)
-        quantize(wn_c[1][:], wn_s[1][:], wn_bf[1][:])
+        for first in (0, 2):
+            cols = slice(first * P, (first + 2) * P)
+            quantize(wn_c[1][:, cols], wn_s[1][:, cols], wn_bf[1][:, first * H : (first + 2) * H])
         weigh_old(1, 0)
-        weigh_old(1, 1)
         for part in range(4):
             round_w2(part)
 
@@ -478,30 +481,37 @@ def tile_list_session_memory_blend_kernel(
                 new_passes(g, u)
                 weigh_new(g, u)
 
-        for g in range(2):
-            weigh_group(g)
-            blend_flat(g)
+        weigh_group(0)
+        blend_flat(0)
+        for u in range(2):
+            new_passes(1, u)
+        old_passes(1, 1)
+        weigh_new(1, 0)
+        weigh_new(1, 1)
+        blend_flat(1)
+        weigh_old(1, 1)
         weigh_rows(0)
         weigh_rows(1)
-        old_passes(1, 2)
-        weigh_old(1, 2)
-        old_passes(1, 3)
-        block_passes(0)
+        for t in range(2, PACK):
+            old_passes(1, t)
         for b in range(2):
-            turn(b, old_part[1][:, b, :], True)
-        turn(0, new_rows[0], False)
-        round_turned(0)
-        block_passes(1)
-        turn(1, new_rows[1], False)
-        round_turned(1)
+            turn(b, old_rows[:, b, :], True)
+        for b in range(2):
+            turn(b, new_rows[b], False)
+            round_turned(b)
+        block_passes(0)
         blend_woven(0, P, WIDE)
-        quantize(w2_c[:], w2_s[:], w2_bf[:])
+        quantize_w2(0)
         quantize_h(0)
-        finish(0)
+        finish(0, [(0, 1)])
+        block_passes(1)
         blend_woven(1, P, WIDE)
-        weigh_old(1, 3)
+        quantize_w2(1)
+        finish(0, [(2, 3)])
         quantize_h(1)
         finish(1)
+        weigh_old(1, 2)
+        weigh_old(1, 3)
         weigh_block(0)
         quantize_h(2)
         finish(2)

@@ -33,6 +33,7 @@ ROWS = 16
 EARLY = 4
 HALF = S // 2
 WIDE = 2 * P
+POOL_EVENTS = (128, 192)
 
 
 def tile_list_session_memory_blend_kernel(
@@ -88,7 +89,7 @@ def tile_list_session_memory_blend_kernel(
         new_rows = [tile([P, H], F32, "new_rows%d" % b) for b in range(2)]
         identity = placed([P, P], F32, "identity", 0)
         new_last = [tile([P, PACK, P], F32, "new_last%d" % part) for part in range(2)]
-        flat = [tile([P, PACK, P], BF16, "flat%d" % g) for g in range(2)]
+        flat = [tile([P, PACK, n], BF16, "flat%d" % g) for g, n in enumerate(POOL_EVENTS)]
         h_bf = [tile([P, 2 * H], BF16, "h_bf%d" % g)[:] for g in range(4)]
         h_c = [tile([P, WIDE], U32, "h_c%d" % g) for g in range(4)]
         h_s = [tile([P, n * P], U8, "h_s%d" % b) for b, n in GROUPS]
@@ -272,14 +273,11 @@ def tile_list_session_memory_blend_kernel(
 
         def weigh_block(part):
             bank = banks[NEW_BANKS[3][part]][:].rearrange("p (t e) -> p t e", t=PACK)
-            for u in range(2):
-                nc.vector.tensor_tensor(
-                    out=new_last[part][:, 2 * u : 2 * u + 2, :], in0=bank[:, 2 * u : 2 * u + 2, :],
-                    in1=sig[1, 1][:, u, :].rearrange("p (k e) -> p k e", k=2)[:, :, part * P : (part + 1) * P], op=ALU.mult,
-                )
+            gate = sig[1, 1][:].rearrange("p u (k e) -> p (u k) e", k=2)[:, :, part * P : (part + 1) * P]
+            nc.vector.tensor_tensor(out=new_last[part][:], in0=bank, in1=gate, op=ALU.mult)
 
         def blend_flat(g):
-            new, old, woven = parts(g, 0, P)
+            new, old, woven = parts(g, 0, POOL_EVENTS[g])
             nc.gpsimd.tensor_tensor(out=flat[g][:], in0=new, in1=old, op=ALU.subtract)
             nc.scalar.copy(
                 woven.rearrange("p (c i t) -> p c t i", i=RUN, t=PACK),
@@ -368,10 +366,6 @@ def tile_list_session_memory_blend_kernel(
         def add_bias_scalar(g, us):
             for u in us:
                 nc.scalar.activation(y[g][:, u, :], sums(g, u), ACT.Identity, bias=bias[:, u : u + 1])
-
-        def quantize_w2(k):
-            cols = slice(k * WIDE, (k + 1) * WIDE)
-            quantize(w2_c[:, cols], w2_s[:, cols], w2_bf[:, PACK * k * WIDE : PACK * (k + 1) * WIDE])
 
         def finish(g, stores=((0, 1), (2, 3))):
             first, count = GROUPS[g]
@@ -494,24 +488,22 @@ def tile_list_session_memory_blend_kernel(
         weigh_rows(1)
         for t in range(2, PACK):
             old_passes(1, t)
+        weigh_old(1, 2)
         for b in range(2):
             turn(b, old_rows[:, b, :], True)
         for b in range(2):
             turn(b, new_rows[b], False)
             round_turned(b)
-        block_passes(0)
-        blend_woven(0, P, WIDE)
-        quantize_w2(0)
+        for part in range(2):
+            block_passes(part)
+        blend_woven(0, POOL_EVENTS[0], WIDE)
+        quantize(w2_c[:], w2_s[:], w2_bf[:])
         quantize_h(0)
-        finish(0, [(0, 1)])
-        block_passes(1)
-        blend_woven(1, P, WIDE)
-        quantize_w2(1)
-        finish(0, [(2, 3)])
+        finish(0)
+        blend_woven(1, POOL_EVENTS[1], WIDE)
+        weigh_old(1, 3)
         quantize_h(1)
         finish(1)
-        weigh_old(1, 2)
-        weigh_old(1, 3)
         weigh_block(0)
         quantize_h(2)
         finish(2)

from contextlib import ExitStack

import concourse.mybir as mybir
from concourse.masks import make_identity

K, H, N, T, S = 1024, 512, 512, 2048, 1024
FLOPS = 2 * S * H * (3 * K + N)

F32 = mybir.dt.float32
BF16 = mybir.dt.bfloat16
I32 = mybir.dt.int32
U32 = mybir.dt.uint32
U16 = mybir.dt.uint16
U8 = mybir.dt.uint8
FP8X4 = mybir.dt.float8_e4m3fn_x4
FP4X4 = mybir.dt.float4_e2m1fn_x4
ALU = mybir.AluOpType
ACT = mybir.ActivationFunctionType

P = 128
PACK = 4
PASSES = K // (P * PACK)
BLOCKS = S // P
RUN = 4
PIECES = [(0, 4), (4, 4)]
GROUPS = [(0, 2), (2, 2), (4, 2), (6, 2)]
SUM_BANKS = [(5, 7), (4, 0), (1, 2)]
NEW_BANKS = [(0, 1), (2, 3), (6, 7), (3, 6)]
OLD_BANKS = [7, 1, 2, 3, 4, 0, 1, 2]
LAST_BANKS = [5, 7, 4, 0]
TURN_BANKS = [4, 0]
ROWS = 16
EARLY = 4
HALF = S // 2
WIDE = 2 * P
POOL_EVENTS = (128, 192)


def tile_list_session_memory_blend_kernel(
    tc, tab_words, tab_scales, offs, wo_words, wo_scales, wg_words, wg_scales, wn, w2, bo, out
):
    nc = tc.nc
    with ExitStack() as ctx:
        keep = ctx.enter_context(tc.tile_pool(name="keep", bufs=1))
        shared = ctx.enter_context(tc.tile_pool(name="shared", bufs=1))
        psum = ctx.enter_context(tc.psum_pool(name="psum", bufs=1))

        def tile(shape, dtype, name):
            return keep.tile(shape, dtype, name=name, align_bytes=64)

        def placed(shape, dtype, name, offset):
            return shared.tile(shape, dtype, name=name, align_bytes=64, offset=offset)

        offsets = keep.tile([P, S // 16], U16, name="offsets")
        tab_w = [tile([P, T], U32, "tab_w%d" % a) for a in range(PASSES)]
        tab_s = tile([P, T], U8, "tab_s")
        picked_s = tile([P, S], U8, "picked_s")
        wg_s_raw = tile([P, H], U8, "wg_s_raw")
        wo_s_raw = tile([P, H], U8, "wo_s_raw")
        rows_s = tile([P, S + 2 * H], U8, "rows_s")
        planes = [tile([P, S + 2 * H], U8, "planes%d" % a) for a in range(PASSES)]
        warm_in = tile([P, 1], F32, "warm_in")
        warm_out = tile([P, 1], F32, "warm_out")
        wg_raw = [placed([P, H], I32, "wg_raw0", 0), tile([P, H], I32, "wg_raw1")]
        wo_raw = tile([P, PASSES * H // 2], I32, "wo_raw")
        wg = tile([P, PASSES * H], I32, "wg")
        wo = tile([P, PASSES * 2 * H], U8, "wo")
        wn_raw = [tile([P, PACK, H], F32, "wn_raw0"), placed([P, 2 * PACK, H], F32, "wn_raw1", 20480)[:, 0:PACK, :]]
        wn_bf = [tile([P, PACK * H], BF16, "wn_bf0"), tile([P, PACK * H], BF16, "wn_bf1")]
        wn_c = [tile([P, H], U32, "wn_c%d" % a) for a in range(PASSES)]
        wn_s = [tile([P, H], U8, "wn_s%d" % a) for a in range(PASSES)]
        w2_raw = placed([P, PACK, N], F32, "w2_raw", 40960)
        w2_bf = tile([P, PACK * N], BF16, "w2_bf")
        w2_c = tile([P, N], U32, "w2_c")
        w2_s = tile([P, N], U8, "w2_s")
        bias = tile([P, N // P], F32, "bias")
        v_w = {(a, f): tile([P, n * P], U32, "v_w%d%d" % (a, f)) for a, f, n in [(0, 0, 4), (0, 4, 4), (1, 0, 4)]}
        v_w[1, 4] = tile([P, 4 * P], U32, "v_w14")
        sig = {
            (0, 0): tile([P, 2, HALF], F32, "sig00"),
            (0, 1): tile([P, 2, HALF], F32, "sig01"),
            (1, 0): tile([P, 2, HALF], F32, "sig10"),
            (1, 1): placed([P, 2, HALF], F32, "sig11", 20480),
        }
        old_wide = tile([P, PACK, HALF], F32, "old_wide")
        old_rows = placed([P, 2, H], F32, "old_rows", 28672)
        old_last = placed([P, 2, HALF], F32, "old_last", 40960)
        new_part = [tile([P, PACK, WIDE], F32, "new%d" % g) for g in range(2)]
        new_rows = [tile([P, H], F32, "new_rows%d" % b) for b in range(2)]
        identity = placed([P, P], F32, "identity", 0)
        new_last = [tile([P, PACK, P], F32, "new_last%d" % part) for part in range(2)]
        flat = [tile([P, PACK, n], BF16, "flat%d" % g) for g, n in enumerate(POOL_EVENTS)]
        h_bf = [tile([P, 2 * H], BF16, "h_bf%d" % g)[:] for g in range(4)]
        h_c = [tile([P, WIDE], U32, "h_c%d" % g) for g in range(4)]
        h_s = [tile([P, n * P], U8, "h_s%d" % b) for b, n in GROUPS]
        y = [tile([P, N // P, n * P], F32, "y%d" % b) for b, n in GROUPS[:-1]]
        last = [tile([P, WIDE], F32, "last%d" % u) for u in range(N // P)]
        banks = [psum.tile([P, 512], F32, name="bank%d" % b) for b in range(8)]

        nc.vector.memset(tab_s[32:64, :].bitcast(I32), 0)
        nc.vector.memset(tab_s[64:P, :].bitcast(I32), 0)
        nc.vector.memset(warm_in[:], 0.0)
        for a in range(PASSES):
            nc.gpsimd.memset(planes[a][:].bitcast(I32), 0)

        def load_rows(queue, dst, src):
            queue.dma_start(out=dst[0 : PASSES * ROWS, :].bitcast(I32), in_=src.rearrange("a q c -> (a q) c").bitcast(I32))

        def load_table(a):
            nc.sync.dma_start(
                out=tab_w[a][:].bitcast(I32), in_=tab_words[a].rearrange("p t i -> p (t i)").bitcast(I32)
            )

        def load_wg(a):
            nc.sync.dma_start(out=wg_raw[a][:], in_=wg_words[a].rearrange("p c i -> p (c i)").bitcast(I32))

        def load_wo():
            nc.sync.dma_start(
                out=wo_raw[:].rearrange("p (a c) -> p a c", a=PASSES),
                in_=wo_words.rearrange("a p c -> p a c").bitcast(I32),
            )

        def load_wn(a, first, count):
            rows = wn[a * 512 : (a + 1) * 512, :].rearrange("(p j) c -> p j c", j=PACK)
            nc.sync.dma_start(out=wn_raw[a][:, first : first + count, :], in_=rows[:, first : first + count, :])

        def load_w2():
            w2_view = w2.rearrange("(g t i) n -> t g i n", t=PACK, i=RUN)
            for t in range(PACK):
                nc.sync.dma_start(out=w2_raw[:, t, :], in_=w2_view[t])

        def load_bias():
            with nc.allow_non_contiguous_dma(reason="one bias value for each partition"):
                nc.sync.dma_start(out=bias[:], in_=bo.rearrange("(u p) -> p u", p=P))

        def spread(a):
            for q in range(4):
                first = ROWS * a + 4 * q
                nc.sync.dma_start(
                    out=planes[a][32 * q : 32 * q + 4, :].bitcast(I32), in_=rows_s[first : first + 4, :].bitcast(I32)
                )

        def gather_words(a, first, count):
            nc.vector.tensor_copy(
                out=v_w[a, first][:],
                in_=tab_w[a][:].indirect(offsets[:, first * P // 16 : (first + count) * P // 16]),
            )

        def permute(engine, dst, src, passes, words):
            engine.tensor_copy(
                out=dst.rearrange("p (a t g i) -> p a t g i", a=passes, t=PACK, i=words),
                in_=src.rearrange("p (a g t i) -> p a t g i", a=passes, t=PACK, i=words),
            )

        def event_pass(bank, b, a, words, scales):
            nc.tensor.matmul_mx(
                out=banks[bank][:], lhsT=v_w[a, PACK][:, b * P : (b + 1) * P].bitcast(FP8X4),
                lhsT_scale=planes[a][:, HALF + b * P : HALF + (b + 1) * P],
                rhs=words, rhs_scale=scales, start=(a == 0), stop=(a == PASSES - 1),
            )

        def gate_pass(half, t, a):
            if half == 1 and t < 2:
                event_pass(PACK + t, t, a, wg[:, a * H : (a + 1) * H].bitcast(FP8X4), planes[a][:, S : S + H])
                return
            if half == 1:
                for k in range(2):
                    at = (2 * (t - 2) + k) * P
                    nc.tensor.matmul_mx(
                        out=banks[PACK + t][:, k * WIDE : (k + 1) * WIDE],
                        lhsT=wg[:, a * H + at : a * H + at + P].bitcast(FP8X4),
                        lhsT_scale=planes[a][:, S + at : S + at + P],
                        rhs=v_w[a, PACK][:, WIDE:HALF].bitcast(FP8X4), rhs_scale=planes[a][:, S - WIDE : S],
                        start=(a == 0 and k == 0), stop=(a == PASSES - 1 and k == 1),
                    )
                return
            nc.tensor.matmul_mx(
                out=banks[PACK * half + t][:],
                lhsT=wg[:, a * H + t * P : a * H + (t + 1) * P].bitcast(FP8X4),
                lhsT_scale=planes[a][:, S + t * P : S + (t + 1) * P],
                rhs=v_w[a, PACK * half][:].bitcast(FP8X4), rhs_scale=planes[a][:, half * HALF : (half + 1) * HALF],
                start=(a == 0), stop=(a == PASSES - 1),
            )

        def old_passes(half, t):
            for a in range(PASSES):
                if half == 1 and t < 2:
                    event_pass(
                        OLD_BANKS[PACK + t], t, a, wo[:, 2 * a * H : 2 * (a + 1) * H].bitcast(FP4X4),
                        planes[a][:, S + H : S + 2 * H],
                    )
                    continue
                if half == 1:
                    for k in range(2):
                        row = (2 * (t - 2) + k) * P
                        for part in range(2):
                            ev = WIDE + part * P
                            nc.tensor.matmul_mx(
                                out=banks[OLD_BANKS[PACK + t]][:, k * WIDE + part * P : k * WIDE + (part + 1) * P],
                                lhsT=wo[:, 2 * (a * H + row) : 2 * (a * H + row + P)].bitcast(FP4X4),
                                lhsT_scale=planes[a][:, S + H + row : S + H + row + P],
                                rhs=v_w[a, PACK][:, ev : ev + P].bitcast(FP8X4),
                                rhs_scale=planes[a][:, HALF + ev : HALF + ev + P],
                                start=(a == 0 and k == 0 and part == 0),
                                stop=(a == PASSES - 1 and k == 1 and part == 1),
                            )
                    continue
                at = a * H + t * P
                nc.tensor.matmul_mx(
                    out=banks[OLD_BANKS[PACK * half + t]][:],
                    lhsT=wo[:, 2 * at : 2 * (at + P)].bitcast(FP4X4),
                    lhsT_scale=planes[a][:, S + H + t * P : S + H + (t + 1) * P],
                    rhs=v_w[a, PACK * half][:].bitcast(FP8X4),
                    rhs_scale=planes[a][:, half * HALF : (half + 1) * HALF],
                    start=(a == 0), stop=(a == PASSES - 1),
                )

        def new_bank(g, u):
            return banks[NEW_BANKS[g][u]][:].rearrange("p (t e) -> p t e", t=2)

        def in_half(g):
            return slice((g % 2) * WIDE, (g % 2 + 1) * WIDE)

        def new_passes(g, u):
            for a in range(PASSES):
                for k in range(2):
                    cols = slice((2 * u + k) * P, (2 * u + k + 1) * P)
                    nc.tensor.matmul_mx(
                        out=new_bank(g, u)[:, k, :],
                        lhsT=wn_c[a][:, cols].bitcast(FP8X4), lhsT_scale=wn_s[a][:, cols],
                        rhs=v_w[a, PACK * (g // 2)][:, in_half(g)].bitcast(FP8X4),
                        rhs_scale=planes[a][:, g * WIDE : (g + 1) * WIDE],
                        start=(a == 0 and k == 0), stop=(a == PASSES - 1 and k == 1),
                    )

        def sigmoid(half, t):
            nc.scalar.activation(sig[half, t // 2][:, t % 2, :], banks[PACK * half + t][:], ACT.Sigmoid)

        def weigh_old(half, t):
            nc.vector.scalar_tensor_tensor(
                out=old_wide[:, t, :] if half == 0 else (old_rows, old_last)[t // 2][:, t % 2, :], in0=sig[half, t // 2][:, t % 2, :], scalar=1.0,
                in1=banks[OLD_BANKS[PACK * half + t]][:], op0=ALU.subtract, op1=ALU.mult,
            )

        def weigh_new(g, u):
            nc.vector.tensor_tensor(
                out=new_part[g][:, 2 * u : 2 * u + 2, :], in0=new_bank(g, u), in1=sig[g // 2, u][:, :, in_half(g)], op=ALU.mult
            )

        def parts(g, first, end):
            at = (g % 2) * WIDE
            if g == 3:
                old = old_last[:].rearrange("p u (k e) -> p (u k) e", k=2)[:, :, first:end]
                return new_last[first // P][:], old, h_bf[g][:, PACK * first : PACK * end]
            return (
                new_part[g][:, :, first:end],
                old_wide[:, :, at + first : at + end],
                h_bf[g][:, PACK * first : PACK * end],
            )

        def block_passes(part):
            bank = banks[NEW_BANKS[3][part]][:].rearrange("p (t e) -> p t e", t=PACK)
            at = WIDE + part * P
            for a in range(PASSES):
                for t in range(PACK):
                    cols = slice(t * P, (t + 1) * P)
                    nc.tensor.matmul_mx(
                        out=bank[:, t, :], lhsT=wn_c[a][:, cols].bitcast(FP8X4), lhsT_scale=wn_s[a][:, cols],
                        rhs=v_w[a, PACK][:, at : at + P].bitcast(FP8X4),
                        rhs_scale=planes[a][:, HALF + at : HALF + at + P],
                        start=(a == 0 and t == 0), stop=(a == PASSES - 1 and t == PACK - 1),
                    )

        def weigh_block(part):
            bank = banks[NEW_BANKS[3][part]][:].rearrange("p (t e) -> p t e", t=PACK)
            gate = sig[1, 1][:].rearrange("p u (k e) -> p (u k) e", k=2)[:, :, part * P : (part + 1) * P]
            nc.vector.tensor_tensor(out=new_last[part][:], in0=bank, in1=gate, op=ALU.mult)

        def blend_flat(g):
            new, old, woven = parts(g, 0, POOL_EVENTS[g])
            nc.gpsimd.tensor_tensor(out=flat[g][:], in0=new, in1=old, op=ALU.subtract)
            nc.scalar.copy(
                woven.rearrange("p (c i t) -> p c t i", i=RUN, t=PACK),
                flat[g][:].rearrange("p t (c i) -> p c t i", i=RUN),
            )

        def weigh_rows(b):
            bank = NEW_BANKS[2][b]
            for a in range(PASSES):
                event_pass(bank, b, a, wn_c[a][:].bitcast(FP8X4), wn_s[a][:])
            nc.vector.scalar_tensor_tensor(
                out=new_rows[b][:], in0=sig[1, 0][:, b, :], scalar=-1.0,
                in1=banks[bank][:], op0=ALU.mult, op1=ALU.mult,
            )

        def turn(b, rows, first):
            for t in range(PACK):
                cols = slice(t * P, (t + 1) * P)
                nc.tensor.matmul(
                    banks[TURN_BANKS[b]][:, cols], rows[:, cols], identity[:],
                    start=(first and t == 0), stop=(not first and t == PACK - 1), is_transpose=True,
                )

        def round_turned(b):
            nc.scalar.activation(
                h_bf[2][:, b * H : (b + 1) * H].rearrange("p (c i t) -> p c t i", i=2, t=PACK),
                banks[TURN_BANKS[b]][:].rearrange("p (t c i) -> p c t i", i=2, t=PACK),
                ACT.Copy, scale=-1.0,
            )

        def blend_woven(g, first, end):
            new, old, woven = parts(g, first, end)
            nc.vector.tensor_tensor(
                out=woven.rearrange("p (c i t) -> p c t i", i=2, t=PACK),
                in0=new.rearrange("p t (c i) -> p c t i", i=2),
                in1=old.rearrange("p t (c i) -> p c t i", i=2),
                op=ALU.subtract,
            )

        def round_wn_scalar(a, t):
            nc.scalar.activation(
                wn_bf[a][:, t * H : (t + 1) * H].rearrange("p (g i j) -> p g j i", i=RUN, j=PACK),
                wn_raw[a][:].rearrange("p j (g t i) -> p t g j i", t=PACK, i=RUN)[:, t],
                ACT.Copy,
            )

        def round_wn_gpsimd(a, t):
            nc.gpsimd.tensor_scalar(
                out=wn_bf[a][:, t * H : (t + 1) * H].rearrange("p (g i j) -> p g i j", i=RUN, j=PACK),
                in0=wn_raw[a][:].rearrange("p j (g t i) -> p t g i j", t=PACK, i=RUN)[:, t],
                scalar1=1.0, scalar2=0.0, op0=ALU.mult, op1=ALU.add,
            )

        def round_wn_vector(a, first, count):
            tiles = slice(first, first + count)
            nc.vector.tensor_copy(
                out=wn_bf[a][:].rearrange("p (t g i j) -> p t g j i", t=PACK, i=RUN, j=PACK)[:, tiles],
                in_=wn_raw[a][:].rearrange("p j (g t i) -> p t g j i", t=PACK, i=RUN)[:, tiles],
            )

        def round_w2(part):
            nc.scalar.activation(
                w2_bf[:, part * N : (part + 1) * N].rearrange("p (c i t) -> p c t i", i=RUN, t=PACK),
                w2_raw[:, :, part * P : (part + 1) * P].rearrange("p t (c i) -> p c t i", i=RUN),
                ACT.Copy,
            )

        def quantize(codes, scales, values):
            nc.vector.quantize_mx(out=codes.bitcast(FP8X4), scales=scales, in_=values)

        def quantize_h(g):
            quantize(h_c[g][:], h_s[g][:], h_bf[g])

        def sums(g, u):
            width = GROUPS[g][1] * P
            return banks[SUM_BANKS[g][u // 2]][:, (u % 2) * width : (u % 2 + 1) * width]

        def predict(g, us):
            for u in us:
                cols = slice(u * P, (u + 1) * P)
                nc.tensor.matmul_mx(
                    out=sums(g, u), lhsT=w2_c[:, cols].bitcast(FP8X4), lhsT_scale=w2_s[:, cols],
                    rhs=h_c[g][:].bitcast(FP8X4), rhs_scale=h_s[g][:], start=True, stop=True,
                )

        def add_bias_scalar(g, us):
            for u in us:
                nc.scalar.activation(y[g][:, u, :], sums(g, u), ACT.Identity, bias=bias[:, u : u + 1])

        def finish(g, stores=((0, 1), (2, 3))):
            first, count = GROUPS[g]
            rows = out.rearrange("(u p) j -> p u j", p=P)[:, :, first * P : (first + count) * P]
            for us in stores:
                predict(g, us)
            for us in stores:
                add_bias_scalar(g, us)
                nc.sync.dma_start(out=rows[:, us[0] : us[-1] + 1, :], in_=y[g][:, us[0] : us[-1] + 1, :])

        def finish_last():
            g = len(GROUPS) - 1
            rows = out.rearrange("(u p) j -> p u j", p=P)[:, :, S - WIDE : S]
            for part in range(2):
                quantize(
                    h_c[g][:, part * P : (part + 1) * P], h_s[g][:, part * P : (part + 1) * P],
                    h_bf[g][:, part * H : (part + 1) * H],
                )
            for u in range(N // P):
                cols = slice(u * P, (u + 1) * P)
                nc.tensor.matmul_mx(
                    out=banks[LAST_BANKS[u]][:, 0:WIDE], lhsT=w2_c[:, cols].bitcast(FP8X4), lhsT_scale=w2_s[:, cols],
                    rhs=h_c[g][:].bitcast(FP8X4), rhs_scale=h_s[g][:], start=True, stop=True,
                )
                if u % 2 == 0:
                    nc.scalar.activation(last[u][:], banks[LAST_BANKS[u]][:, 0:WIDE], ACT.Identity, bias=bias[:, u : u + 1])
                else:
                    nc.vector.tensor_scalar(
                        out=last[u][:], in0=banks[LAST_BANKS[u]][:, 0:WIDE], scalar1=bias[:, u : u + 1], scalar2=None, op0=ALU.add
                    )
                nc.sync.dma_start(out=rows[:, u, :], in_=last[u][:])

        rows32 = slice(0, PASSES * ROWS)
        nc.sync.dma_start(offsets[:], offs)
        load_rows(nc.sync, tab_s, tab_scales)
        load_rows(nc.sync, wg_s_raw, wg_scales)
        load_rows(nc.sync, wo_s_raw, wo_scales)
        load_wg(0)
        load_table(0)
        load_table(1)
        nc.scalar.activation(warm_out[:], warm_in[:], ACT.Sigmoid)
        nc.vector.tensor_copy(out=picked_s[:], in_=tab_s[:].indirect(offsets[:]))
        permute(nc.gpsimd, rows_s[rows32, S : S + H].bitcast(I32), wg_s_raw[rows32, :].bitcast(I32), 1, RUN // 4)
        permute(nc.gpsimd, rows_s[rows32, S + H : S + 2 * H].bitcast(I32), wo_s_raw[rows32, :].bitcast(I32), 1, RUN // 4)
        nc.vector.tensor_copy(out=rows_s[rows32, 0:S].bitcast(I32), in_=picked_s[rows32, :].bitcast(I32))
        permute(nc.gpsimd, wg[:, 0:H], wg_raw[0][:], 1, RUN)
        spread(0)
        load_wg(1)
        load_wo()
        spread(1)
        load_wn(0, 0, PACK)
        load_wn(1, 0, PACK)
        load_w2()
        load_bias()
        for k in range(5):
            nc.tensor.matmul_mx(
                out=banks[7][:], lhsT=wg_raw[0][:, 0:P].bitcast(FP8X4), lhsT_scale=picked_s[:, 0:P],
                rhs=wg_raw[0][:].bitcast(FP8X4), rhs_scale=picked_s[:, 0:H], start=True, stop=True,
            )

        make_identity(nc, identity[:])
        for first, count in PIECES:
            gather_words(0, first, count)
        for half in range(2):
            for t in range(PACK - half):
                gate_pass(half, t, 0)
        gather_words(1, 0, 4)
        permute(nc.gpsimd, wg[:, H : 2 * H], wg_raw[1][:], 1, RUN)
        permute(nc.gpsimd, wo[:].bitcast(I32), wo_raw[:], PASSES, RUN // 2)
        gather_words(1, 4, 4)
        for first in (0, 2):
            round_wn_vector(0, first, 2)
        for first in (0, 2):
            cols = slice(first * P, (first + 2) * P)
            quantize(wn_c[0][:, cols], wn_s[0][:, cols], wn_bf[0][:, first * H : (first + 2) * H])
        round_wn_gpsimd(1, 2)
        round_wn_gpsimd(1, 3)
        for t in range(PACK):
            gate_pass(0, t, 1)
            sigmoid(0, t)
            if t == 1:
                old_passes(0, 0)
                weigh_old(0, 0)
        for t in range(1, PACK):
            gate_pass(1, t - 1, 1)
            old_passes(0, t)
        sigmoid(1, 0)
        sigmoid(1, 1)
        round_wn_scalar(1, 0)
        round_wn_scalar(1, 1)
        old_passes(1, 0)
        for a in range(PASSES):
            gate_pass(1, PACK - 1, a)
        sigmoid(1, 2)
        sigmoid(1, 3)
        for t in range(1, PACK):
            weigh_old(0, t)
        for first in (0, 2):
            cols = slice(first * P, (first + 2) * P)
            quantize(wn_c[1][:, cols], wn_s[1][:, cols], wn_bf[1][:, first * H : (first + 2) * H])
        weigh_old(1, 0)
        for part in range(4):
            round_w2(part)

        def weigh_group(g):
            for u in range(2):
                new_passes(g, u)
                weigh_new(g, u)

        weigh_group(0)
        blend_flat(0)
        for u in range(2):
            new_passes(1, u)
        old_passes(1, 1)
        weigh_new(1, 0)
        weigh_new(1, 1)
        blend_flat(1)
        weigh_old(1, 1)
        weigh_rows(0)
        weigh_rows(1)
        for t in range(2, PACK):
            old_passes(1, t)
        weigh_old(1, 2)
        for b in range(2):
            turn(b, old_rows[:, b, :], True)
        for b in range(2):
            turn(b, new_rows[b], False)
            round_turned(b)
        for part in range(2):
            block_passes(part)
        blend_woven(0, POOL_EVENTS[0], WIDE)
        quantize(w2_c[:], w2_s[:], w2_bf[:])
        quantize_h(0)
        finish(0)
        blend_woven(1, POOL_EVENTS[1], WIDE)
        weigh_old(1, 3)
        quantize_h(1)
        finish(1)
        weigh_block(0)
        quantize_h(2)
        finish(2)
        weigh_block(1)
        blend_woven(3, 0, P)
        blend_woven(3, P, WIDE)
        finish_last()
